import numpy as np, ml_dtypes
CORES = [24,25,26,27,28,29,30,31]
N = 8
BF = ml_dtypes.bfloat16
def gentries(a):
    return np.ascontiguousarray(a.reshape(8, 16, -1).transpose(0, 2, 1)).reshape(8, -1)
def gtable(e):
    e = np.asarray(e); return np.ascontiguousarray(e.reshape(8, -1, 16).transpose(0, 2, 1)).reshape(128, -1).astype(np.int32)
W, F, FC, LM, CAP, TS, LB, RO = 3072, 224, 512, 28, 32, 2048, 3, 2
WT = 255 - 14 * np.arange(16)
M = 8
def pick(t, ix):
    return np.take_along_axis(t, ix[:, :, None, :], 3)
def letters(rng, uneven):
    C = W // M; A = C // 4; hc = (A // 2) * 4; hw = hc * M
    if uneven:
        v = (np.floor(np.exp2(8 * rng.random((N, 8, 1, C))) * rng.random((N, 8, 16, C))) * (rng.random((N, 8, 1, C)) > 0.0625)).astype(np.int64)
        q = (np.floor(np.exp2(8 * rng.random((N, 8, 1, W))) * rng.random((N, 8, 16, W))) * (rng.random((N, 8, 1, W)) > 0.0625)).astype(np.int64)
    else:
        v = rng.integers(0, 256, (N, 8, 16, C)); q = rng.integers(0, 256, (N, 8, 16, W))
    base = rng.integers(0, C, (N, 8, A, 16)); base[:, :, :A // 2] %= hc
    alt = rng.integers(0, C, (N, 8, C, 16)); alt[:, :, :hc] %= hc
    seq = np.repeat(base, 4, axis=2); seq = np.where(rng.random(seq.shape) < 0.08, alt, seq)
    blk = np.repeat(np.add.accumulate((rng.random((N, 8, A, 16)) < 0.6).astype(np.int64), axis=3), 4 * M, axis=2)
    loose = np.take_along_axis(rng.random((N, 8, W, 17)), blk, 3) < rng.choice(np.array([0.15, 0.3, 0.5]), (N, 8, 1, 1))
    order = np.argsort(blk + np.where(loose, rng.random(blk.shape), 0.0625 * np.arange(16)), axis=3)
    mem = np.repeat(rng.integers(0, M, (N, 8, A, 16)), 4 * M, axis=2)
    mem = np.where(rng.random(mem.shape) < rng.choice(np.array([0.02, 0.06, 0.15, 0.4]), (N, 8, 1, 1)), rng.integers(0, M, mem.shape), mem)
    kid = np.take_along_axis(np.repeat(seq, M, axis=2) * M + mem, order, 3)
    v[:, :, :, :hc] = v[:1, :, :, :hc].copy(); q[:, :, :, :hw] = q[:1, :, :, :hw].copy(); kid[:, :, :hw] = kid[:1, :, :hw].copy()
    return np.repeat(v, M, axis=3), q, kid
def front(rng, skew):
    A = W // (4 * M)
    st = rng.random((N, 8, F)) < rng.choice(np.array([0.3, 0.5, 0.8]), (N, 8, 1)); st[:, :, 0] = True
    st = st.astype(np.int64); sid = np.add.accumulate(st, axis=2) - 1
    fam = (A * rng.random((N, 8, F)) ** (3 if skew else 1)).astype(np.int64)
    fam = np.take_along_axis(np.where(rng.random(fam.shape) < 0.7, fam % (A // 2), fam), sid, 2)
    c = fam * 4 + rng.integers(0, 4, fam.shape); m = rng.integers(0, M, fam.shape)
    o = np.argsort(sid + 0.99 * rng.random(fam.shape), axis=2)
    mv = np.where(rng.random(fam.shape) < 0.3, np.take_along_axis(m, o, 2), rng.integers(0, M, fam.shape))
    fv = np.take_along_axis(c, o, 2) * M + mv
    return c * M + m, np.where(rng.random(fam.shape) < 0.04, rng.integers(0, W, fam.shape), fv), st
def mix(rng, v, q, kid, fu, fv):
    pm = np.argsort(rng.random((N, 8, W)), axis=2); inv = np.argsort(pm, axis=2)
    k = np.take_along_axis(pm, kid.reshape(N, 8, 16 * W), 2).reshape(N, 8, W, 16)
    k = np.ascontiguousarray(np.take_along_axis(k, inv[:, :, :, None], 2).transpose(0, 1, 3, 2))
    return pick(v, inv), pick(q, inv), k, np.take_along_axis(pm, fu, 2), np.take_along_axis(pm, fv, 2)
def pack(v, q, k, fu, fv, st):
    return {"vec": v.reshape(N, 128, W).astype(np.float32).astype(BF), "mark": q.reshape(N, 128, W).astype(np.float32).astype(BF), "kids": np.ascontiguousarray(k.reshape(N, 128, W)).astype(np.int32),
            "fu": np.stack([gtable(a) for a in fu]), "fv": np.stack([gtable(a) for a in fv]), "fs": np.ascontiguousarray(st).astype(np.int32)}
def setup_inputs(rng):
    v, q, kid = letters(rng, False); fu, fv, st = front(rng, False)
    return pack(*mix(rng, v, q, kid, fu, fv), st)
def setup_inputs_room(rng):
    v = np.zeros((N, 8, 16, W), np.int64); q = np.zeros((N, 8, 16, W), np.int64); k = np.zeros((N, 8, 16, W), np.int64)
    fu = np.zeros((N, 8, F), np.int64); fv = np.zeros((N, 8, F), np.int64); st = np.zeros((N, 8, F), np.int64); st[:, :, 0] = 1
    for r in range(N):
        for g in range(8):
            o = rng.permutation(W); z0 = o[2 * F]; rest = o[2 * F + 1:]
            b = rng.integers(0, 2, W); b[z0] = 0; i = int(rng.integers(0, 16))
            v[r, g] = rng.integers(0, 128, (16, 1)); v[r, g, i] += b * int(rng.integers(1, 128))
            own = rng.integers(0, N, W); w = rng.integers(0, 256, (16, W)); w[0] -= w[0] % N; w[0] += (WT @ w - own) % N; w[:, z0] = 0; q[r, g] = w
            pool = [rest[(own[rest] == a) & (b[rest] == 0)] for a in range(N)]; zero = rest[b[rest] == 0]; ones = rest[b[rest] == 1]
            pu = rng.choice(rest, 16 * F); pv = pu.copy(); mode = g if g in (2, 3) else (0, 1, 0, 4)[(r + g) % 4]
            if mode in (0, 1):
                if mode == 0:
                    n = rng.choice(np.array([0, 1, CAP - 1, CAP, CAP + 1, CAP + 8]), N)
                    if r == 0: n[1] = CAP
                    x = rng.permutation(np.concatenate([np.resize(rng.permutation(pool[a]), int(n[a])) for a in range(N)]))
                else:
                    a = rng.permutation(N)
                    x = np.concatenate([np.resize(rng.permutation(pool[a[0]]), FC - 2), np.resize(rng.permutation(pool[a[1]]), 5)])
                t = np.sort(rng.permutation(16 * F)[:len(x)])
                pu[t] = x; pv[t] = z0
            elif mode in (2, 3):
                t = int(rng.integers(0, 8))
                for n in ([LM + 1] + [LM] * (F // LM) + [1] if mode == 2 else [LM] * (F // LM - 1) + [LM - 1, 2, 1, 1]):
                    if n == 1:
                        pu[t] = rng.choice(zero); pv[t] = z0
                    else:
                        pu[t] = rng.choice(zero); pv[t] = rng.choice(ones); pu[t + n - 1] = rng.choice(ones); pv[t + n - 1] = rng.choice(zero)
                    t += n + int(rng.integers(0, 4))
            else:
                lu, lv, lx, ly = int(o[0]), int(o[F]), int(rest[0]), int(rest[1])
                j = 13 if r == 0 else 0 if r == 1 else int(rng.integers(0, 14))
                for c in (lv, lx, ly): v[r, g, :, c] = v[r, g, :, lu]
                q[r, g, j:j + 3, lu] = np.minimum(np.maximum(q[r, g, j:j + 3, lu], 2), 254)
                q[r, g, :, lx] = q[r, g, :, lu]; q[r, g, j:j + 3, lx] += np.array([1, -2, 1])
                q[r, g, :, lv] = 0; q[r, g, :, ly] = 0
                pu[0] = lu; pv[0] = lv; pu[1] = lx; pv[1] = ly
            kk = rng.choice(rest, (16, W)); kk[:, o[:F]] = pu.reshape(F, 16).T; kk[:, o[F:2 * F]] = pv.reshape(F, 16).T
            k[r, g] = kk; fu[r, g] = o[:F]; fv[r, g] = o[F:2 * F]
    return pack(v, q, k, fu, fv, st)
def swing(rng, pu, pv, t, n, low, high):
    x, y = (pu, pv) if rng.random() < 0.5 else (pv, pu)
    x[t] = rng.choice(low); y[t] = rng.choice(high); x[t + n - 1] = rng.choice(high); y[t + n - 1] = rng.choice(low)
def setup_inputs_deep(rng):
    v = np.zeros((N, 8, 16, W), np.int64); q = np.zeros((N, 8, 16, W), np.int64); k = np.zeros((N, 8, 16, W), np.int64)
    fu = np.zeros((N, 8, F), np.int64); fv = np.zeros((N, 8, F), np.int64); st = np.zeros((N, 8, F), np.int64); st[:, :, 0] = 1
    P = 16 * F; C = (LM + 15) // 16
    for r in range(N):
        for g in range(8):
            mode = (r + g) % 4; o = rng.permutation(W); z0 = int(o[2 * F]); rest = o[2 * F + 1:]
            b = rng.integers(0, 3, W) if mode > 1 else rng.integers(0, 2, W) * mode
            b[z0] = 0
            half = 8 * int(rng.integers(0, 2)); m = rng.random((16, 1)) < 0.4; m[np.arange(16) // 8 * 8 != half] = False; m[half + int(rng.integers(0, 8))] = True
            j = 8 - half + int(rng.integers(0, 6)); tri = np.zeros((16, 1), np.int64); tri[j:j + 3, 0] = int(rng.integers(1, 33)) * np.array([1, -2, 1])
            two = m.astype(np.int64) if mode == 2 else tri
            v[r, g] = np.where(m, 0, rng.integers(64, 128, (16, 1))) + 255 * m.astype(np.int64) * (b == 1) + two * (b == 2)
            own = rng.integers(0, N, W); w = rng.integers(0, 256, (16, W)); w[0] -= w[0] % N; w[0] += (WT @ w - own) % N; w[:, z0] = 0; q[r, g] = w
            pool = [rest[(own[rest] == a) & (b[rest] == 0)] for a in range(N)]; kind = [rest[b[rest] == c] for c in range(3)]
            pu = rng.choice(rest, P); pv = pu.copy(); kk = rng.choice(rest, (16, W)); a = rng.permutation(N); a0 = int(a[0]); a1 = int(a[1])
            if mode == 0:
                heads = rest[:64]; t = np.sort(rng.permutation(P)[:64]); pu[t] = heads; pv[t] = z0
                n0 = FC // 16 + (16 if g < 4 else 0)
                kk[:, z0] = z0; kk[:, heads[:n0]] = rng.choice(pool[a0], (16, n0)); kk[:, heads[n0:]] = rng.choice(pool[a1], (16, 64 - n0))
            elif mode == 1:
                t = int(rng.integers(0, 4))
                for n in range(8):
                    swing(rng, pu, pv, t, LM + 1, kind[0], kind[1]); t += LM + 1 + int(rng.integers(0, 4))
                x = np.concatenate([np.resize(rng.permutation(pool[a0]), FC - 16), np.resize(rng.permutation(pool[a1]), 20)])
                i = t + np.sort(rng.permutation(P - t)[:len(x)]); pu[i] = x; pv[i] = z0
            elif mode == 2:
                x, y = (pu, pv) if r % 2 == 0 else (pv, pu)
                t = int(rng.integers(0, 8))
                x[t:t + 257] = rng.choice(kind[1], 257); x[t + 257] = rng.choice(kind[2]); y[t:t + 258] = rng.choice(kind[0], 258); t += 258
                i = t + np.sort(rng.permutation(800)[:24]); pu[i] = rng.choice(kind[0], 24); pv[i] = z0; t += 800
                y[t:t + 257] = rng.choice(kind[1], 257); y[t + 257] = rng.choice(kind[2]); x[t:t + 258] = rng.choice(kind[0], 258); t += 258
                while t + LM + 16 < P:
                    t += int(rng.integers(0, 16)); n = int(rng.integers(2, LM + 1))
                    swing(rng, pu, pv, t, n, kind[0], kind[int(rng.integers(1, 3))]); t += n
            else:
                s = int(rng.integers(1, 6)); e = F - 4 * C
                st[r, g, s] = 1; st[r, g, e + C * np.arange(4)] = 1
                i = int(rng.integers(0, 16 * s)); pu[i] = rng.choice(kind[0]); pv[i] = rng.choice(kind[1])
                t = 16 * s
                while t + LM + 48 < 16 * e:
                    t += int(rng.integers(0, 48))
                    if rng.random() < 0.5:
                        pu[t] = rng.choice(kind[0]); pv[t] = z0; t += 1
                    else:
                        n = int(rng.integers(2, LM + 1)); swing(rng, pu, pv, t, n, kind[0], kind[2]); t += n
                for c in range(4):
                    i = 16 * (e + C * (c + 1)); x, y = (pv, pu) if c < 3 else (pu, pv)
                    x[i - LM:i] = rng.choice(kind[1], LM); y[i - LM:i] = rng.choice(kind[0], LM)
            kk[:, o[:F]] = pu.reshape(F, 16).T; kk[:, o[F:2 * F]] = pv.reshape(F, 16).T
            k[r, g] = kk; fu[r, g] = o[:F]; fv[r, g] = o[F:2 * F]
    return pack(v, q, k, fu, fv, st)
def setup_inputs_ends(rng):
    v, q, kid = letters(rng, False); fu, fv, st = front(rng, False)
    v, q, k, fu, fv = mix(rng, v, q, kid, fu, fv)
    st[:, 0] = 1; st[:, 1] = 0
    two = np.array([0, W - 1]); few = np.array([0, 1, W - 1])
    fu[:, 2] = rng.choice(two, (N, F)); fv[:, 2] = rng.choice(two, (N, F)); k[:, 2, :, 0] = rng.choice(few, (N, 16)); k[:, 2, :, W - 1] = rng.choice(few, (N, 16))
    for r in range(N):
        i = int(rng.integers(0, 16)); x = v[r, 3, i].copy(); v[r, 3] = 7; v[r, 3, i] = x
    v[:, 4] = 255 * (np.arange(W) >= W // 2); k[:, 4] = rng.integers(0, W // 2, (N, 16, W)) + (W // 2) * (np.arange(W) % 2 == 0)
    even = 2 * rng.integers(0, W // 2, (N, F)); odd = 2 * rng.integers(0, W // 2, (N, F)) + 1
    fu[:, 4] = even; fv[:, 4] = odd; fu[1::2, 4] = odd[1::2]; fv[1::2, 4] = even[1::2]; st[:, 4] = 0; st[:, 4, F - 4:] = 1
    fv[:, 5] = rng.integers(0, W, (N, F)); st[:, 5] = np.arange(F) % 3 != 1
    fv[:, 6] = fu[:, 6]; fv[:, 6, F - 1] = (fu[:, 6, F - 1] + 1 + rng.integers(0, W - 1, N)) % W
    q[:, 7] = 0; q[1::2, 7] = 255
    st[:, :, 0] = 1
    return pack(v, q, k, fu, fv, st)
def setup_inputs_alike(rng):
    v, q, kid = letters(rng, False); fu, fv, st = front(rng, False)
    v[:] = v[:1].copy(); q[:] = q[:1].copy(); kid[:] = kid[:1].copy()
    for x in (fu, fv, st):
        for r in range(1, N):
            x[r, ::2] = x[0, ::2]; x[r, 1::2] = np.roll(x[0, 1::2], r * (F // N), axis=1)
    st[:, :, 0] = 1
    return pack(*mix(rng, v, q, kid, fu, fv), st)
def setup_inputs_spread(rng):
    v, q, kid = letters(rng, True); fu, fv, st = front(rng, True)
    return pack(*mix(rng, v, q, kid, fu, fv), st)
def check_inputs(d):
    bad = []
    for k, hi in (("vec", 255), ("mark", 255), ("kids", W - 1), ("fu", W - 1), ("fv", W - 1), ("fs", 1)):
        a = np.asarray(d[k]).astype(np.float32)
        if not np.all((a >= 0) & (a <= hi) & (a == np.floor(a))): bad.append("range of " + k)
    if not np.all(np.asarray(d["fs"])[:, :, 0] == 1): bad.append("first place of fs")
    return bad
def reference(vec, mark, kids, fu, fv, fs):
    vt = vec.astype(np.float32).astype(np.int64).reshape(N, 8, 16, W); qt = mark.astype(np.float32).astype(np.int64).reshape(N, 8, 16, W); kt = kids.astype(np.int64).reshape(N, 8, 16, W)
    u = np.stack([gentries(a) for a in fu]).astype(np.int64); v = np.stack([gentries(a) for a in fv]).astype(np.int64); st = fs.astype(np.int64)
    store = np.full((N, 8, 16, TS), -1, np.int64)
    for rnd in range(RO):
        a = pick(kt, u).transpose(0, 1, 3, 2).reshape(N, 8, 16 * F); b = pick(kt, v).transpose(0, 1, 3, 2).reshape(N, 8, 16 * F)
        d = np.add.accumulate(pick(vt, a) - pick(vt, b), axis=3)
        s0 = 16 * np.repeat(np.maximum.accumulate(np.where(st == 1, np.arange(F), 0), axis=2), 16, axis=2)
        d = d - np.where((s0 > 0)[:, :, None, :], pick(d, np.maximum(s0 - 1, 0)), 0)
        last = np.zeros((N, 8, F, 16), bool); last[:, :, F - 1, 15] = True; last[:, :, :F - 1, 15] = st[:, :, 1:] == 1
        cut = np.all(d == 0, axis=2) | last.reshape(N, 8, 16 * F)
        e = np.maximum(pick(qt, a), pick(qt, b)) + d; run = np.add.accumulate(e, axis=3)
        fac = {}
        for r in range(N):
            for g in range(8):
                t1 = np.flatnonzero(cut[r, g]); t0 = np.concatenate([np.zeros(1, np.int64), t1[:-1] + 1]); ln = t1 - t0 + 1
                c = np.flatnonzero((ln <= LM) & ~((ln == 1) & (a[r, g, t0] == b[r, g, t0])))[:FC]
                t0 = t0[c]; t1 = t1[c]; ln = ln[c]
                z = (run[r, g][:, t1] - run[r, g][:, t0] + e[r, g][:, t0]) & 255
                h = (WT @ z) & (N * TS - 1)
                fac[r, g] = (t0, ln, z, h & (N - 1), h >> LB, np.zeros(len(c), bool))
        for o in range(N):
            for g in range(8):
                ix = [np.flatnonzero(fac[r, g][3] == o)[:CAP] for r in range(N)]
                zz = np.concatenate([fac[r, g][2][:, ix[r]] for r in range(N)], axis=1); pp = np.concatenate([fac[r, g][4][ix[r]] for r in range(N)])
                i = np.flatnonzero(np.any(store[o, g][:, pp] != zz, axis=0))
                win = i[np.unique(pp[i], return_index=True)[1]]
                store[o, g][:, pp[win]] = zz[:, win]
                new = np.zeros(len(pp), bool); new[win] = True; n = 0
                for r in range(N):
                    fac[r, g][5][ix[r]] = new[n:n + len(ix[r])]; n += len(ix[r])
        u = np.zeros((N, 8, F), np.int64); v = np.zeros((N, 8, F), np.int64); st = np.ones((N, 8, F), np.int64)
        for r in range(N):
            for g in range(8):
                t0, ln, z, o, p, new = fac[r, g]
                n = np.flatnonzero(new); to = np.add.accumulate(ln[n]); n = n[to <= F]; j = 0
                for x in n:
                    L = int(ln[x]); t = int(t0[x])
                    u[r, g, j:j + L] = a[r, g, t:t + L]; v[r, g, j:j + L] = b[r, g, t:t + L]; st[r, g, j + 1:j + L] = 0; j += L
    return {"yt": store.reshape(N, 128, TS).astype(np.float32).astype(BF), "yu": u.astype(np.float32), "yv": v.astype(np.float32), "ys": st.astype(np.float32)}

@@ -1,0 +1,719 @@
+import math
+from concourse.bass import DstId, RemoteDMATransfer
+from concourse.mybir import AluOpType as OP, ActivationFunctionType as AF
+
+W, F, P, K, TS = 3072, 224, 3584, 512, 2048
+CW, NCH, LC = 448, 8, 28
+ST = 512
+CLAMP = 7168.0
+LN4, LN2 = math.log(4.0), math.log(2.0)
+CFG = {
+    "vs": ["vvvsssvv", "vsvvvsss"],
+    "qs": ["vsssssss", "ssvsvsss"],
+    "cs": ["vssvssss", "vvsvssss"],
+}
+
+SCRATCH = {}
+for _d, _l in (
+    ("int32", "kidb:3072 fuv:28 fsb:224 rmi:2 li:224 zi:512 hi:32 ow:32 hri:256 hli:16 pli:16 taui:224 tj:16 cint:160 cpi:160"),
+    ("uint16", "uv:28 ku:224 kv:224 cof:16 jl:32 t1u:32 t0u:32 ql:32 plu:16 su:16 ofu:32 tju:16 qd:16"),
+    ("float16", "prh:256 tauh:224 suv:448 ch:272"),
+    ("bfloat16", "vecb:3072 markb:3072 va:1792 vb:1792 nz:3584 qa:3584 mq:3584 msk:3584 flg:232 fsf:224 last:232 z0:232 z0m:224 cand:224 "
+     "nls:16 cwin:7920 jk:512 oh:512 lh:512 lrep:512 zb:512 ind:288 swin:4608 fwin:4608 land0:256 land1:256 store:2304 inv:256 ne:256 "
+     "nel:256 mb:2176 dg:256 nw:256 ncu:1040 ex:512 fa:224 fb:224 cb:4400 cj:1600"),
+    ("float32", "uf:224 vf:224 dd:3584 dc:3584 run:3592 rmf:2 lbig:224 eqt:224 gam:224 m2:224 aa:224 wm:224 yl:224 cinc:224 rf:224 et:16 "
+     "ci:16 o1:16 o2:16 t1s:32 t0s:32 r1:512 cs:288 cd:288 mt:224 pm:16 sx:16 sy:16 sz:16 ea:32 eb:32 st:32 s2:32 s3:32 s5:32 "
+     "d0:512 pwin:1536 unf:224 hold:224 oh2:224 adl:28 uvs:28 fin:672 adr:224 cf:720 ck:4200"),
+):
+    for _x in _l.split():
+        SCRATCH[_x.split(":")[0]] = ("sbuf", [128, int(_x.split(":")[1])], _d)
+for _x in range(8):
+    SCRATCH["ps%d" % _x] = ("psum", [128, 512], "float32")
+SEMAPHORES = ["qv", "qs", "qt", "qg"] + ["d_" + _x for _x in "l0 l1 l2 l3 l4 l5 w0 w1 w2 w3 ka0 ka1 fa0 fa1 ks0 ks1 fs0 fs1".split()]
+
+
+def A(b, c0, c1, st=1, p=None):
+    return (b, c0, c1, st, p)
+
+
+def IX(b, c0, c1, off, o0, o1):
+    return (b, c0, c1, off, o0, o1)
+
+
+def bank(b):
+    return b.startswith("ps") and b[2:].isdigit()
+
+
+CYCLE = 0.00095
+
+
+def estimate(q, out, ins, two):
+    if q == "t":
+        return max(64, (out[2] - out[1])) / 1220.0
+    for a, rate in ((out, 2.5), (ins[0], 1.4)):
+        if len(a) == 6:
+            return 0.06 + 16 * (a[5] - a[4]) * rate * CYCLE
+    n = (out[2] - out[1] + out[3] - 1) // out[3]
+    f = 1.0
+    if q == "g":
+        return 0.13 + 2 * n * CYCLE
+    if q == "v" and two and not any(bank(a[0]) for a in ins):
+        f = 2.0
+    elif q == "v" and not two and all(SCRATCH[a[0]][2] in ("bfloat16", "float16", "uint16") for a in [out] + ins):
+        f = 0.5
+    return max(64, n * f) * CYCLE + 0.02
+
+
+def build(core, T, topo):
+    rank = T.rank_of(core)
+    ops = []
+    isap = lambda s: isinstance(s, tuple)
+
+    def X(a):
+        if len(a) == 6:
+            return T[a[0]][:, a[1]:a[2]].indirect(T[a[3]][:, a[4]:a[5]])
+        p = a[4]
+        if p is None:
+            return T[a[0]][:, a[1]:a[2]:a[3]] if a[3] != 1 else T[a[0]][:, a[1]:a[2]]
+        return T[a[0]][p[0]:p[1]:p[2], a[1]:a[2]]
+
+    def acc(a):
+        return [(a[0], a[1], a[2]), (a[3], a[4], a[5])] if len(a) == 6 else [(a[0], a[1], a[2])]
+
+    def add(q, fn, reads, writes, sem=None, inc=0, est=None, two=False):
+        rd = []
+        wr = []
+        for a in reads:
+            rd += acc(a)
+        for a in writes:
+            x = acc(a)
+            wr += x[:1]
+            rd += x[1:]
+        whole = [len(a) == 5 and a[3] == 1 and a[4] is None for a in writes]
+        if est is None:
+            est = estimate(q, writes[0], [a for a in reads if a[2] - a[1] > 1] or reads[:1] or [writes[0]], two)
+        ops.append({"q": q, "fn": fn, "r": rd, "w": wr, "whole": whole, "sem": sem, "inc": inc, "est": est})
+
+    def tt(out, a, b, op):
+        add("v", lambda g: g.vector.tensor_tensor(X(out), X(a), X(b), op), [a, b], [out], two=True)
+
+    def ts(out, a, s1, op0, s2=None, op1=None):
+        rd = [a] + [s for s in (s1, s2) if isap(s)]
+        x = lambda s: X(s) if isap(s) else s
+        if op1 is None:
+            add("v", lambda g: g.vector.tensor_scalar(X(out), X(a), x(s1), None, op0), rd, [out])
+        else:
+            add("v", lambda g: g.vector.tensor_scalar(X(out), X(a), x(s1), x(s2), op0, op1), rd, [out])
+
+    def cp(out, a):
+        add("v", lambda g: g.vector.tensor_copy(X(out), X(a)), [a], [out])
+
+    def ms(out, v):
+        add("v", lambda g: g.vector.memset(X(out), v), [], [out])
+
+    def scan(out, a, b, init, op0, op1):
+        rd = [a, b] + ([init] if isap(init) else [])
+        add("v", lambda g: g.vector.tensor_tensor_scan(X(out), X(a), X(b), X(init) if isap(init) else init, op0, op1), rd, [out])
+
+    def act(out, a, func, bias=0.0, scale=1.0):
+        rd = [a] + ([scale] if isap(scale) else [])
+        add("s", lambda g: g.scalar.activation(X(out), X(a), func, bias=bias, scale=X(scale) if isap(scale) else scale), rd, [out])
+
+    def mm(out, l, r, start, stop):
+        add("t", lambda g: g.tensor.matmul(X(out), X(l), X(r), start, stop), [l, r], [out])
+
+    def iota(out, pat, base, cm, f):
+        if f:
+            add("g", lambda g: g.iota(X(out), pat, base, cm, allow_small_or_imprecise_dtypes=True), [], [out])
+        else:
+            add("g", lambda g: g.iota(X(out), pat, base, cm), [], [out])
+
+    def dma(q, out, a, sem, est):
+        o = (lambda: T[out][:]) if isinstance(out, str) else (lambda: X(out))
+        i = (lambda: T[a][:]) if isinstance(a, str) else (lambda: X(a))
+        e = (lambda g: g.sync) if q == "y" else (lambda g: g.scalar)
+        add(q, lambda g: e(g).dma_start(o(), i()), [] if isinstance(a, str) else [a], [] if isinstance(out, str) else [out], "d_" + sem, 16, est)
+
+    def share(a, b):
+        return len(topo.engines(a, b)) // 8
+
+    def send(src, dst, rsem, lsem, after=()):
+        others = [r for r in range(8) if r != rank]
+
+        def fn(g):
+            tr = []
+            for n, r in enumerate(others):
+                d = T.cores[r]
+                rid, pid = topo.addr(d)[:2]
+                e = share(core, d)
+                m = 0
+                for x in topo.engines(core, d)[n * e:n * e + e]:
+                    m |= 1 << x
+                tr.append(RemoteDMATransfer(dst_ids=[DstId(rid=rid, pnc=pid)], dma_engine_mask=m, remote_sem=T.sem["d_" + rsem], srcs=[X(src(r))], dsts=[X(dst)]))
+            return g.remote_dma_fused(tr, local_sem=T.sem["d_" + lsem])
+        add("g", fn, [src(r) for r in others] + list(after), [], "d_" + lsem, sum(share(core, T.cores[r]) for r in others), 2.5)
+
+    def arrive(rsem, dsts):
+        add("x", None, [], dsts, "d_" + rsem, sum(share(T.cores[r], core) for r in range(8) if r != rank), 0.3)
+
+    dma("y", A("fuv", 0, 14), "fu", "l0", 2.0)
+    dma("y", A("fuv", 14, 28), "fv", "l1", 2.0)
+    dma("s", A("fsb", 0, F, 1, (0, 8, 1)), "fs", "l2", 2.0)
+    dma("y", A("kidb", 0, W), "kids", "l3", 8.3)
+    dma("y", A("vecb", 0, W), "vec", "l4", 5.1)
+    dma("y", A("markb", 0, W), "mark", "l5", 5.1)
+    iota(A("cint", 0, 1), [[0, 1]], 0, 1, False)
+    iota(A("cint", 8, 152), [[1, 144]], 0, 0, False)
+    iota(A("msk", 0, P), [[0, P]], 1, 0, True)
+    iota(A("ck", 0, 512), [[1, 512]], 8193, 0, True)
+    iota(A("ck", 512, 736), [[1, F]], 0, 0, True)
+    iota(A("ck", 736, 960), [[1, F]], -1, 0, True)
+    iota(A("ck", 960, 1184), [[1, F]], -2049, 0, True)
+    iota(A("ck", 1184, 1216), [[16, 32]], 0, 0, True)
+    iota(A("ck", 2560, 2816), [[0, 16], [1, 16]], 0, 0, True)
+    iota(A("cj", 0, F), [[1, F]], 0, 0, True)
+    iota(A("ck", 1792, 2080), [[ST, 9], [0, 32]], 8192, 0, True)
+    for a, v in ((A("cj", 224, 738), 255), (A("cj", 738, 1026), 1), (A("ck", 1312, 1536), 0), (A("z0", 0, F + 8), 1), (A("last", 0, F + 8), 0),
+                 (A("run", 0, 8), 0), (A("cwin", 0, K), 0), (A("pwin", 0, F), 0), (A("ncu", 0, 8), 0), (A("swin", 0, 8 * ST), -1),
+                 (A("fwin", 0, 9 * ST), 0), (A("store", 0, TS + 256), -1)):
+        iota(a, [[0, a[2] - a[1]]], v, 0, True)
+    P0 = A("cf", 0, 1)
+    PI = A("cf", 1, 2)
+    PG = A("cf", 2, 3)
+    PB = A("cf", 3, 4)
+    W2 = A("cf", 4, 5)
+    M15 = A("cf", 5, 6)
+    PW = A("cf", 6, 7)
+    P4 = A("cf", 7, 8)
+    PI2 = A("cf", 8, 9)
+    MBIG = A("cf", 10, 11)
+    NL4 = A("cf", 12, 13)
+    cp(P0, A("cint", 0, 1))
+    ts(A("cpi", 0, 1), A("cint", 0, 1), 15, OP.bitwise_and)
+    ts(A("cpi", 1, 2), A("cint", 0, 1), 4, OP.arith_shift_right)
+    cp(A("cf", 1, 3), A("cpi", 0, 2))
+    ts(PB, PG, 16.0, OP.mult, 16.0, OP.add)
+    ts(W2, PI, -28.0, OP.mult, 510.0, OP.add)
+    ts(M15, PI, 15.0, OP.is_equal)
+    ts(MBIG, M15, 2.0 ** 24, OP.mult)
+    ts(PI2, PI, 2.0, OP.add)
+    YC = A("cf", 16, 160)
+    Y128 = A("cf", 16, 144)
+    MI = A("cf", 160, 288)
+    MG = A("cf", 288, 416)
+    BLK = A("cf", 416, 544)
+    T1 = A("cf", 544, 672)
+    cp(YC, A("cint", 8, 152))
+    ts(A("cpi", 8, 136), A("cint", 8, 136), 15, OP.bitwise_and)
+    cp(MI, A("cpi", 8, 136))
+    ts(A("cint", 8, 136), A("cint", 8, 136), 4, OP.arith_shift_right)
+    cp(MG, A("cint", 8, 136))
+    ts(BLK, MG, PG, OP.is_equal)
+    nb = [0]
+    c = {}
+    sel_ = {}
+
+    def cbuf(n):
+        nb[0] += n
+        return A("cb", nb[0] - n, nb[0])
+
+    def mksel(name, wt):
+        a = cbuf(144)
+        if wt is None:
+            ts(a, YC, PB, OP.is_equal)
+        else:
+            act(a, A("cb", sel_["one"], sel_["one"] + 144), AF.Copy, scale=wt)
+        sel_[name] = a[1]
+
+    def sel(name, i):
+        b = sel_[name] + 16 - i
+        return A("cb", b, b + 128)
+    mksel("one", None)
+    IDN, IDM, OB, REP = cbuf(128), cbuf(128), cbuf(128), cbuf(128)
+    ts(IDN, Y128, P0, OP.is_equal)
+    act(IDM, IDN, AF.Copy, scale=-1.0)
+    act(OB, BLK, AF.Copy)
+    ts(REP, MG, P0, OP.is_equal)
+    cp(A("uv", 0, 28), A("fuv", 0, 28))
+    add("v", lambda g: g.vector.tensor_copy(T.fsf[0:8, :], T.fsb[0:8, :]), [A("fsb", 0, F)], [A("fsf", 0, F)])
+    add("t", lambda g: g.tensor.matmul(T.ps0[:, 0:F], T.cb[0:8, REP[1]:REP[2]], T.fsf[0:8, :], True, True), [REP, A("fsf", 0, F)], [A("ps0", 0, F)])
+    ms(A("flg", 0, F + 8), 1.0)
+    cp(A("flg", 0, F), A("ps0", 0, F))
+
+    def expand():
+        cp(A("ku", 0, F), IX("kidb", 0, W, "uv", 0, 14))
+        cp(A("kv", 0, F), IX("kidb", 0, W, "uv", 14, 28))
+        ts(A("msk", 0, P, 16), A("flg", 0, F), -1.0, OP.mult, 1.0, OP.add)
+        ts(A("uf", 0, F), A("ku", 0, F), -1536.0, OP.add)
+        ts(A("vf", 0, F), A("kv", 0, F), -1536.0, OP.add)
+
+    E, U, D = A("ck", 3792, 3920), A("ck", 3920, 4048), A("ck", 4048, 4176)
+    for name, wt in (("six", 1.0 / 16), ("pi", PI), ("w2", W2), ("n512", -512.0)):
+        mksel(name, wt)
+    act(PW, PI, AF.Exp, scale=-LN2)
+    act(P4, PI, AF.Exp, scale=LN4)
+    E4 = cbuf(128)
+    act(E4, MI, AF.Exp, scale=-LN4)
+    pw = cbuf(16)[1]
+    cp(A("cb", pw, pw + 2), A("cf", 6, 8))
+    cp(A("cf", 9, 10), A("cb", pw, pw + 1))
+    ts(E, E4, A("cb", pw + 1, pw + 2), OP.mult)
+    tt(E, E, BLK, OP.mult)
+    ts(D, MI, PI, OP.subtract)
+    for name, lo, hi_, f in (("b0", 1, 15, 1.0), ("b1", -15, 12, 4.0 ** -16), ("b2", -15, -4, 4.0 ** -32)):
+        c[name] = cbuf(128)
+        ts(U, D, float(lo), OP.is_ge, f, OP.mult)
+        ts(T1, D, float(hi_), OP.is_le)
+        tt(U, U, T1, OP.mult)
+        tt(c[name], U, E, OP.mult)
+    c["idm2"] = cbuf(128)
+    ts(T1, Y128, P0, OP.is_equal)
+    ts(c["idm2"], T1, -2.0, OP.mult)
+    expand()
+    c["nui"] = cbuf(128)
+    ts(U, D, 0.0, OP.is_le, -1.0, OP.mult)
+    tt(U, U, BLK, OP.mult)
+    cp(c["nui"], U)
+    for name, v in (("rkm", 8193.0), ("nsl", -8191.0)):
+        c[name] = cbuf(128)
+        ts(E, T1, v, OP.mult)
+        tt(E, E, U, OP.add)
+        cp(c[name], E)
+    for name, wt in (("obw2", W2), ("obp", A("cf", 9, 10)), ("obpi", PI2), ("ob4", 4.0), ("ob16", 1.0 / 16), ("obm", -1.0)):
+        c[name] = cbuf(128)
+        act(c[name], BLK, AF.Copy, scale=wt)
+    cp(A("qd", 0, 16), A("cf", 16, 32))
+    ts(A("ch", 0, 144), YC, PB, OP.is_equal)
+    cp(A("ch", 144, 272), BLK)
+    ts(A("ck", 1216, 1230), A("ck", 1184, 1198), PI, OP.add, 4096.0, OP.add)
+    ts(A("ck", 1232, 1264), A("ck", 1184, 1216), PI, OP.add, 256.0, OP.add)
+    ts(A("ck", 1264, 1296), A("ck", 1184, 1216), PI, OP.add, 1024.0, OP.add)
+    ts(A("ck", 1296, 1312), A("ck", 1184, 1200), PI, OP.add, 2048.0, OP.add)
+    act(A("ck", 1536, 1792), A("ck", 2560, 2816), AF.Exp, scale=-LN2)
+    cp(A("cj", 1056, 1312), A("ck", 1536, 1792))
+    ts(A("ck", 1536, 1792), A("cj", 1056, 1312), 2.0, OP.mult)
+    act(A("cf", 11, 12), A("cj", 1058, 1059), AF.Ln)
+    add("v", lambda g: g.vector.reciprocal(T.cf[:, 12:13], T.cf[:, 11:12]), [A("cf", 11, 12)], [NL4])
+    ms(A("cj", 738, 1026, 32), 0.0)
+    ts(A("ck", 2080, 2368), A("cj", 738, 1026), -1.0, OP.mult, 1.0, OP.add)
+    tt(A("ck", 1792, 2080), A("ck", 1792, 2080), A("ck", 2080, 2368), OP.mult)
+    cp(A("cj", 1312, 1600), A("ck", 1792, 2080))
+
+    def big(rnd):
+        vs, qs, cs = [CFG[k][rnd] for k in ("vs", "qs", "cs")]
+        size = 0
+        for i in range(NCH):
+            lo = i * CW
+            vl = (i % 4) * CW
+            va, vb = A("va", vl, vl + CW), A("vb", vl, vl + CW)
+            iv = IX("vecb", 0, W, "kv", i * LC, i * LC + LC)
+            act(va, IX("vecb", 0, W, "ku", i * LC, i * LC + LC), AF.Copy)
+            src, op = vb, OP.subtract
+            if vs[i] == "s":
+                act(vb, iv, AF.Copy)
+                src, op = A("ps%d" % (i % 2), 0, CW), OP.add
+                mm(src, IDN, va, True, False)
+                mm(src, IDM, vb, False, True)
+            else:
+                tt(vb, iv, va, OP.subtract)
+            d = A("dd", lo, lo + CW)
+            scan(d, A("msk", lo, lo + CW), src, 0.0 if i == 0 else A("dd", lo - 1, lo), OP.mult, op)
+            act(A("nz", lo, lo + CW), d, AF.Abs)
+            if i % 2 == 1:
+                b = (i - 1) * CW
+                for x in range(16):
+                    mm(A("ps2", (i - 1) * LC, (i + 1) * LC), sel("one", x), A("nz", b + x, b + 2 * CW, 16), x == 0, x == 15)
+        for i in range(NCH):
+            lo = i * CW
+            d, dc, m, qa = [A(b, lo, lo + CW) for b in ("dd", "dc", "mq", "qa")]
+            o = A("run", lo + 8, lo + 8 + CW)
+            iu = IX("markb", 0, W, "ku", i * LC, i * LC + LC)
+            if qs[i] == "v":
+                cp(qa, iu)
+            else:
+                act(qa, iu, AF.Copy)
+            tt(m, IX("markb", 0, W, "kv", i * LC, i * LC + LC), qa, OP.max)
+            init = 0.0 if i == 0 else A("run", lo + 7, lo + 8)
+            step = CW * ((2 if cs[i] == "s" else 1) * CLAMP + 255)
+            size += step
+            if size > 2 ** 24 - 1:
+                size = step + 255
+                cp(A("rmi", 0, 1), A("run", lo + 7, lo + 8))
+                ts(A("rmi", 1, 2), A("rmi", 0, 1), 255, OP.bitwise_and)
+                cp(A("rmf", 0, 1), A("rmi", 1, 2))
+                init = A("rmf", 0, 1)
+            if cs[i] == "v":
+                ts(dc, d, CLAMP, OP.min, -CLAMP, OP.max)
+                scan(o, dc, m, init, OP.add, OP.add)
+            else:
+                act(dc, d, AF.Relu, bias=CLAMP)
+                act(dc, dc, AF.Relu, bias=2 * CLAMP, scale=-1.0)
+                scan(o, m, dc, init, OP.add, OP.subtract)
+
+    def side():
+        ts(A("last", 2, 2 + F), A("flg", 1, F + 1), M15, OP.mult)
+        for k in range(3):
+            mm(A("ps3", 0, F), c["b%d" % k], A("last", 2 - k, 2 - k + F), k == 0, False)
+        ts(A("lbig", 0, F), A("flg", 1, F + 1), MBIG, OP.mult, 0.5, OP.add)
+        tt(A("eqt", 0, F), A("uf", 0, F), A("vf", 0, F), OP.is_equal)
+        tt(A("gam", 0, F), A("lbig", 0, F), A("eqt", 0, F), OP.subtract)
+        ts(A("m2", 0, F), A("gam", 0, F), 2.0 ** 24 - 1, OP.is_equal)
+
+    def control(rnd):
+        cnt = A("ps2", 0, F)
+        ts(A("z0", 2, 2 + F), cnt, 0.5, OP.is_le)
+        for k in range(3):
+            mm(A("ps3", 0, F), c["b%d" % k], A("z0", 2 - k, 2 - k + F), False, False)
+        tt(A("z0m", 0, F), cnt, A("m2", 0, F), OP.is_lt)
+        mm(A("ps3", 0, F), c["idm2"], A("z0m", 0, F), False, True)
+        tt(A("aa", 0, F), cnt, A("gam", 0, F), OP.is_gt)
+        tt(A("cand", 0, F), A("ps3", 0, F), A("aa", 0, F), OP.is_gt)
+        for x in range(16):
+            mm(A("ps4", 0, 14), sel("one", x), A("cand", x, F, 16), x == 0, x == 15)
+        mm(A("ps5", 0, F), OB, A("cand", 0, F), True, True)
+        mm(A("ps6", 0, F), c["rkm"], A("cand", 0, F), True, True)
+        act(A("wm", 0, F), A("ps3", 0, F), AF.Relu)
+        act(A("yl", 0, F), A("wm", 0, F), AF.Ln, bias=2.0 ** -60)
+        cp(A("nls", 0, 14), A("ps4", 0, 14))
+        mm(A("ps7", 0, 14), OB, A("nls", 0, 14), True, True)
+        mm(A("ps2", 0, 14), c["nui"], A("nls", 0, 14), True, True)
+        ts(A("et", 0, 14), A("ps4", 0, 14), 0.0, OP.is_equal)
+        tt(A("et", 0, 14), A("et", 0, 14), A("ck", 1216, 1230), OP.mult)
+        scan(A("ci", 0, 14), A("ps7", 0, 14), A("ck", 1312, 1326), 0.0, OP.add, OP.max)
+        tt(A("o1", 0, 14), A("ps2", 0, 14), A("et", 0, 14), OP.add)
+        tt(A("o2", 0, 14), A("o1", 0, 14), A("ci", 0, 14), OP.add)
+        cp(A("cof", 0, 14), A("o2", 0, 14))
+        cp(IX("cwin", 0, 7920, "cof", 0, 14), A("cj", 0, F))
+        scan(A("jk", 0, K), A("cwin", 0, K), A("cwin", 0, K), 0.0, OP.max, OP.max)
+        for x in range(16):
+            mm(A("ps4", 0, 32), sel("six", x), A("jk", x, K, 16), x == 0, x == 15)
+        for x in range(16):
+            mm(A("ps7", 0, 32), sel("one", x), A("jk", x, K, 16), x == 0, False)
+        mm(A("ps3", 0, K), OB, A("jk", 0, K), True, False)
+        scan(A("cinc", 0, F), A("ps5", 0, F), A("ck", 1312, 1312 + F), 0.0, OP.add, OP.max)
+        tt(A("rf", 0, F), A("ps6", 0, F), A("cinc", 0, F), OP.add)
+        ts(A("li", 0, F), A("yl", 0, F), NL4, OP.mult, 0.354, OP.add)
+        cp(A("jl", 0, 32), A("ps4", 0, 32))
+        tt(A("oh", 0, K), IX("rf", 0, F, "jl", 0, 32), A("ck", 0, K), OP.is_equal)
+        for x in range(16):
+            mm(A("ps7", 0, 32), sel("pi", x), A("oh", x, K, 16), False, x == 15)
+        mm(A("ps3", 0, K), c["obpi"], A("oh", 0, K), False, False)
+        tt(A("lh", 0, K), IX("li", 0, F, "jl", 0, 32), A("oh", 0, K), OP.mult)
+        for x in range(16):
+            mm(A("ps2", 0, 32), sel("one", x), A("lh", x, K, 16), x == 0, x == 15)
+        for x in range(16):
+            mm(A("ps5", 0, 32), sel("one", x), A("oh", x, K, 16), x == 0, False)
+        mm(A("ps6", 0, K), OB, A("lh", 0, K), True, True)
+        mm(A("ps3", 0, K), c["obm"], A("lh", 0, K), False, False)
+        ts(A("t1s", 0, 32), A("ps7", 0, 32), 8.0, OP.add)
+        ts(A("t1u", 0, 32), A("ps7", 0, 32), 8.0, OP.add)
+        tt(A("t0s", 0, 32), A("t1s", 0, 32), A("ps2", 0, 32), OP.subtract)
+        cp(A("t0u", 0, 32), A("t0s", 0, 32))
+        act(A("r1", 0, K), IX("run", 0, P + 8, "t1u", 0, 32), AF.Identity, bias=1.0)
+        tt(A("zi", 0, K), IX("run", 0, P + 8, "t0u", 0, 32), A("r1", 0, K), OP.subtract)
+        ts(A("zi", 0, K), A("zi", 0, K), 255, OP.bitwise_and)
+        ts(A("zb", 0, K), A("zi", 0, K), -1.0, OP.mult, 255.0, OP.add)
+        for x in range(16):
+            mm(A("ps5", 0, 32), sel("w2", x), A("zb", x, K, 16), False, x == 15)
+        cp(A("hi", 0, 32), A("ps5", 0, 32))
+        ts(A("ow", 0, 32), A("hi", 0, 32), 15, OP.bitwise_and)
+        for o in range(9):
+            ts(A("ind", 32 * o, 32 * o + 32), A("ow", 0, 32), float(2 * o + 1) if o < 8 else 0.0, OP.is_equal)
+        mm(A("ps1", 0, 288), IDN, A("cj", 1312, 1600), True, False)
+        mm(A("ps1", 0, 288), OB, A("ind", 0, 288), False, True)
+        mm(A("ps0", 0, 288), c["nsl"], A("ind", 0, 288), True, True)
+        scan(A("cs", 0, 288), A("cj", 738, 1026), A("ps1", 0, 288), 0.0, OP.mult, OP.add)
+        tt(A("cd", 0, 288), A("ps0", 0, 288), A("cs", 0, 288), OP.add)
+        tt(A("mt", 0, 128), A("cd", 0, 128), A("cd", 128, 256), OP.min)
+        tt(A("mt", 128, 192), A("mt", 0, 64), A("mt", 64, 128), OP.min)
+        tt(A("mt", 192, 224), A("mt", 128, 160), A("mt", 160, 192), OP.min)
+        tt(A("mt", 0, 32), A("mt", 192, 224), A("cd", 256, 288), OP.min)
+        ts(A("ql", 0, 32), A("mt", 0, 32), -1.0, OP.add)
+        cp(IX("swin", 0, 9 * ST, "ql", 0, 32), A("zb", 0, K))
+        land = "land%d" % rnd
+        send(lambda r: A("swin", r * ST, r * ST + 32), A(land, rank * 32, rank * 32 + 32), "ka%d" % rnd, "ks%d" % rnd, [A("fwin", 0, 9 * ST)] if rnd == 0 else [])
+        cp(A(land, rank * 32, rank * 32 + 32), A("swin", rank * ST, rank * ST + 32))
+        cp(A("lrep", 0, K), A("ps6", 0, K))
+        if rnd == 0:
+            ms(A("cwin", 0, K), 0.0)
+            for o in range(8):
+                ms(A("swin", o * ST, o * ST + 32), -1.0)
+
+    def owner(rnd):
+        ld = "land%d" % rnd
+        land = A(ld, 0, 256)
+        nel = A("nel", 0, 256)
+        arrive("ka%d" % rnd, [A(ld, 32 * r, 32 * r + 32) for r in range(8) if r != rank])
+        for x in range(16):
+            mm(A("ps0", 0, 16), sel("w2", x), A(ld, x, 256, 16), x == 0, x == 15)
+        mm(A("ps1", 0, 256), c["obw2"], land, True, True)
+        ts(A("nel" if rnd == 0 else "inv", 0, 256), land, 0.0, OP.is_lt)
+        cp(A("hli", 0, 16), A("ps0", 0, 16))
+        ts(A("pli", 0, 16), A("hli", 0, 16), 32767, OP.bitwise_and, 4, OP.arith_shift_right)
+        if rnd == 1:
+            cp(A("plu", 0, 16), A("pli", 0, 16))
+            tt(A("ne", 0, 256), IX("store", 0, TS + 256, "plu", 0, 16), land, OP.not_equal)
+            mm(A("ps2", 0, 256), c["obm"], A("inv", 0, 256), True, False)
+            mm(A("ps2", 0, 256), OB, A("ne", 0, 256), False, True)
+            ts(nel, A("ps2", 0, 256), 0.5, OP.is_lt)
+        cp(A("hri", 0, 256), A("ps1", 0, 256))
+        ts(A("hri", 0, 256), A("hri", 0, 256), 32767, OP.bitwise_and, 4, OP.arith_shift_right)
+        cp(A("prh", 0, 256), A("hri", 0, 256))
+        mm(A("ps5", 0, 256), c["ob4"], nel, True, False)
+        if rnd == 0:
+            ts(A("sx", 0, 16), A("hli", 0, 16), 0.0, OP.is_lt, -8192.0, OP.mult)
+            tt(A("pm", 0, 16), A("sx", 0, 16), A("pli", 0, 16), OP.add)
+        else:
+            for x in range(16):
+                mm(A("ps4", 0, 16), sel("n512", x), A("nel", x, 256, 16), x == 0, x == 15)
+            tt(A("pm", 0, 16), A("ps4", 0, 16), A("pli", 0, 16), OP.add)
+        tt(A("dg", 0, 256), IX("pm", 0, 16, "qd", 0, 16), A("prh", 0, 256), OP.is_equal)
+        mm(A("ps5", 0, 256), c["obp"], A("dg", 0, 256), False, False)
+        for a in range(15):
+            m = 256 * a - 8 * a * (a - 1)
+            n = 240 - 16 * a
+            ts(A("mb", m, m + n), A("prh", 16 * a + 16, 256), A("pm", a, a + 1), OP.is_equal)
+            mm(A("ps5", 16 * a + 16, 256), c["ob4"], A("mb", m, m + n), False, a == 14)
+        tt(A("nw", 0, 256), A("ps5", 0, 256), A("ck", 1536, 1792), OP.is_lt)
+        send(lambda r: A("nw", r * 32, r * 32 + 32), A("fwin", rank * ST, rank * ST + 32), "fa%d" % rnd, "fs%d" % rnd)
+        cp(A("fwin", rank * ST, rank * ST + 32), A("nw", rank * 32, rank * 32 + 32))
+        arrive("fa%d" % rnd, [A("fwin", ST * r, ST * r + 32) for r in range(8) if r != rank])
+
+    def store(rnd):
+        for x in range(16):
+            mm(A("ps5", 0, 16), sel("six", x), A("nw", x, 256, 16), x == 0, x == 15)
+        tt(A("sx", 0, 16), A("pli", 0, 16), A("ck", 1296, 1312), OP.subtract)
+        tt(A("sy", 0, 16), A("ps5", 0, 16), A("sx", 0, 16), OP.mult)
+        tt(A("sz", 0, 16), A("sy", 0, 16), A("ck", 1296, 1312), OP.add)
+        cp(A("su", 0, 16), A("sz", 0, 16))
+        cp(IX("store", 0, TS + 256, "su", 0, 16), A("land%d" % rnd, 0, 256))
+        if rnd == 1:
+            dma("y", "yt", A("store", 0, TS), "w0", 4.1)
+
+    def nextfront(rnd):
+        cum = A("ncu", 520, 1032)
+        hold = A("hold", 0, F)
+        tt(A("ncu", 8, 520), IX("fwin", 0, 9 * ST, "ql", 0, 32), A("lrep", 0, K), OP.mult)
+        scan(A("ncu", 520, 1033), A("ncu", 7, 520), A("cj", 224, 737), 0.0, OP.add, OP.min)
+        for x in range(16):
+            mm(A("ps0", 0, 64), sel("six", x), A("ncu", 8 + x, 1032, 16), x == 0, x == 15)
+        ts(A("ex", 0, K), A("ncu", 521, 1033), 224.0, OP.is_gt, 8448.0, OP.mult)
+        mm(A("ps3", 0, K), c["ob16"], A("ex", 0, K), False, True)
+        ts(A("unf", 0, F), A("ck", 512, 736), A("ncu", 1032, 1033), OP.is_ge, 8448.0, OP.mult)
+        ts(A("ea", 0, 32), A("ps0", 0, 32), 0.0, OP.is_equal)
+        ts(A("s2", 0, 32), A("ps0", 32, 64), 224.0, OP.is_gt)
+        tt(A("eb", 0, 32), A("ea", 0, 32), A("ck", 1264, 1296), OP.mult)
+        tt(A("s3", 0, 32), A("s2", 0, 32), A("ck", 1232, 1264), OP.mult)
+        tt(A("st", 0, 32), A("eb", 0, 32), A("s3", 0, 32), OP.max)
+        tt(A("s5", 0, 32), A("ps0", 32, 64), A("st", 0, 32), OP.max)
+        cp(A("ofu", 0, 32), A("s5", 0, 32))
+        tt(A("d0", 0, K), A("ps3", 0, K), cum, OP.subtract)
+        cp(IX("pwin", 0, 1536, "ofu", 0, 32), A("d0", 0, K))
+        scan(hold, A("pwin", 0, F), A("unf", 0, F), 0.0, OP.max, OP.max)
+        tt(A("tauh", 0, F), hold, A("ck", 960, 1184), OP.add)
+        for x in range(16):
+            mm(A("ps2", 0, 14), A("ch", 16 - x, 144 - x), A("tauh", x, F, 16), x == 0, x == 15)
+        tt(A("taui", 0, F), hold, A("ck", 736, 960), OP.add)
+        ts(A("taui", 0, F), A("taui", 0, F), 8207, OP.bitwise_and)
+        ts(A("oh2", 0, F), A("taui", 0, F), PI, OP.is_equal)
+        ts(A("tj", 0, 14), A("ps2", 0, 14), 1.0 / 256, OP.mult, 128.0 - 15.0 / 32, OP.add)
+        ts(A("tju", 0, 14), A("tj", 0, 14), 223.0, OP.min)
+        tt(A("suv", 0, F), IX("uf", 0, F, "tju", 0, 14), A("oh2", 0, F), OP.mult)
+        tt(A("suv", F, 2 * F), IX("vf", 0, F, "tju", 0, 14), A("oh2", 0, F), OP.mult)
+        ts(A("fa", 0, F), A("pwin", 0, F), 0.0, OP.is_gt)
+        ts(A("fb", 0, F), hold, 8192.0, OP.is_ge)
+        if rnd == 0:
+            for x in range(16):
+                mm(A("ps4", 0, 28), A("ch", 16 - x, 144 - x), A("suv", x, 2 * F, 16), x == 0, x == 15)
+            for x in (0, 14):
+                ts(A("adl", x, x + 14), A("tj", 0, 14), 375.0, OP.is_lt, 1536.0, OP.mult)
+            tt(A("flg", 0, F), A("fa", 0, F), A("fb", 0, F), OP.max)
+            tt(A("uvs", 0, 28), A("ps4", 0, 28), A("adl", 0, 28), OP.add)
+            cp(A("uv", 0, 28), A("uvs", 0, 28))
+            expand()
+            ms(A("pwin", 0, F), 0.0)
+        else:
+            row = (0, 128, 16)
+            mm(A("ps4", 0, F), A("ch", 144, 272), A("suv", 0, F), True, True)
+            mm(A("ps1", 0, F), A("ch", 144, 272), A("suv", F, 2 * F), True, True)
+            ts(A("adr", 0, F), hold, 8000.0, OP.is_lt, 1536.0, OP.mult)
+            tt(A("fin", 2 * F, 3 * F), A("fa", 0, F), A("fb", 0, F), OP.max)
+            dma("y", "ys", A("fin", 2 * F, 3 * F, 1, row), "w3", 2.0)
+            tt(A("fin", 0, F), A("ps4", 0, F), A("adr", 0, F), OP.add)
+            dma("y", "yu", A("fin", 0, F, 1, row), "w1", 2.0)
+            tt(A("fin", F, 2 * F), A("ps1", 0, F), A("adr", 0, F), OP.add)
+            dma("s", "yv", A("fin", F, 2 * F, 1, row), "w2", 2.0)
+
+    for rnd in range(2):
+        side()
+        big(rnd)
+        control(rnd)
+        owner(rnd)
+        store(rnd)
+        nextfront(rnd)
+    return ops
+
+
+def schedule(ops, hop=0.03):
+    n = len(ops)
+    ent = {}
+    succ = [[] for _ in ops]
+    left = [0] * n
+    sent = None
+    for i, o in enumerate(ops):
+        deps = set()
+        if o["q"] == "x":
+            deps.add(sent)
+        elif o["q"] == "g" and o["sem"]:
+            sent = i
+        acc = [(b, c0, c1, w, wh) for w, lst in ((False, o["r"]), (True, o["w"])) for (b, c0, c1), wh in zip(lst, o["whole"] if w else [False] * len(lst))]
+        acc = [(b, 0, 512, True, True) if bank(b) else (b, c0, c1, w, wh) for b, c0, c1, w, wh in acc]
+        for b, c0, c1, w, wh in acc:
+            for d0, d1, j, jw in ent.get(b, []):
+                if d0 < c1 and c0 < d1 and (w or jw):
+                    deps.add(j)
+        for b, c0, c1, w, wh in acc:
+            e = ent.setdefault(b, [])
+            if w and wh:
+                e[:] = [y for y in e if not (c0 <= y[0] and y[1] <= c1)]
+            e.append((c0, c1, i, w))
+        deps.discard(i)
+        left[i] = len(deps)
+        for j in deps:
+            succ[j].append(i)
+    tail = [0.0] * n
+    for i in range(n - 1, -1, -1):
+        tail[i] = ops[i]["est"] + max([tail[k] for k in succ[i]], default=0.0)
+    can = [0.0] * n
+    free = {}
+    ready = {}
+    for i, o in enumerate(ops):
+        if left[i] == 0:
+            ready.setdefault(o["q"], []).append(i)
+    line = {q: [i for i, o in enumerate(ops) if o["q"] == q] for q in "gy"}
+    order = []
+    dmas = 0.0
+    while len(order) < n:
+        best = None
+        for q, lst in ready.items():
+            if q in line:
+                lst = [i for i in lst if i == line[q][0]]
+            if not lst:
+                continue
+            f = free.get(q, 0.0)
+            m = min(max(f, can[i]) for i in lst)
+            i = max((i for i in lst if max(f, can[i]) <= m), key=lambda i: tail[i])
+            k = (max(f, can[i]), -tail[i], i)
+            if best is None or k < best:
+                best = k
+        t, _, i = best
+        o = ops[i]
+        q = o["q"]
+        ready[q].remove(i)
+        if q in line:
+            line[q].pop(0)
+        end = t + o["est"]
+        free[q] = end
+        if o["sem"] and q in "ys":
+            end = max(t, dmas) + o["est"]
+            dmas = end - 2.0
+            free[q] = t + 0.1
+        elif o["sem"] and q == "g":
+            free[q] = t + 1.0
+        order.append(o)
+        for k in succ[i]:
+            can[k] = max(can[k], end + (0.0 if q == "t" and ops[k]["q"] == "t" else hop))
+            left[k] -= 1
+            if left[k] == 0:
+                ready.setdefault(ops[k]["q"], []).append(k)
+    return order
+
+
+def sync(ops):
+    ent = {}
+    know = {}
+    snap = []
+    qn = {}
+    for i, o in enumerate(ops):
+        q = o["q"]
+        deps = set()
+        for w, lst in ((False, o["r"]), (True, o["w"])):
+            for b, c0, c1 in lst:
+                ps = bank(b)
+                if ps:
+                    c0, c1 = 0, 512
+                for (d0, d1, j, jw) in ent.get(b, []):
+                    if d0 >= c1 or c0 >= d1:
+                        continue
+                    same = ops[j]["q"] == q and ops[j]["sem"] is None
+                    if ps and same and (q == "t" or not (w or jw)):
+                        continue
+                    if not (w or jw) and not ps:
+                        continue
+                    deps.add(j)
+        kn = know.setdefault(q, {})
+        waits = []
+        for j in sorted(deps, reverse=True):
+            key = ops[j]["sem"] or ops[j]["q"]
+            if kn.get(key, -1) >= ops[j]["n"]:
+                continue
+            waits.append(j)
+            for k, v in list(snap[j].items()) + [(key, ops[j]["n"])]:
+                if kn.get(k, -1) < v:
+                    kn[k] = v
+        o["n"] = 0 if o["sem"] else qn.get(q, 0)
+        qn[q] = qn.get(q, 0) + 1
+        o["waits"] = waits
+        snap.append(dict(kn))
+        for w, lst in ((False, o["r"]), (True, o["w"])):
+            for x, (b, c0, c1) in enumerate(lst):
+                ps = bank(b)
+                if ps:
+                    c0, c1 = 0, 512
+                e = ent.setdefault(b, [])
+                if (ps and q != "t") or (w and not ps and o["whole"][x]):
+                    e[:] = [y for y in e if not (c0 <= y[0] and y[1] <= c1)]
+                elif ps:
+                    e[:] = [y for y in e if ops[y[2]]["q"] == "t"][-1:] + [y for y in e if ops[y[2]]["q"] != "t"]
+                e.append((c0, c1, i, w))
+    need = set()
+    for o in ops:
+        need.update(o["waits"])
+    cnt = {}
+    for j, o in enumerate(ops):
+        o["cnt"] = None
+        if o["sem"] is None and j in need:
+            cnt[o["q"]] = cnt.get(o["q"], 0) + 1
+            o["cnt"] = cnt[o["q"]]
+    return cnt
+
+
+def rank_program(g, core, T, topo):
+    if T.rank_of(core) is None:
+        return
+    ops = schedule(build(core, T, topo))
+    cnt = sync(ops)
+    sems = {"v": "qv", "s": "qs", "t": "qt", "g": "qg"}
+    queue = {"v": g.vector, "s": g.scalar, "t": g.tensor, "g": g, "y": g.sync}
+    done = {}
+    for o in ops:
+        if o["sem"]:
+            done[o["sem"]] = o["inc"]
+        if o["fn"] is None:
+            continue
+        best = {}
+        for j in o["waits"]:
+            d = ops[j]
+            k, v = (d["sem"], d["inc"]) if d["sem"] else (sems[d["q"]], d["cnt"])
+            best[k] = max(best.get(k, 0), v)
+        for k, v in best.items():
+            queue[o["q"]].wait_ge(T.sem[k], v)
+        h = o["fn"](g)
+        if o["cnt"] is not None:
+            h.then_inc(T.sem[sems[o["q"]]], 1)
+        elif o["sem"] and o["q"] != "g":
+            h.then_inc(T.sem[o["sem"]], 16)
+    for q, n in cnt.items():
+        g.wait_ge(T.sem[sems[q]], n)
+    for k, v in done.items():
+        g.wait_ge(T.sem[k], v)

@@ -5,25 +5,26 @@ from concourse.mybir import AluOpType as OP, ActivationFunctionType as AF
 W, F, P, K, TS = 3072, 224, 3584, 512, 2048
 CW, NCH, LC = 448, 8, 28
 ST = 512
-CLAMP = 7168.0
+TW = P + 16
+KS = K + 16
+CLAMP = 6912.0
 LN4, LN2 = math.log(4.0), math.log(2.0)
 CFG = {
-    "vs": ["vvvsssvv", "vsvvvsss"],
-    "qs": ["vsssssss", "ssvsvsss"],
-    "cs": ["vssvssss", "vvsvssss"],
+    "vs": ["vvvvvvss", "vvvvvvss"],
+    "qs": ["vsssssss", "vsssssss"],
+    "gr": [[[0], [1], [2, 3], [4, 5], [6, 7]], [[0], [1], [2, 3], [4, 5], [6, 7]]],
 }
 
 SCRATCH = {}
 for _d, _l in (
-    ("int32", "kidb:3072 fuv:28 fsb:224 rmi:2 li:224 zi:512 hi:32 ow:32 hri:256 hli:16 pli:16 taui:224 tj:16 cint:160 cpi:160"),
-    ("uint16", "uv:28 ku:224 kv:224 cof:16 jl:32 t1u:32 t0u:32 ql:32 plu:16 su:16 ofu:32 tju:16 qd:16"),
-    ("float16", "prh:256 tauh:224 suv:448 ch:272"),
-    ("bfloat16", "vecb:3072 markb:3072 va:1792 vb:1792 nz:3584 qa:3584 mq:3584 msk:3584 flg:232 fsf:224 last:232 z0:232 z0m:224 cand:224 "
-     "nls:16 cwin:7920 jk:512 oh:512 lh:512 lrep:512 zb:512 ind:288 swin:4608 fwin:4608 land0:256 land1:256 store:2304 inv:256 ne:256 "
-     "nel:256 mb:2176 dg:256 nw:256 ncu:1040 ex:512 fa:224 fb:224 cb:4400 cj:1600"),
-    ("float32", "uf:224 vf:224 dd:3584 dc:3584 run:3592 rmf:2 lbig:224 eqt:224 gam:224 m2:224 aa:224 wm:224 yl:224 cinc:224 rf:224 et:16 "
-     "ci:16 o1:16 o2:16 t1s:32 t0s:32 r1:512 cs:288 cd:288 mt:224 pm:16 sx:16 sy:16 sz:16 ea:32 eb:32 st:32 s2:32 s3:32 s5:32 "
-     "d0:512 pwin:1536 unf:224 hold:224 oh2:224 adl:28 uvs:28 fin:672 adr:224 cf:720 ck:4200"),
+    ("int32", "kidb:3072 fuv:28 fsb:224 rmi:2 zi:512 hi:32 ow:32 hri:256 hli:16 pli:16 pl2:16 cint:160 cpi:160"),
+    ("uint16", "uv:28 kk:448 cof:16 jl:32 t1u:32 t0u:32 ql:34 plu:16 su:16 ofu:34 tju:16 cu:24"),
+    ("float16", "prh:256 uvh:448 cs:288 prod:288 owf:32 cum:536 hold:224 ch:1200"),
+    ("bfloat16", "vecb:3072 markb:3072 va:1792 vb:1792 nz:1792 qa:3584 mq:3584 nf:232 fsf:224 adv:224 lbn:224 z0:232 drp:224 cand:224 lb:224 "
+     "nls:16 cwin:3808 jk:512 oh:512 lh:512 lrep:528 zb:512 ind:288 swin:4608 fwin:4624 land0:256 land1:256 store:2304 inv:256 ne:256 "
+     "nel:256 mb:2176 nw:256 xl:528 xf:224 cb:4600 cj:1400"),
+    ("float32", "dd:3584 run:3592 tuv:7200 eb:232 bc:224 rmf:2 yl:224 cinc:224 rf:224 ci:16 o1:16 o2:16 r1:512 pm:16 sn:16 sx:16 sy:16 sz:16 "
+     "yb:34 t0c:528 ex:528 pwin:2624 fin:672 cf:720 ck:2600"),
 ):
     for _x in _l.split():
         SCRATCH[_x.split(":")[0]] = ("sbuf", [128, int(_x.split(":")[1])], _d)
@@ -45,15 +46,16 @@ def bank(b):
 
 
 CYCLE = 0.00095
+GATHER, SCATTER = 1.4, 2.5
 
 
 def estimate(q, out, ins, two):
+    n = (out[2] - out[1] + out[3] - 1) // out[3] if len(out) == 5 else 0
     if q == "t":
-        return max(64, (out[2] - out[1])) / 1220.0
-    for a, rate in ((out, 2.5), (ins[0], 1.4)):
+        return max(64, n) * (4 if SCRATCH[ins[0][0]][2] == "float32" else 1) * CYCLE / 2
+    for a, rate in ((out, SCATTER), (ins[0], GATHER)):
         if len(a) == 6:
             return 0.06 + 16 * (a[5] - a[4]) * rate * CYCLE
-    n = (out[2] - out[1] + out[3] - 1) // out[3]
     f = 1.0
     if q == "g":
         return 0.13 + 2 * n * CYCLE
@@ -128,6 +130,9 @@ def build(core, T, topo):
         else:
             add("g", lambda g: g.iota(X(out), pat, base, cm), [], [out])
 
+    def fill(a, v):
+        iota(a, [[0, a[2] - a[1]]], v, 0, True)
+
     def dma(q, out, a, sem, est):
         o = (lambda: T[out][:]) if isinstance(out, str) else (lambda: X(out))
         i = (lambda: T[a][:]) if isinstance(a, str) else (lambda: X(a))
@@ -162,31 +167,52 @@ def build(core, T, topo):
     dma("y", A("kidb", 0, W), "kids", "l3", 8.3)
     dma("y", A("vecb", 0, W), "vec", "l4", 5.1)
     dma("y", A("markb", 0, W), "mark", "l5", 5.1)
+    KC = A("ck", 0, K)
+    S16 = A("ck", 512, 545)
+    QM = A("ck", 560, 816)
+    THR = A("ck", 816, 1072)
+    CAP = A("ck", 1072, 1600)
+    ZERO = A("ck", 1600, 1824)
+    JC = A("ck", 1824, 1838)
+    QC = A("ck", 1840, 1856)
+    NC = A("ck", 1856, 1889)
+    R32 = A("ck", 1896, 1914)
+    I32 = A("ck", 1920, 2048)
+    D, DLO, DHI = A("ck", 2048, 2176), A("ck", 2176, 2304), A("ck", 2304, 2432)
+    JV = A("cj", 0, F)
+    M16 = A("cj", 224, 672)
+    M32 = A("cj", 672, 960)
+    OWN = A("cj", 960, 1248)
+    ONE = A("cj", 225, 226)
     iota(A("cint", 0, 1), [[0, 1]], 0, 1, False)
     iota(A("cint", 8, 152), [[1, 144]], 0, 0, False)
-    iota(A("msk", 0, P), [[0, P]], 1, 0, True)
-    iota(A("ck", 0, 512), [[1, 512]], 8193, 0, True)
-    iota(A("ck", 512, 736), [[1, F]], 0, 0, True)
-    iota(A("ck", 736, 960), [[1, F]], -1, 0, True)
-    iota(A("ck", 960, 1184), [[1, F]], -2049, 0, True)
-    iota(A("ck", 1184, 1216), [[16, 32]], 0, 0, True)
-    iota(A("ck", 2560, 2816), [[0, 16], [1, 16]], 0, 0, True)
-    iota(A("cj", 0, F), [[1, F]], 0, 0, True)
-    iota(A("ck", 1792, 2080), [[ST, 9], [0, 32]], 8192, 0, True)
-    for a, v in ((A("cj", 224, 738), 255), (A("cj", 738, 1026), 1), (A("ck", 1312, 1536), 0), (A("z0", 0, F + 8), 1), (A("last", 0, F + 8), 0),
-                 (A("run", 0, 8), 0), (A("cwin", 0, K), 0), (A("pwin", 0, F), 0), (A("ncu", 0, 8), 0), (A("swin", 0, 8 * ST), -1),
-                 (A("fwin", 0, 9 * ST), 0), (A("store", 0, TS + 256), -1)):
-        iota(a, [[0, a[2] - a[1]]], v, 0, True)
+    iota(S16, [[16, 33]], 0, 0, True)
+    iota(R32, [[0, 9], [16, 2]], 0, 0, True)
+    fill(A("cj", 224, 960), 1)
+    for a, v in ((A("nf", F, F + 8), 0), (A("eb", 0, 8), 0), (A("z0", 0, 8), 1), (A("run", 0, 8), 0), (ZERO, 0)):
+        fill(a, v)
+    iota(QM, [[0, 16], [1, 16]], 0, 0, True)
+    iota(JV, [[1, F]], 0, 0, True)
+    fill(A("cwin", 0, K), 0)
+    iota(KC, [[1, K]], -8192, 0, True)
+    iota(CAP, [[1, KS]], 256, 0, True)
+    iota(A("cj", 960, 1216), [[2, 8], [0, 32]], 1, 0, True)
+    fill(A("cj", 1216, 1248), 0)
+    for o in range(8):
+        fill(A("swin", o * ST, o * ST + 32), -1)
+    for a, v in ((A("fwin", 0, 9 * ST + 16), 0), (A("fwin", 9 * ST, 9 * ST + 1), 1), (A("store", 0, TS + 256), -1), (A("pwin", 0, 2 * F), -2048),
+                 (A("lrep", K, KS), F + 1), (A("t0c", K, KS), 0), (A("xf", 0, F), 1)):
+        fill(a, v)
     P0 = A("cf", 0, 1)
     PI = A("cf", 1, 2)
     PG = A("cf", 2, 3)
     PB = A("cf", 3, 4)
     W2 = A("cf", 4, 5)
-    M15 = A("cf", 5, 6)
-    PW = A("cf", 6, 7)
-    P4 = A("cf", 7, 8)
-    PI2 = A("cf", 8, 9)
-    MBIG = A("cf", 10, 11)
+    MB = A("cf", 5, 6)
+    MBN = A("cf", 6, 7)
+    PW = A("cf", 7, 8)
+    P128 = A("cf", 8, 9)
+    P129 = A("cf", 9, 10)
     NL4 = A("cf", 12, 13)
     cp(P0, A("cint", 0, 1))
     ts(A("cpi", 0, 1), A("cint", 0, 1), 15, OP.bitwise_and)
@@ -194,9 +220,10 @@ def build(core, T, topo):
     cp(A("cf", 1, 3), A("cpi", 0, 2))
     ts(PB, PG, 16.0, OP.mult, 16.0, OP.add)
     ts(W2, PI, -28.0, OP.mult, 510.0, OP.add)
-    ts(M15, PI, 15.0, OP.is_equal)
-    ts(MBIG, M15, 2.0 ** 24, OP.mult)
-    ts(PI2, PI, 2.0, OP.add)
+    ts(MB, PI, 15.0, OP.is_equal, 2.0 ** 19, OP.mult)
+    ts(MBN, MB, -1.0, OP.mult, -0.5, OP.add)
+    ts(P128, PI, 128.0, OP.add)
+    ts(P129, PI, 129.0, OP.add)
     YC = A("cf", 16, 160)
     Y128 = A("cf", 16, 144)
     MI = A("cf", 160, 288)
@@ -226,214 +253,213 @@ def build(core, T, topo):
         sel_[name] = a[1]
 
     def sel(name, i):
+        if name in ("h16", "h8"):
+            b = {"h16": 0, "h8": 144}[name] + 16 - i
+            return A("ch", b, b + 128)
         b = sel_[name] + 16 - i
         return A("cb", b, b + 128)
+
+    def tolist(out, name, b, c0, c1, start, stop):
+        for x in range(16):
+            mm(out, sel(name, x), A(b, c0 + x, c1, 16), start and x == 0, stop and x == 15)
+
     mksel("one", None)
     IDN, IDM, OB, REP = cbuf(128), cbuf(128), cbuf(128), cbuf(128)
+    I16, IM16, CAPH = A("ch", 288, 416), A("ch", 416, 544), A("ch", 544, 544 + KS)
     ts(IDN, Y128, P0, OP.is_equal)
     act(IDM, IDN, AF.Copy, scale=-1.0)
+    act(I32, IDN, AF.Copy)
     act(OB, BLK, AF.Copy)
     ts(REP, MG, P0, OP.is_equal)
+    ts(I16, Y128, P0, OP.is_equal)
+    ts(IM16, Y128, P0, OP.is_equal, -1.0, OP.mult)
+    ms(A("cj", 224, 672, 16), 0.0)
+    ms(A("cu", 0, 2), 0)
     cp(A("uv", 0, 28), A("fuv", 0, 28))
     add("v", lambda g: g.vector.tensor_copy(T.fsf[0:8, :], T.fsb[0:8, :]), [A("fsb", 0, F)], [A("fsf", 0, F)])
     add("t", lambda g: g.tensor.matmul(T.ps0[:, 0:F], T.cb[0:8, REP[1]:REP[2]], T.fsf[0:8, :], True, True), [REP, A("fsf", 0, F)], [A("ps0", 0, F)])
-    ms(A("flg", 0, F + 8), 1.0)
-    cp(A("flg", 0, F), A("ps0", 0, F))
-
-    def expand():
-        cp(A("ku", 0, F), IX("kidb", 0, W, "uv", 0, 14))
-        cp(A("kv", 0, F), IX("kidb", 0, W, "uv", 14, 28))
-        ts(A("msk", 0, P, 16), A("flg", 0, F), -1.0, OP.mult, 1.0, OP.add)
-        ts(A("uf", 0, F), A("ku", 0, F), -1536.0, OP.add)
-        ts(A("vf", 0, F), A("kv", 0, F), -1536.0, OP.add)
-
-    E, U, D = A("ck", 3792, 3920), A("ck", 3920, 4048), A("ck", 4048, 4176)
-    for name, wt in (("six", 1.0 / 16), ("pi", PI), ("w2", W2), ("n512", -512.0)):
+    ts(A("nf", 0, F), A("ps0", 0, F), -1.0, OP.mult, 1.0, OP.add)
+    mksel("neg", -1.0)
+    cp(A("kk", 0, F), IX("kidb", 0, W, "uv", 0, 14))
+    cp(A("kk", F, 2 * F), IX("kidb", 0, W, "uv", 14, 28))
+    for name, wt in (("six", 1.0 / 16), ("pi", PI), ("p128", P128), ("w2", W2), ("n256", -256.0)):
         mksel(name, wt)
     act(PW, PI, AF.Exp, scale=-LN2)
-    act(P4, PI, AF.Exp, scale=LN4)
-    E4 = cbuf(128)
-    act(E4, MI, AF.Exp, scale=-LN4)
-    pw = cbuf(16)[1]
-    cp(A("cb", pw, pw + 2), A("cf", 6, 8))
-    cp(A("cf", 9, 10), A("cb", pw, pw + 1))
-    ts(E, E4, A("cb", pw + 1, pw + 2), OP.mult)
-    tt(E, E, BLK, OP.mult)
+    act(THR, QM, AF.Exp, bias=math.log(2.5), scale=-LN2)
     ts(D, MI, PI, OP.subtract)
-    for name, lo, hi_, f in (("b0", 1, 15, 1.0), ("b1", -15, 12, 4.0 ** -16), ("b2", -15, -4, 4.0 ** -32)):
-        c[name] = cbuf(128)
-        ts(U, D, float(lo), OP.is_ge, f, OP.mult)
-        ts(T1, D, float(hi_), OP.is_le)
-        tt(U, U, T1, OP.mult)
-        tt(c[name], U, E, OP.mult)
-    c["idm2"] = cbuf(128)
-    ts(T1, Y128, P0, OP.is_equal)
-    ts(c["idm2"], T1, -2.0, OP.mult)
-    expand()
+    ts(T1, BLK, 64.0, OP.mult, -64.0, OP.add)
+    tt(DLO, D, T1, OP.add)
+    tt(DHI, D, T1, OP.subtract)
+    for k, (src, v, op) in enumerate(((DLO, 1.0, OP.is_ge), (DHI, 12.0, OP.is_le), (DHI, -4.0, OP.is_le))):
+        c["wc%d" % k], c["b%d" % k] = cbuf(128), cbuf(128)
+        ts(c["wc%d" % k], src, v, op)
+        act(c["b%d" % k], D, AF.Exp, bias=-16.0 * k * LN4, scale=-LN4)
+        tt(c["b%d" % k], c["b%d" % k], c["wc%d" % k], OP.mult)
     c["nui"] = cbuf(128)
-    ts(U, D, 0.0, OP.is_le, -1.0, OP.mult)
-    tt(U, U, BLK, OP.mult)
-    cp(c["nui"], U)
-    for name, v in (("rkm", 8193.0), ("nsl", -8191.0)):
+    ts(c["nui"], DHI, 0.0, OP.is_le, -1.0, OP.mult)
+    for name, wt in (("p64", 64.0), ("n8k", -8192.0), ("i4352", 4352.0)):
         c[name] = cbuf(128)
-        ts(E, T1, v, OP.mult)
-        tt(E, E, U, OP.add)
-        cp(c[name], E)
-    for name, wt in (("obw2", W2), ("obp", A("cf", 9, 10)), ("obpi", PI2), ("ob4", 4.0), ("ob16", 1.0 / 16), ("obm", -1.0)):
+        act(c[name], IDN, AF.Copy, scale=wt)
+    for name, wt in (("obw2", W2), ("obp", PW), ("obpi", P129), ("ob4", 4.0), ("obm", -1.0), ("obn", -128.0)):
         c[name] = cbuf(128)
         act(c[name], BLK, AF.Copy, scale=wt)
-    cp(A("qd", 0, 16), A("cf", 16, 32))
-    ts(A("ch", 0, 144), YC, PB, OP.is_equal)
-    cp(A("ch", 144, 272), BLK)
-    ts(A("ck", 1216, 1230), A("ck", 1184, 1198), PI, OP.add, 4096.0, OP.add)
-    ts(A("ck", 1232, 1264), A("ck", 1184, 1216), PI, OP.add, 256.0, OP.add)
-    ts(A("ck", 1264, 1296), A("ck", 1184, 1216), PI, OP.add, 1024.0, OP.add)
-    ts(A("ck", 1296, 1312), A("ck", 1184, 1200), PI, OP.add, 2048.0, OP.add)
-    act(A("ck", 1536, 1792), A("ck", 2560, 2816), AF.Exp, scale=-LN2)
-    cp(A("cj", 1056, 1312), A("ck", 1536, 1792))
-    ts(A("ck", 1536, 1792), A("cj", 1056, 1312), 2.0, OP.mult)
-    act(A("cf", 11, 12), A("cj", 1058, 1059), AF.Ln)
+    ts(A("ch", 0, 144), YC, PB, OP.is_equal, 1.0 / 16, OP.mult)
+    ts(A("ch", 144, 288), YC, PB, OP.is_equal, 1.0 / 8, OP.mult)
+    ts(JC, A("ck", 512, 526), PI, OP.add, float(P), OP.add)
+    ts(QC, A("ck", 512, 528), PI, OP.add, float(TS), OP.add)
+    ts(NC, S16, PI, OP.add, 0.5, OP.add)
+    ts(NC, NC, 2.0, OP.mult)
+    ts(A("cu", 2, 20), R32, PI, OP.add)
+    ts(A("ql", 32, 33), PI, 0.0, OP.is_gt, 9.0 * ST, OP.add)
+    cp(CAPH, CAP)
+    ms(A("cj", 672, 960, 32), 0.0)
+    ts(A("cum", 0, 8), A("ck", 1600, 1608), 0.0, OP.add)
+    add("s", lambda g: g.scalar.activation(X(A("cf", 11, 12)), X(ONE), AF.Ln, scale=0.25), [ONE, PW, THR, c["b0"], c["b1"], c["b2"]], [A("cf", 11, 12)], est=1.6)
     add("v", lambda g: g.vector.reciprocal(T.cf[:, 12:13], T.cf[:, 11:12]), [A("cf", 11, 12)], [NL4])
-    ms(A("cj", 738, 1026, 32), 0.0)
-    ts(A("ck", 2080, 2368), A("cj", 738, 1026), -1.0, OP.mult, 1.0, OP.add)
-    tt(A("ck", 1792, 2080), A("ck", 1792, 2080), A("ck", 2080, 2368), OP.mult)
-    cp(A("cj", 1312, 1600), A("ck", 1792, 2080))
+
+    def side():
+        ts(A("lbn", 0, F), A("nf", 1, F + 1), MB, OP.mult, MBN, OP.add)
+        ts(A("uvh", 0, 2 * F), A("kk", 0, 2 * F), -1536.0, OP.add)
+        mm(A("ps7", 0, F), I16, A("uvh", 0, F), True, False)
+        mm(A("ps7", 0, F), IM16, A("uvh", F, 2 * F), False, True)
+        act(A("adv", 0, F), A("ps7", 0, F), AF.Abs)
 
     def big(rnd):
-        vs, qs, cs = [CFG[k][rnd] for k in ("vs", "qs", "cs")]
-        size = 0
+        vs, qs, gr = [CFG[k][rnd] for k in ("vs", "qs", "gr")]
+        for n, grp in enumerate(gr):
+            for i in grp:
+                vl = (i % 4) * CW
+                va, vb = A("va", vl, vl + CW), A("vb", vl, vl + CW)
+                iv = IX("vecb", 0, W, "kk", F + i * LC, F + i * LC + LC)
+                act(va, IX("vecb", 0, W, "kk", i * LC, i * LC + LC), AF.Copy)
+                if vs[i] == "s":
+                    act(vb, iv, AF.Copy)
+                else:
+                    tt(vb, iv, va, OP.subtract)
+            j0, j1 = grp[0] * LC, (grp[-1] + 1) * LC
+            vl, vh = (grp[0] % 4) * CW, (grp[-1] % 4 + 1) * CW
+            two = vs[grp[0]] == "s"
+            sb = A("ps%d" % (4 + n % 2), 0, j1 - j0)
+            for x in range(16):
+                if two:
+                    mm(sb, IDN, A("va", vl + x, vh, 16), x == 0, False)
+                mm(sb, IDM, A("vb", vl + x, vh, 16), x == 0 and not two, x == 15)
+            for i in grp:
+                vl = (i % 4) * CW
+                if two:
+                    mm(A("ps%d" % (i % 4), 0, CW), IDN, A("va", vl, vl + CW), True, False)
+                mm(A("ps%d" % (i % 4), 0, CW), IDM, A("vb", vl, vl + CW), not two, False)
+            scan(A("eb", 1 + j0, 1 + j1), sb, A("nf", 1 + j0, 1 + j1), A("eb", j0, j0 + 1), OP.add, OP.mult)
+            ts(A("bc", j0, j1), A("eb", j0, j1), CLAMP, OP.min, -CLAMP, OP.max)
+            for i in grp:
+                lo, vl = i * CW, (i % 4) * CW
+                mm(A("ps%d" % (i % 4), 0, CW, 16), I32, A("bc", i * LC, i * LC + LC), False, True)
+                scan(A("dd", lo, lo + CW), M16, A("ps%d" % (i % 4), 0, CW), 0.0, OP.mult, OP.add)
+                act(A("nz", vl, vl + CW), A("dd", lo, lo + CW), AF.Abs)
+                if i % 2 == 1:
+                    tolist(A("ps6", (i - 1) * LC, (i + 1) * LC), "neg", "nz", vl - CW, vl + CW, True, True)
         for i in range(NCH):
             lo = i * CW
-            vl = (i % 4) * CW
-            va, vb = A("va", vl, vl + CW), A("vb", vl, vl + CW)
-            iv = IX("vecb", 0, W, "kv", i * LC, i * LC + LC)
-            act(va, IX("vecb", 0, W, "ku", i * LC, i * LC + LC), AF.Copy)
-            src, op = vb, OP.subtract
-            if vs[i] == "s":
-                act(vb, iv, AF.Copy)
-                src, op = A("ps%d" % (i % 2), 0, CW), OP.add
-                mm(src, IDN, va, True, False)
-                mm(src, IDM, vb, False, True)
-            else:
-                tt(vb, iv, va, OP.subtract)
-            d = A("dd", lo, lo + CW)
-            scan(d, A("msk", lo, lo + CW), src, 0.0 if i == 0 else A("dd", lo - 1, lo), OP.mult, op)
-            act(A("nz", lo, lo + CW), d, AF.Abs)
-            if i % 2 == 1:
-                b = (i - 1) * CW
-                for x in range(16):
-                    mm(A("ps2", (i - 1) * LC, (i + 1) * LC), sel("one", x), A("nz", b + x, b + 2 * CW, 16), x == 0, x == 15)
-        for i in range(NCH):
-            lo = i * CW
-            d, dc, m, qa = [A(b, lo, lo + CW) for b in ("dd", "dc", "mq", "qa")]
-            o = A("run", lo + 8, lo + 8 + CW)
-            iu = IX("markb", 0, W, "ku", i * LC, i * LC + LC)
+            d, m, qa = [A(b, lo, lo + CW) for b in ("dd", "mq", "qa")]
+            iu = IX("markb", 0, W, "kk", i * LC, i * LC + LC)
             if qs[i] == "v":
                 cp(qa, iu)
             else:
                 act(qa, iu, AF.Copy)
-            tt(m, IX("markb", 0, W, "kv", i * LC, i * LC + LC), qa, OP.max)
+            tt(m, IX("markb", 0, W, "kk", F + i * LC, F + i * LC + LC), qa, OP.max)
             init = 0.0 if i == 0 else A("run", lo + 7, lo + 8)
-            step = CW * ((2 if cs[i] == "s" else 1) * CLAMP + 255)
-            size += step
-            if size > 2 ** 24 - 1:
-                size = step + 255
+            if i == NCH // 2:
                 cp(A("rmi", 0, 1), A("run", lo + 7, lo + 8))
                 ts(A("rmi", 1, 2), A("rmi", 0, 1), 255, OP.bitwise_and)
                 cp(A("rmf", 0, 1), A("rmi", 1, 2))
                 init = A("rmf", 0, 1)
-            if cs[i] == "v":
-                ts(dc, d, CLAMP, OP.min, -CLAMP, OP.max)
-                scan(o, dc, m, init, OP.add, OP.add)
-            else:
-                act(dc, d, AF.Relu, bias=CLAMP)
-                act(dc, dc, AF.Relu, bias=2 * CLAMP, scale=-1.0)
-                scan(o, m, dc, init, OP.add, OP.subtract)
+            scan(A("run", lo + 8, lo + 8 + CW), d, m, init, OP.add, OP.add)
 
-    def side():
-        ts(A("last", 2, 2 + F), A("flg", 1, F + 1), M15, OP.mult)
-        for k in range(3):
-            mm(A("ps3", 0, F), c["b%d" % k], A("last", 2 - k, 2 - k + F), k == 0, False)
-        ts(A("lbig", 0, F), A("flg", 1, F + 1), MBIG, OP.mult, 0.5, OP.add)
-        tt(A("eqt", 0, F), A("uf", 0, F), A("vf", 0, F), OP.is_equal)
-        tt(A("gam", 0, F), A("lbig", 0, F), A("eqt", 0, F), OP.subtract)
-        ts(A("m2", 0, F), A("gam", 0, F), 2.0 ** 24 - 1, OP.is_equal)
+    def tables(rnd):
+        if rnd == 1:
+            iota(A("kidb", 0, W), [[1, W]], 0, 0, False)
+        for h in range(2):
+            act(A("tuv", h * TW + P, h * TW + TW), IX("kidb", 0, W, "cu", 0, 1), AF.Copy)
+            for i in range(NCH):
+                act(A("tuv", h * TW + i * CW, h * TW + i * CW + CW), IX("kidb", 0, W, "kk", h * F + i * LC, h * F + i * LC + LC), AF.Copy)
 
     def control(rnd):
-        cnt = A("ps2", 0, F)
-        ts(A("z0", 2, 2 + F), cnt, 0.5, OP.is_le)
+        cnt = A("ps6", 0, F)
+        cand = A("cand", 0, F)
+        tt(A("z0", 2, 2 + F), cnt, A("lbn", 0, F), OP.is_ge)
+        tt(A("drp", 0, F), A("adv", 0, F), cnt, OP.is_le)
         for k in range(3):
-            mm(A("ps3", 0, F), c["b%d" % k], A("z0", 2 - k, 2 - k + F), False, False)
-        tt(A("z0m", 0, F), cnt, A("m2", 0, F), OP.is_lt)
-        mm(A("ps3", 0, F), c["idm2"], A("z0m", 0, F), False, True)
-        tt(A("aa", 0, F), cnt, A("gam", 0, F), OP.is_gt)
-        tt(A("cand", 0, F), A("ps3", 0, F), A("aa", 0, F), OP.is_gt)
-        for x in range(16):
-            mm(A("ps4", 0, 14), sel("one", x), A("cand", x, F, 16), x == 0, x == 15)
-        mm(A("ps5", 0, F), OB, A("cand", 0, F), True, True)
-        mm(A("ps6", 0, F), c["rkm"], A("cand", 0, F), True, True)
-        act(A("wm", 0, F), A("ps3", 0, F), AF.Relu)
-        act(A("yl", 0, F), A("wm", 0, F), AF.Ln, bias=2.0 ** -60)
-        cp(A("nls", 0, 14), A("ps4", 0, 14))
+            mm(A("ps1", 0, F), c["wc%d" % k], A("z0", 2 - k, 2 - k + F), k == 0, False)
+        mm(A("ps1", 0, F), c["p64"], A("z0", 2, 2 + F), False, False)
+        mm(A("ps1", 0, F), c["n8k"], A("drp", 0, F), False, True)
+        for k in range(3):
+            mm(A("ps0", 0, F), c["b%d" % k], A("z0", 2 - k, 2 - k + F), k == 0, k == 2)
+        ts(cand, A("ps1", 0, F), 64.0, OP.is_gt)
+        act(A("yl", 0, F), A("ps0", 0, F), AF.Ln, bias=2.0 ** -60)
+        act(A("lb", 0, F), A("yl", 0, F), AF.Identity, bias=128.1, scale=NL4)
+        mm(A("ps5", 0, 14), I32, JC, True, False)
+        tolist(A("ps2", 0, 14), "one", "cand", 0, F, True, True)
+        mm(A("ps3", 0, F), OB, cand, True, True)
+        mm(A("ps4", 0, F), c["nui"], cand, True, False)
+        mm(A("ps4", 0, F), c["n8k"], cand, False, False)
+        cp(A("nls", 0, 14), A("ps2", 0, 14))
         mm(A("ps7", 0, 14), OB, A("nls", 0, 14), True, True)
-        mm(A("ps2", 0, 14), c["nui"], A("nls", 0, 14), True, True)
-        ts(A("et", 0, 14), A("ps4", 0, 14), 0.0, OP.is_equal)
-        tt(A("et", 0, 14), A("et", 0, 14), A("ck", 1216, 1230), OP.mult)
-        scan(A("ci", 0, 14), A("ps7", 0, 14), A("ck", 1312, 1326), 0.0, OP.add, OP.max)
-        tt(A("o1", 0, 14), A("ps2", 0, 14), A("et", 0, 14), OP.add)
-        tt(A("o2", 0, 14), A("o1", 0, 14), A("ci", 0, 14), OP.add)
+        mm(A("ps6", 0, 14), c["nui"], A("nls", 0, 14), True, True)
+        mm(A("ps5", 0, 14), c["n8k"], A("nls", 0, 14), False, True)
+        scan(A("ci", 0, 14), A("ps7", 0, 14), A("ck", 1600, 1614), 0.0, OP.add, OP.add)
+        tt(A("o1", 0, 14), A("ps6", 0, 14), A("ci", 0, 14), OP.add)
+        tt(A("o2", 0, 14), A("ps5", 0, 14), A("o1", 0, 14), OP.max)
         cp(A("cof", 0, 14), A("o2", 0, 14))
-        cp(IX("cwin", 0, 7920, "cof", 0, 14), A("cj", 0, F))
+        cp(IX("cwin", 0, P + F, "cof", 0, 14), JV)
         scan(A("jk", 0, K), A("cwin", 0, K), A("cwin", 0, K), 0.0, OP.max, OP.max)
-        for x in range(16):
-            mm(A("ps4", 0, 32), sel("six", x), A("jk", x, K, 16), x == 0, x == 15)
-        for x in range(16):
-            mm(A("ps7", 0, 32), sel("one", x), A("jk", x, K, 16), x == 0, False)
-        mm(A("ps3", 0, K), OB, A("jk", 0, K), True, False)
-        scan(A("cinc", 0, F), A("ps5", 0, F), A("ck", 1312, 1312 + F), 0.0, OP.add, OP.max)
-        tt(A("rf", 0, F), A("ps6", 0, F), A("cinc", 0, F), OP.add)
-        ts(A("li", 0, F), A("yl", 0, F), NL4, OP.mult, 0.354, OP.add)
-        cp(A("jl", 0, 32), A("ps4", 0, 32))
-        tt(A("oh", 0, K), IX("rf", 0, F, "jl", 0, 32), A("ck", 0, K), OP.is_equal)
-        for x in range(16):
-            mm(A("ps7", 0, 32), sel("pi", x), A("oh", x, K, 16), False, x == 15)
-        mm(A("ps3", 0, K), c["obpi"], A("oh", 0, K), False, False)
-        tt(A("lh", 0, K), IX("li", 0, F, "jl", 0, 32), A("oh", 0, K), OP.mult)
-        for x in range(16):
-            mm(A("ps2", 0, 32), sel("one", x), A("lh", x, K, 16), x == 0, x == 15)
-        for x in range(16):
-            mm(A("ps5", 0, 32), sel("one", x), A("oh", x, K, 16), x == 0, False)
-        mm(A("ps6", 0, K), OB, A("lh", 0, K), True, True)
-        mm(A("ps3", 0, K), c["obm"], A("lh", 0, K), False, False)
-        ts(A("t1s", 0, 32), A("ps7", 0, 32), 8.0, OP.add)
-        ts(A("t1u", 0, 32), A("ps7", 0, 32), 8.0, OP.add)
-        tt(A("t0s", 0, 32), A("t1s", 0, 32), A("ps2", 0, 32), OP.subtract)
-        cp(A("t0u", 0, 32), A("t0s", 0, 32))
-        act(A("r1", 0, K), IX("run", 0, P + 8, "t1u", 0, 32), AF.Identity, bias=1.0)
-        tt(A("zi", 0, K), IX("run", 0, P + 8, "t0u", 0, 32), A("r1", 0, K), OP.subtract)
-        ts(A("zi", 0, K), A("zi", 0, K), 255, OP.bitwise_and)
-        ts(A("zb", 0, K), A("zi", 0, K), -1.0, OP.mult, 255.0, OP.add)
-        for x in range(16):
-            mm(A("ps5", 0, 32), sel("w2", x), A("zb", x, K, 16), False, x == 15)
-        cp(A("hi", 0, 32), A("ps5", 0, 32))
+        scan(A("cinc", 0, F), A("ps3", 0, F), ZERO, 0.0, OP.add, OP.add)
+        mm(A("ps4", 0, F), I32, A("cinc", 0, F), False, True)
+        act(A("rf", 0, F), A("ps4", 0, F), AF.Copy)
+        tolist(A("ps0", 0, 32), "six", "jk", 0, K, True, True)
+        tolist(A("ps1", 0, 32), "one", "jk", 0, K, True, False)
+        tolist(A("ps2", 0, 32), "one", "jk", 0, K, True, False)
+        mm(A("ps6", 0, K), OB, A("jk", 0, K), True, False)
+        cp(A("jl", 0, 32), A("ps0", 0, 32))
+        tt(A("oh", 0, K), IX("rf", 0, F, "jl", 0, 32), KC, OP.is_equal)
+        tolist(A("ps1", 0, 32), "pi", "oh", 0, K, False, True)
+        tolist(A("ps2", 0, 32), "p128", "oh", 0, K, False, False)
+        tolist(A("ps3", 0, 32), "one", "oh", 0, K, True, False)
+        tt(A("lh", 0, K), IX("lb", 0, F, "jl", 0, 32), A("oh", 0, K), OP.mult)
+        tolist(A("ps2", 0, 32), "neg", "lh", 0, K, False, True)
+        ts(A("t1u", 0, 32), A("ps1", 0, 32), 8.0, OP.add)
+        ts(A("t0u", 0, 32), A("ps2", 0, 32), 8.0, OP.add)
+        mm(A("ps6", 0, K), c["obpi"], A("oh", 0, K), False, False)
+        mm(A("ps6", 0, K), c["obm"], A("lh", 0, K), False, True)
+        mm(A("ps5", 0, K), c["obn"], A("oh", 0, K), True, False)
+        mm(A("ps5", 0, K), OB, A("lh", 0, K), False, True)
+        act(A("t0c", 0, K), A("ps6", 0, K), AF.Identity, bias=-P / 2.0)
+        act(A("lrep", 0, K), A("ps5", 0, K), AF.Copy)
+        for h in range(2):
+            a, b = h * 256, h * 256 + 256
+            act(A("r1", a, b), IX("run", 0, P + 8, "t1u", 16 * h, 16 * h + 16), AF.Identity, bias=1.0)
+            tt(A("zi", a, b), IX("run", 0, P + 8, "t0u", 16 * h, 16 * h + 16), A("r1", a, b), OP.subtract)
+            ts(A("zi", a, b), A("zi", a, b), 255, OP.bitwise_and)
+            act(A("zb", a, b), A("zi", a, b), AF.Identity, bias=255.0, scale=-1.0)
+            tolist(A("ps3", 16 * h, 16 * h + 16), "w2", "zb", a, b, False, h == 1)
+        cp(A("hi", 0, 32), A("ps3", 0, 32))
         ts(A("ow", 0, 32), A("hi", 0, 32), 15, OP.bitwise_and)
+        ind = A("ind", 0, 288)
+        tt(ind, IX("ow", 0, 32, "cu", 2, 20), OWN, OP.is_equal)
+        mm(A("ps7", 0, 288), OB, ind, True, True)
+        mm(A("ps4", 0, 288), c["nui"], ind, True, False)
+        ts(A("owf", 0, 32), A("ow", 0, 32), 256.0, OP.mult)
+        mm(A("ps0", 0, 32), c["i4352"], A("ind", 256, 288), True, False)
+        mm(A("ps0", 0, 32), I16, A("owf", 0, 32), False, False)
+        scan(A("cs", 0, 288), M32, A("ps7", 0, 288), 0.0, OP.mult, OP.add)
+        mm(A("ps4", 0, 288), I16, A("cs", 0, 288), False, True)
+        tt(A("prod", 0, 288), ind, A("ps4", 0, 288), OP.mult)
         for o in range(9):
-            ts(A("ind", 32 * o, 32 * o + 32), A("ow", 0, 32), float(2 * o + 1) if o < 8 else 0.0, OP.is_equal)
-        mm(A("ps1", 0, 288), IDN, A("cj", 1312, 1600), True, False)
-        mm(A("ps1", 0, 288), OB, A("ind", 0, 288), False, True)
-        mm(A("ps0", 0, 288), c["nsl"], A("ind", 0, 288), True, True)
-        scan(A("cs", 0, 288), A("cj", 738, 1026), A("ps1", 0, 288), 0.0, OP.mult, OP.add)
-        tt(A("cd", 0, 288), A("ps0", 0, 288), A("cs", 0, 288), OP.add)
-        tt(A("mt", 0, 128), A("cd", 0, 128), A("cd", 128, 256), OP.min)
-        tt(A("mt", 128, 192), A("mt", 0, 64), A("mt", 64, 128), OP.min)
-        tt(A("mt", 192, 224), A("mt", 128, 160), A("mt", 160, 192), OP.min)
-        tt(A("mt", 0, 32), A("mt", 192, 224), A("cd", 256, 288), OP.min)
-        ts(A("ql", 0, 32), A("mt", 0, 32), -1.0, OP.add)
+            mm(A("ps0", 0, 32), I16, A("prod", 32 * o, 32 * o + 32), False, o == 8)
+        ts(A("ql", 0, 32), A("ps0", 0, 32), -256.0, OP.add)
         cp(IX("swin", 0, 9 * ST, "ql", 0, 32), A("zb", 0, K))
         land = "land%d" % rnd
         send(lambda r: A("swin", r * ST, r * ST + 32), A(land, rank * 32, rank * 32 + 32), "ka%d" % rnd, "ks%d" % rnd, [A("fwin", 0, 9 * ST)] if rnd == 0 else [])
         cp(A(land, rank * 32, rank * 32 + 32), A("swin", rank * ST, rank * ST + 32))
-        cp(A("lrep", 0, K), A("ps6", 0, K))
         if rnd == 0:
             ms(A("cwin", 0, K), 0.0)
             for o in range(8):
@@ -444,109 +470,90 @@ def build(core, T, topo):
         land = A(ld, 0, 256)
         nel = A("nel", 0, 256)
         arrive("ka%d" % rnd, [A(ld, 32 * r, 32 * r + 32) for r in range(8) if r != rank])
-        for x in range(16):
-            mm(A("ps0", 0, 16), sel("w2", x), A(ld, x, 256, 16), x == 0, x == 15)
-        mm(A("ps1", 0, 256), c["obw2"], land, True, True)
-        ts(A("nel" if rnd == 0 else "inv", 0, 256), land, 0.0, OP.is_lt)
-        cp(A("hli", 0, 16), A("ps0", 0, 16))
-        ts(A("pli", 0, 16), A("hli", 0, 16), 32767, OP.bitwise_and, 4, OP.arith_shift_right)
+        if rnd == 0:
+            mm(A("ps2", 0, 256), c["obw2"], land, True, True)
+        tolist(A("ps1", 0, 16), "w2", ld, 0, 256, True, True)
         if rnd == 1:
-            cp(A("plu", 0, 16), A("pli", 0, 16))
+            mm(A("ps2", 0, 256), c["obw2"], land, True, True)
+        act(A("nel" if rnd == 0 else "inv", 0, 256), land, AF.Relu, scale=-1.0)
+        cp(A("hli", 0, 16), A("ps1", 0, 16))
+        if rnd == 1:
+            ts(A("pl2", 0, 16), A("hli", 0, 16), 32767, OP.bitwise_and, 4, OP.arith_shift_right)
+            cp(A("plu", 0, 16), A("pl2", 0, 16))
             tt(A("ne", 0, 256), IX("store", 0, TS + 256, "plu", 0, 16), land, OP.not_equal)
-            mm(A("ps2", 0, 256), c["obm"], A("inv", 0, 256), True, False)
-            mm(A("ps2", 0, 256), OB, A("ne", 0, 256), False, True)
-            ts(nel, A("ps2", 0, 256), 0.5, OP.is_lt)
-        cp(A("hri", 0, 256), A("ps1", 0, 256))
+            tolist(A("ps6", 0, 16), "one", "ne", 0, 256, True, True)
+            mm(A("ps5", 0, 256), c["obm"], A("inv", 0, 256), True, False)
+            mm(A("ps5", 0, 256), OB, A("ne", 0, 256), False, True)
+            act(nel, A("ps5", 0, 256), AF.Relu, bias=1.0, scale=-1.0)
+        ts(A("pli", 0, 16), A("hli", 0, 16), 2 ** 21 + 32767, OP.bitwise_and, 4, OP.arith_shift_right)
+        cp(A("hri", 0, 256), A("ps2", 0, 256))
         ts(A("hri", 0, 256), A("hri", 0, 256), 32767, OP.bitwise_and, 4, OP.arith_shift_right)
         cp(A("prh", 0, 256), A("hri", 0, 256))
-        mm(A("ps5", 0, 256), c["ob4"], nel, True, False)
+        mm(A("ps3", 0, 256), c["ob4"], nel, True, False)
         if rnd == 0:
-            ts(A("sx", 0, 16), A("hli", 0, 16), 0.0, OP.is_lt, -8192.0, OP.mult)
-            tt(A("pm", 0, 16), A("sx", 0, 16), A("pli", 0, 16), OP.add)
+            cp(A("pm", 0, 16), A("pli", 0, 16))
         else:
-            for x in range(16):
-                mm(A("ps4", 0, 16), sel("n512", x), A("nel", x, 256, 16), x == 0, x == 15)
-            tt(A("pm", 0, 16), A("ps4", 0, 16), A("pli", 0, 16), OP.add)
-        tt(A("dg", 0, 256), IX("pm", 0, 16, "qd", 0, 16), A("prh", 0, 256), OP.is_equal)
-        mm(A("ps5", 0, 256), c["obp"], A("dg", 0, 256), False, False)
-        for a in range(15):
-            m = 256 * a - 8 * a * (a - 1)
-            n = 240 - 16 * a
-            ts(A("mb", m, m + n), A("prh", 16 * a + 16, 256), A("pm", a, a + 1), OP.is_equal)
-            mm(A("ps5", 16 * a + 16, 256), c["ob4"], A("mb", m, m + n), False, a == 14)
-        tt(A("nw", 0, 256), A("ps5", 0, 256), A("ck", 1536, 1792), OP.is_lt)
+            ts(A("sn", 0, 16), A("ps6", 0, 16), 0.0, OP.is_equal, 4096.0, OP.mult)
+            tt(A("pm", 0, 16), A("sn", 0, 16), A("pli", 0, 16), OP.add)
+        m = 0
+        for a in range(16):
+            n = 256 - 16 * a
+            ts(A("mb", m, m + n), A("prh", 16 * a, 256), A("pm", a, a + 1), OP.is_equal)
+            mm(A("ps3", 16 * a, 16 * a + 16), c["obp"], A("mb", m, m + 16), False, a == 15)
+            if a < 15:
+                mm(A("ps3", 16 * a + 16, 256), c["ob4"], A("mb", m + 16, m + n), False, False)
+            m += n
+        tt(A("nw", 0, 256), A("ps3", 0, 256), THR, OP.is_lt)
         send(lambda r: A("nw", r * 32, r * 32 + 32), A("fwin", rank * ST, rank * ST + 32), "fa%d" % rnd, "fs%d" % rnd)
         cp(A("fwin", rank * ST, rank * ST + 32), A("nw", rank * 32, rank * 32 + 32))
         arrive("fa%d" % rnd, [A("fwin", ST * r, ST * r + 32) for r in range(8) if r != rank])
 
     def store(rnd):
-        for x in range(16):
-            mm(A("ps5", 0, 16), sel("six", x), A("nw", x, 256, 16), x == 0, x == 15)
-        tt(A("sx", 0, 16), A("pli", 0, 16), A("ck", 1296, 1312), OP.subtract)
-        tt(A("sy", 0, 16), A("ps5", 0, 16), A("sx", 0, 16), OP.mult)
-        tt(A("sz", 0, 16), A("sy", 0, 16), A("ck", 1296, 1312), OP.add)
+        tolist(A("ps7", 0, 16), "six", "nw", 0, 256, True, True)
+        tt(A("sx", 0, 16), A("pli", 0, 16), QC, OP.subtract)
+        tt(A("sy", 0, 16), A("ps7", 0, 16), A("sx", 0, 16), OP.mult)
+        tt(A("sz", 0, 16), A("sy", 0, 16), QC, OP.add)
         cp(A("su", 0, 16), A("sz", 0, 16))
         cp(IX("store", 0, TS + 256, "su", 0, 16), A("land%d" % rnd, 0, 256))
         if rnd == 1:
             dma("y", "yt", A("store", 0, TS), "w0", 4.1)
 
     def nextfront(rnd):
-        cum = A("ncu", 520, 1032)
         hold = A("hold", 0, F)
-        tt(A("ncu", 8, 520), IX("fwin", 0, 9 * ST, "ql", 0, 32), A("lrep", 0, K), OP.mult)
-        scan(A("ncu", 520, 1033), A("ncu", 7, 520), A("cj", 224, 737), 0.0, OP.add, OP.min)
-        for x in range(16):
-            mm(A("ps0", 0, 64), sel("six", x), A("ncu", 8 + x, 1032, 16), x == 0, x == 15)
-        ts(A("ex", 0, K), A("ncu", 521, 1033), 224.0, OP.is_gt, 8448.0, OP.mult)
-        mm(A("ps3", 0, K), c["ob16"], A("ex", 0, K), False, True)
-        ts(A("unf", 0, F), A("ck", 512, 736), A("ncu", 1032, 1033), OP.is_ge, 8448.0, OP.mult)
-        ts(A("ea", 0, 32), A("ps0", 0, 32), 0.0, OP.is_equal)
-        ts(A("s2", 0, 32), A("ps0", 32, 64), 224.0, OP.is_gt)
-        tt(A("eb", 0, 32), A("ea", 0, 32), A("ck", 1264, 1296), OP.mult)
-        tt(A("s3", 0, 32), A("s2", 0, 32), A("ck", 1232, 1264), OP.mult)
-        tt(A("st", 0, 32), A("eb", 0, 32), A("s3", 0, 32), OP.max)
-        tt(A("s5", 0, 32), A("ps0", 32, 64), A("st", 0, 32), OP.max)
-        cp(A("ofu", 0, 32), A("s5", 0, 32))
-        tt(A("d0", 0, K), A("ps3", 0, K), cum, OP.subtract)
-        cp(IX("pwin", 0, 1536, "ofu", 0, 32), A("d0", 0, K))
-        scan(hold, A("pwin", 0, F), A("unf", 0, F), 0.0, OP.max, OP.max)
-        tt(A("tauh", 0, F), hold, A("ck", 960, 1184), OP.add)
-        for x in range(16):
-            mm(A("ps2", 0, 14), A("ch", 16 - x, 144 - x), A("tauh", x, F, 16), x == 0, x == 15)
-        tt(A("taui", 0, F), hold, A("ck", 736, 960), OP.add)
-        ts(A("taui", 0, F), A("taui", 0, F), 8207, OP.bitwise_and)
-        ts(A("oh2", 0, F), A("taui", 0, F), PI, OP.is_equal)
-        ts(A("tj", 0, 14), A("ps2", 0, 14), 1.0 / 256, OP.mult, 128.0 - 15.0 / 32, OP.add)
-        ts(A("tju", 0, 14), A("tj", 0, 14), 223.0, OP.min)
-        tt(A("suv", 0, F), IX("uf", 0, F, "tju", 0, 14), A("oh2", 0, F), OP.mult)
-        tt(A("suv", F, 2 * F), IX("vf", 0, F, "tju", 0, 14), A("oh2", 0, F), OP.mult)
-        ts(A("fa", 0, F), A("pwin", 0, F), 0.0, OP.is_gt)
-        ts(A("fb", 0, F), hold, 8192.0, OP.is_ge)
+        starts = A("pwin", 0, 2 * F, 2)
+        mm(A("ps0", 0, 33), I32, NC, True, False)
+        tt(A("xl", 0, KS), IX("fwin", 0, 9 * ST + 16, "ql", 0, 33), A("lrep", 0, KS), OP.mult)
+        scan(A("cum", 1, KS + 1), A("xl", 0, KS), CAPH, 0.0, OP.add, OP.min)
+        tolist(A("ps0", 0, 33), "n256", "xl", 0, KS, False, True)
+        tolist(A("ps1", 0, 33), "h8", "cum", 0, KS, True, False)
+        act(A("yb", 0, 33), A("ps0", 0, 33), AF.Relu)
+        mm(A("ps1", 0, 33), I32, A("yb", 0, 33), False, True)
+        ts(A("ex", 0, KS), A("cum", 1, KS + 1), float(F), OP.is_gt, 4096.0, OP.mult)
+        cp(A("ofu", 0, 33), A("ps1", 0, 33))
+        tt(IX("pwin", 0, 2624, "ofu", 0, 33), A("t0c", 0, KS), A("ex", 0, KS), OP.add)
+        scan(hold, A("xf", 0, F), starts, -4096.0, OP.add, OP.max)
+        tolist(A("ps2", 0, 14), "h16", "hold", 0, F, True, True)
+        ts(A("tju", 0, 14), A("ps2", 0, 14), P / 2.0, OP.add, float(P), OP.min)
+        iu, iv = IX("tuv", 0, TW, "tju", 0, 14), IX("tuv", TW, 2 * TW, "tju", 0, 14)
+        ts(A("drp", 0, F), hold, -1.0, OP.mult, -2000.0, OP.min)
         if rnd == 0:
-            for x in range(16):
-                mm(A("ps4", 0, 28), A("ch", 16 - x, 144 - x), A("suv", x, 2 * F, 16), x == 0, x == 15)
-            for x in (0, 14):
-                ts(A("adl", x, x + 14), A("tj", 0, 14), 375.0, OP.is_lt, 1536.0, OP.mult)
-            tt(A("flg", 0, F), A("fa", 0, F), A("fb", 0, F), OP.max)
-            tt(A("uvs", 0, 28), A("ps4", 0, 28), A("adl", 0, 28), OP.add)
-            cp(A("uv", 0, 28), A("uvs", 0, 28))
-            expand()
-            ms(A("pwin", 0, F), 0.0)
+            cp(A("kk", 0, F), iu)
+            cp(A("kk", F, 2 * F), iv)
+            tt(A("nf", 0, F), starts, A("drp", 0, F), OP.is_le)
+            ms(A("pwin", 0, 2 * F), -2048.0)
         else:
             row = (0, 128, 16)
-            mm(A("ps4", 0, F), A("ch", 144, 272), A("suv", 0, F), True, True)
-            mm(A("ps1", 0, F), A("ch", 144, 272), A("suv", F, 2 * F), True, True)
-            ts(A("adr", 0, F), hold, 8000.0, OP.is_lt, 1536.0, OP.mult)
-            tt(A("fin", 2 * F, 3 * F), A("fa", 0, F), A("fb", 0, F), OP.max)
+            tt(A("fin", 2 * F, 3 * F), starts, A("drp", 0, F), OP.is_gt)
             dma("y", "ys", A("fin", 2 * F, 3 * F, 1, row), "w3", 2.0)
-            tt(A("fin", 0, F), A("ps4", 0, F), A("adr", 0, F), OP.add)
-            dma("y", "yu", A("fin", 0, F, 1, row), "w1", 2.0)
-            tt(A("fin", F, 2 * F), A("ps1", 0, F), A("adr", 0, F), OP.add)
+            act(A("fin", F, 2 * F), iv, AF.Copy)
             dma("s", "yv", A("fin", F, 2 * F, 1, row), "w2", 2.0)
+            cp(A("fin", 0, F), iu)
+            dma("y", "yu", A("fin", 0, F, 1, row), "w1", 2.0)
 
     for rnd in range(2):
         side()
         big(rnd)
+        tables(rnd)
         control(rnd)
         owner(rnd)
         store(rnd)
@@ -554,7 +561,7 @@ def build(core, T, topo):
     return ops
 
 
-def schedule(ops, hop=0.03):
+def schedule(ops, hop=0.045):
     n = len(ops)
     ent = {}
     succ = [[] for _ in ops]
@@ -583,7 +590,7 @@ def schedule(ops, hop=0.03):
             succ[j].append(i)
     tail = [0.0] * n
     for i in range(n - 1, -1, -1):
-        tail[i] = ops[i]["est"] + max([tail[k] for k in succ[i]], default=0.0)
+        tail[i] = ops[i]["est"] + max([tail[k] + (0.0 if ops[i]["q"] == "t" and ops[k]["q"] == "t" else hop) for k in succ[i]], default=0.0)
     can = [0.0] * n
     free = {}
     ready = {}
@@ -603,6 +610,9 @@ def schedule(ops, hop=0.03):
             f = free.get(q, 0.0)
             m = min(max(f, can[i]) for i in lst)
             i = max((i for i in lst if max(f, can[i]) <= m), key=lambda i: tail[i])
+            for j in lst:
+                if m < can[j] < m + ops[i]["est"] and max(can[j] + tail[j], can[j] + ops[j]["est"] + tail[i]) < max(m + tail[i], m + ops[i]["est"] + tail[j]):
+                    i, m = j, can[j]
             k = (max(f, can[i]), -tail[i], i)
             if best is None or k < best:
                 best = k
@@ -621,6 +631,7 @@ def schedule(ops, hop=0.03):
         elif o["sem"] and q == "g":
             free[q] = t + 1.0
         order.append(o)
+        o["t0"], o["t1"] = t, end
         for k in succ[i]:
             can[k] = max(can[k], end + (0.0 if q == "t" and ops[k]["q"] == "t" else hop))
             left[k] -= 1

@@ -6,25 +6,26 @@ W, F, P, K, TS = 3072, 224, 3584, 512, 2048
 CW, NCH, LC = 448, 8, 28
 ST = 512
 TW = P + 16
-KS = K + 16
+KS = 256 + 16
+SA = 11
 CLAMP = 6912.0
 LN4, LN2 = math.log(4.0), math.log(2.0)
 CFG = {
-    "vs": ["vvvvvvss", "vvvvvvss"],
-    "qs": ["vsssssss", "vsssssss"],
-    "gr": [[[0], [1], [2, 3], [4, 5], [6, 7]], [[0], [1], [2, 3], [4, 5], [6, 7]]],
+    "vs": ["vvvvvvsv", "vvvvvvsv"],
+    "qs": ["ssssszzz", "ssssszzz"],
+    "gr": [[[0, 1], [2, 3], [4, 5], [6], [7]], [[0, 1], [2, 3], [4, 5], [6], [7]]],
 }
 
 SCRATCH = {}
 for _d, _l in (
-    ("int32", "kidb:3072 fuv:28 fsb:224 rmi:2 zi:512 hi:32 ow:32 hri:256 hli:16 pli:16 pl2:16 cint:160 cpi:160"),
-    ("uint16", "uv:28 kk:448 cof:16 jl:32 t1u:32 t0u:32 ql:34 plu:16 su:16 ofu:34 tju:16 cu:24"),
-    ("float16", "prh:256 uvh:448 cs:288 prod:288 owf:32 cum:536 hold:224 ch:1200"),
+    ("int32", "kidb:3072 fuv:28 fsb:224 rmi:2 zi:512 hi:32 ow:32 hli:16 pli:16 pl2:16 cint:160 cpi:160"),
+    ("uint16", "uv:28 kk:448 cof:32 jl:32 t1u:32 t0u:32 ql:32 qc:18 plu:16 su:16 ofu:18 tju:16 cu:24"),
+    ("float16", "prh:256 uvh:448 cs:288 prod:288 owf:32 cum:280 hold:224 ch:1000"),
     ("bfloat16", "vecb:3072 markb:3072 va:1792 vb:1792 nz:1792 qa:3584 mq:3584 nf:232 fsf:224 adv:224 lbn:224 z0:232 drp:224 cand:224 lb:224 "
-     "nls:16 cwin:3808 jk:512 oh:512 lh:512 lrep:528 zb:512 ind:288 swin:4608 fwin:4624 land0:256 land1:256 store:2304 inv:256 ne:256 "
-     "nel:256 mb:2176 nw:256 xl:528 xf:224 cb:4600 cj:1400"),
-    ("float32", "dd:3584 run:3592 tuv:7200 eb:232 bc:224 rmf:2 yl:224 cinc:224 rf:224 ci:16 o1:16 o2:16 r1:512 pm:16 sn:16 sx:16 sy:16 sz:16 "
-     "yb:34 t0c:528 ex:528 pwin:2624 fin:672 cf:720 ck:2600"),
+     "nls:16 cwin:3808 jk:512 oh:512 lh:512 lrep:272 zb:512 ind:288 swin:4608 fwin:272 land0:256 land1:256 store:2304 inv:256 ne:256 "
+     "nel:256 mb:2176 nw:256 xl:272 xf:224 sid:32 snt:32 vl:32 jb:32 qb:256 rb:272 cb:6640 cj:1400"),
+    ("float32", "dd:3584 run:3592 tuv:7200 eb:232 bc:224 rmf:2 yl:224 cinc:224 rf:224 ci:32 o1:32 o2:32 r1:512 pm:32 sn:16 sx:16 sy:16 sz:16 "
+     "yb:18 t0c:272 ex:272 pwin:1600 fin:672 rec:512 rwin:784 cf:720 ck:3000"),
 ):
     for _x in _l.split():
         SCRATCH[_x.split(":")[0]] = ("sbuf", [128, int(_x.split(":")[1])], _d)
@@ -118,11 +119,17 @@ def build(core, T, topo):
         add("v", lambda g: g.vector.tensor_tensor_scan(X(out), X(a), X(b), X(init) if isap(init) else init, op0, op1), rd, [out])
 
     def act(out, a, func, bias=0.0, scale=1.0):
-        rd = [a] + ([scale] if isap(scale) else [])
-        add("s", lambda g: g.scalar.activation(X(out), X(a), func, bias=bias, scale=X(scale) if isap(scale) else scale), rd, [out])
+        rd = [a] + [s for s in (scale, bias) if isap(s)]
+        x = lambda s: X(s) if isap(s) else s
+        add("s", lambda g: g.scalar.activation(X(out), X(a), func, bias=x(bias), scale=x(scale)), rd, [out])
+
+    def mms(lst):
+        def fn(g):
+            return [g.tensor.matmul(X(o), X(l), X(r), s0, s1) for o, l, r, s0, s1 in lst][-1]
+        add("t", fn, list(dict.fromkeys([x[1] for x in lst] + [x[2] for x in lst])), [lst[0][0]], est=sum(estimate("t", x[0], [x[1]], False) for x in lst))
 
     def mm(out, l, r, start, stop):
-        add("t", lambda g: g.tensor.matmul(X(out), X(l), X(r), start, stop), [l, r], [out])
+        mms([(out, l, r, start, stop)])
 
     def iota(out, pat, base, cm, f):
         if f:
@@ -171,24 +178,26 @@ def build(core, T, topo):
     S16 = A("ck", 512, 545)
     QM = A("ck", 560, 816)
     THR = A("ck", 816, 1072)
-    CAP = A("ck", 1072, 1600)
+    CAP = A("ck", 1072, 1072 + KS)
+    K2 = A("ck", 1344, 1376)
+    EI = 1376
+    R2 = A("ck", 1400, 1528)
     ZERO = A("ck", 1600, 1824)
     JC = A("ck", 1824, 1838)
     QC = A("ck", 1840, 1856)
-    NC = A("ck", 1856, 1889)
-    R32 = A("ck", 1896, 1914)
+    NC = A("ck", 1856, 1873)
     I32 = A("ck", 1920, 2048)
     D, DLO, DHI = A("ck", 2048, 2176), A("ck", 2176, 2304), A("ck", 2304, 2432)
+    MH, U = A("ck", 2432, 2560), A("ck", 2560, 2688)
+    RD = A("ck", 2688, 2688 + KS)
     JV = A("cj", 0, F)
     M16 = A("cj", 224, 672)
-    M32 = A("cj", 672, 960)
-    OWN = A("cj", 960, 1248)
+    OWN = A("cj", 960, 1104)
     ONE = A("cj", 225, 226)
     iota(A("cint", 0, 1), [[0, 1]], 0, 1, False)
     iota(A("cint", 8, 152), [[1, 144]], 0, 0, False)
     iota(S16, [[16, 33]], 0, 0, True)
-    iota(R32, [[0, 9], [16, 2]], 0, 0, True)
-    fill(A("cj", 224, 960), 1)
+    fill(A("cj", 224, 672), 1)
     for a, v in ((A("nf", F, F + 8), 0), (A("eb", 0, 8), 0), (A("z0", 0, 8), 1), (A("run", 0, 8), 0), (ZERO, 0)):
         fill(a, v)
     iota(QM, [[0, 16], [1, 16]], 0, 0, True)
@@ -196,12 +205,11 @@ def build(core, T, topo):
     fill(A("cwin", 0, K), 0)
     iota(KC, [[1, K]], -8192, 0, True)
     iota(CAP, [[1, KS]], 256, 0, True)
-    iota(A("cj", 960, 1216), [[2, 8], [0, 32]], 1, 0, True)
-    fill(A("cj", 1216, 1248), 0)
+    iota(A("cj", 960, 1088), [[2, 8], [0, 16]], 1, 0, True)
+    fill(A("cj", 1088, 1104), 0)
     for o in range(8):
         fill(A("swin", o * ST, o * ST + 32), -1)
-    for a, v in ((A("fwin", 0, 9 * ST + 16), 0), (A("fwin", 9 * ST, 9 * ST + 1), 1), (A("store", 0, TS + 256), -1), (A("pwin", 0, 2 * F), -2048),
-                 (A("lrep", K, KS), F + 1), (A("t0c", K, KS), 0), (A("xf", 0, F), 1)):
+    for a, v in ((A("fwin", 256, KS), 0), (A("fwin", 256, 257), 1), (A("store", 0, TS + 256), -1), (A("pwin", 0, 2 * F), -2048), (A("xf", 0, F), 1)):
         fill(a, v)
     P0 = A("cf", 0, 1)
     PI = A("cf", 1, 2)
@@ -213,6 +221,7 @@ def build(core, T, topo):
     PW = A("cf", 7, 8)
     P128 = A("cf", 8, 9)
     P129 = A("cf", 9, 10)
+    RB = A("cf", 10, 11)
     NL4 = A("cf", 12, 13)
     cp(P0, A("cint", 0, 1))
     ts(A("cpi", 0, 1), A("cint", 0, 1), 15, OP.bitwise_and)
@@ -222,8 +231,8 @@ def build(core, T, topo):
     ts(W2, PI, -28.0, OP.mult, 510.0, OP.add)
     ts(MB, PI, 15.0, OP.is_equal, 2.0 ** 19, OP.mult)
     ts(MBN, MB, -1.0, OP.mult, -0.5, OP.add)
-    ts(P128, PI, 128.0, OP.add)
-    ts(P129, PI, 129.0, OP.add)
+    ts(P128, PI, -1.0, OP.mult, 143.1, OP.add)
+    ts(P129, PI, -143.0, OP.add)
     YC = A("cf", 16, 160)
     Y128 = A("cf", 16, 144)
     MI = A("cf", 160, 288)
@@ -260,12 +269,11 @@ def build(core, T, topo):
         return A("cb", b, b + 128)
 
     def tolist(out, name, b, c0, c1, start, stop):
-        for x in range(16):
-            mm(out, sel(name, x), A(b, c0 + x, c1, 16), start and x == 0, stop and x == 15)
+        mms([(out, sel(name, x), A(b, c0 + x, c1, 16), start and x == 0, stop and x == 15) for x in range(16)])
 
     mksel("one", None)
     IDN, IDM, OB, REP = cbuf(128), cbuf(128), cbuf(128), cbuf(128)
-    I16, IM16, CAPH = A("ch", 288, 416), A("ch", 416, 544), A("ch", 544, 544 + KS)
+    I16, IM16, CAPH, IS16 = A("ch", 288, 416), A("ch", 416, 544), A("ch", 544, 544 + KS), A("ch", 816, 944)
     ts(IDN, Y128, P0, OP.is_equal)
     act(IDM, IDN, AF.Copy, scale=-1.0)
     act(I32, IDN, AF.Copy)
@@ -282,7 +290,7 @@ def build(core, T, topo):
     mksel("neg", -1.0)
     cp(A("kk", 0, F), IX("kidb", 0, W, "uv", 0, 14))
     cp(A("kk", F, 2 * F), IX("kidb", 0, W, "uv", 14, 28))
-    for name, wt in (("six", 1.0 / 16), ("pi", PI), ("p128", P128), ("w2", W2), ("n256", -256.0)):
+    for name, wt in (("six", 1.0 / 16), ("pi", PI), ("w2", W2), ("n256", -256.0)):
         mksel(name, wt)
     act(PW, PI, AF.Exp, scale=-LN2)
     act(THR, QM, AF.Exp, bias=math.log(2.5), scale=-LN2)
@@ -297,22 +305,45 @@ def build(core, T, topo):
         tt(c["b%d" % k], c["b%d" % k], c["wc%d" % k], OP.mult)
     c["nui"] = cbuf(128)
     ts(c["nui"], DHI, 0.0, OP.is_le, -1.0, OP.mult)
-    for name, wt in (("p64", 64.0), ("n8k", -8192.0), ("i4352", 4352.0)):
+    for name, wt in (("p64", 64.0), ("n8k", -8192.0), ("i4352", 4352.0), ("i16", 16.0), ("i143", 143.0), ("n2k", -2048.0)):
         c[name] = cbuf(128)
         act(c[name], IDN, AF.Copy, scale=wt)
-    for name, wt in (("obw2", W2), ("obp", PW), ("obpi", P129), ("ob4", 4.0), ("obm", -1.0), ("obn", -128.0)):
+    ei = lambda x: A("ck", EI + x, EI + x + 1)
+    ts(A("ck", EI, EI + 16), A("cf", 16, 32), PI, OP.is_equal)
+    for name, wt in (("obw2", W2), ("obp", PW), ("ob4", 4.0), ("obm", -1.0), ("r1", ei(1))):
         c[name] = cbuf(128)
         act(c[name], BLK, AF.Copy, scale=wt)
+    c["obw8"] = cbuf(128)
+    act(c["obw8"], c["obw2"], AF.Copy, scale=1.0 / 16)
+    act(R2, BLK, AF.Copy, scale=ei(2))
+    mksel("r0", ei(0))
+    tt(MH, MI, T1, OP.subtract)
+    for name in ("to0", "to1", "ljk", "llh", "loh"):
+        c[name] = cbuf(128)
+    for name, v in (("to0", 0.0), ("to1", 1.0), ("ljk", 2.0)):
+        ts(c[name], MH, v, OP.is_equal)
+    tt(c["llh"], c["to1"], c["ljk"], OP.subtract)
+    act(U, c["ljk"], AF.Copy, scale=144.0)
+    act(c["loh"], c["to1"], AF.Copy, scale=P129)
+    tt(c["loh"], c["loh"], U, OP.add)
+    for x in range(16):
+        c[x] = cbuf(128)
+        act(c[x], c["to0"], AF.Copy, scale=ei(x))
+    ts(RB, ei(2), -P / 2.0, OP.mult)
+    ts(A("cf", 13, 14), ei(0), 258.0, OP.mult)
+    ts(A("cf", 14, 15), ei(1), F + 1.0, OP.mult)
+    ts(RD, CAP, 0.0, OP.mult, A("cf", 13, 14), OP.add)
+    ts(A("ck", RD[1] + 256, RD[1] + 257), ei(0), 256.0, OP.mult, A("cf", 14, 15), OP.add)
+    ts(IS16, Y128, P0, OP.is_equal, 1.0 / 16, OP.mult)
     ts(A("ch", 0, 144), YC, PB, OP.is_equal, 1.0 / 16, OP.mult)
     ts(A("ch", 144, 288), YC, PB, OP.is_equal, 1.0 / 8, OP.mult)
     ts(JC, A("ck", 512, 526), PI, OP.add, float(P), OP.add)
     ts(QC, A("ck", 512, 528), PI, OP.add, float(TS), OP.add)
-    ts(NC, S16, PI, OP.add, 0.5, OP.add)
+    ts(K2, A("ck", 512, 544), PI, OP.add, float(KS), OP.add)
+    ts(NC, A("ck", 512, 529), PI, OP.add, 0.5, OP.add)
     ts(NC, NC, 2.0, OP.mult)
-    ts(A("cu", 2, 20), R32, PI, OP.add)
-    ts(A("ql", 32, 33), PI, 0.0, OP.is_gt, 9.0 * ST, OP.add)
+    ts(A("cu", 2, 12), A("ck", 1600, 1610), PI, OP.add)
     cp(CAPH, CAP)
-    ms(A("cj", 672, 960, 32), 0.0)
     ts(A("cum", 0, 8), A("ck", 1600, 1608), 0.0, OP.add)
     add("s", lambda g: g.scalar.activation(X(A("cf", 11, 12)), X(ONE), AF.Ln, scale=0.25), [ONE, PW, THR, c["b0"], c["b1"], c["b2"]], [A("cf", 11, 12)], est=1.6)
     add("v", lambda g: g.vector.reciprocal(T.cf[:, 12:13], T.cf[:, 11:12]), [A("cf", 11, 12)], [NL4])
@@ -338,14 +369,16 @@ def build(core, T, topo):
                     tt(vb, iv, va, OP.subtract)
             j0, j1 = grp[0] * LC, (grp[-1] + 1) * LC
             vl, vh = (grp[0] % 4) * CW, (grp[-1] % 4 + 1) * CW
-            two = vs[grp[0]] == "s"
+            raw = [i for i in grp if vs[i] == "s"]
             sb = A("ps%d" % (4 + n % 2), 0, j1 - j0)
-            for x in range(16):
-                if two:
-                    mm(sb, IDN, A("va", vl + x, vh, 16), x == 0, False)
-                mm(sb, IDM, A("vb", vl + x, vh, 16), x == 0 and not two, x == 15)
+            if len(raw) == len(grp):
+                mms([(sb, IDN, A("va", vl + x, vh, 16), x == 0, False) for x in range(16)])
+            mms([(sb, IDM, A("vb", vl + x, vh, 16), x == 0 and len(raw) < len(grp), x == 15 and len(raw) in (0, len(grp))) for x in range(16)])
+            if 0 < len(raw) < len(grp):
+                mms([(A(sb[0], raw[0] * LC - j0, (raw[-1] + 1) * LC - j0), IDN, A("va", (raw[0] % 4) * CW + x, (raw[-1] % 4 + 1) * CW, 16), False, x == 15) for x in range(16)])
             for i in grp:
                 vl = (i % 4) * CW
+                two = vs[i] == "s"
                 if two:
                     mm(A("ps%d" % (i % 4), 0, CW), IDN, A("va", vl, vl + CW), True, False)
                 mm(A("ps%d" % (i % 4), 0, CW), IDM, A("vb", vl, vl + CW), not two, False)
@@ -358,15 +391,27 @@ def build(core, T, topo):
                 act(A("nz", vl, vl + CW), A("dd", lo, lo + CW), AF.Abs)
                 if i % 2 == 1:
                     tolist(A("ps6", (i - 1) * LC, (i + 1) * LC), "neg", "nz", vl - CW, vl + CW, True, True)
-        for i in range(NCH):
+        marks(rnd, [i for i in range(NCH) if i < (qs + "z").index("z")])
+
+    def marks(rnd, chunks):
+        qs = CFG["qs"][rnd]
+        for i in chunks:
             lo = i * CW
             d, m, qa = [A(b, lo, lo + CW) for b in ("dd", "mq", "qa")]
-            iu = IX("markb", 0, W, "kk", i * LC, i * LC + LC)
+            iu, iv = IX("markb", 0, W, "kk", i * LC, i * LC + LC), IX("markb", 0, W, "kk", F + i * LC, F + i * LC + LC)
             if qs[i] == "v":
                 cp(qa, iu)
             else:
                 act(qa, iu, AF.Copy)
-            tt(m, IX("markb", 0, W, "kk", F + i * LC, F + i * LC + LC), qa, OP.max)
+            if qs[i] != "z":
+                tt(m, iv, qa, OP.max)
+            else:
+                act(m, iv, AF.Copy)
+                ps, more = A("ps%d" % (5 if i % 2 else 1), 0, CW), A("va", (i % 4) * CW, (i % 4 + 1) * CW)
+                mms([(ps, IDN, m, True, False), (ps, IDM, qa, False, True)])
+                act(more, ps, AF.Relu)
+                mms([(ps, IDN, qa, True, False), (ps, IDN, more, False, True)])
+                m = ps
             init = 0.0 if i == 0 else A("run", lo + 7, lo + 8)
             if i == NCH // 2:
                 cp(A("rmi", 0, 1), A("run", lo + 7, lo + 8))
@@ -376,8 +421,6 @@ def build(core, T, topo):
             scan(A("run", lo + 8, lo + 8 + CW), d, m, init, OP.add, OP.add)
 
     def tables(rnd):
-        if rnd == 1:
-            iota(A("kidb", 0, W), [[1, W]], 0, 0, False)
         for h in range(2):
             act(A("tuv", h * TW + P, h * TW + TW), IX("kidb", 0, W, "cu", 0, 1), AF.Copy)
             for i in range(NCH):
@@ -396,19 +439,19 @@ def build(core, T, topo):
             mm(A("ps0", 0, F), c["b%d" % k], A("z0", 2 - k, 2 - k + F), k == 0, k == 2)
         ts(cand, A("ps1", 0, F), 64.0, OP.is_gt)
         act(A("yl", 0, F), A("ps0", 0, F), AF.Ln, bias=2.0 ** -60)
-        act(A("lb", 0, F), A("yl", 0, F), AF.Identity, bias=128.1, scale=NL4)
-        mm(A("ps5", 0, 14), I32, JC, True, False)
+        act(A("lb", 0, F), A("yl", 0, F), AF.Identity, bias=P128, scale=NL4)
+        marks(rnd, [i for i in range(NCH) if i >= (CFG["qs"][rnd] + "z").index("z")])
+        mm(A("ps7", 32, 46), I32, JC, True, False)
         tolist(A("ps2", 0, 14), "one", "cand", 0, F, True, True)
         mm(A("ps3", 0, F), OB, cand, True, True)
         mm(A("ps4", 0, F), c["nui"], cand, True, False)
         mm(A("ps4", 0, F), c["n8k"], cand, False, False)
         cp(A("nls", 0, 14), A("ps2", 0, 14))
-        mm(A("ps7", 0, 14), OB, A("nls", 0, 14), True, True)
-        mm(A("ps6", 0, 14), c["nui"], A("nls", 0, 14), True, True)
-        mm(A("ps5", 0, 14), c["n8k"], A("nls", 0, 14), False, True)
+        nls = A("nls", 0, 14)
+        mms([(A("ps7", 32, 46), c["n8k"], nls, False, True), (A("ps7", 0, 14), OB, nls, True, True), (A("ps7", 16, 30), c["nui"], nls, True, True)])
         scan(A("ci", 0, 14), A("ps7", 0, 14), A("ck", 1600, 1614), 0.0, OP.add, OP.add)
-        tt(A("o1", 0, 14), A("ps6", 0, 14), A("ci", 0, 14), OP.add)
-        tt(A("o2", 0, 14), A("ps5", 0, 14), A("o1", 0, 14), OP.max)
+        tt(A("o1", 0, 14), A("ps7", 16, 30), A("ci", 0, 14), OP.add)
+        tt(A("o2", 0, 14), A("ps7", 32, 46), A("o1", 0, 14), OP.max)
         cp(A("cof", 0, 14), A("o2", 0, 14))
         cp(IX("cwin", 0, P + F, "cof", 0, 14), JV)
         scan(A("jk", 0, K), A("cwin", 0, K), A("cwin", 0, K), 0.0, OP.max, OP.max)
@@ -416,102 +459,136 @@ def build(core, T, topo):
         mm(A("ps4", 0, F), I32, A("cinc", 0, F), False, True)
         act(A("rf", 0, F), A("ps4", 0, F), AF.Copy)
         tolist(A("ps0", 0, 32), "six", "jk", 0, K, True, True)
-        tolist(A("ps1", 0, 32), "one", "jk", 0, K, True, False)
-        tolist(A("ps2", 0, 32), "one", "jk", 0, K, True, False)
-        mm(A("ps6", 0, K), OB, A("jk", 0, K), True, False)
+        ts(A("vl", 0, 32), K2, -float(KS), OP.add, A("cinc", F - 1, F), OP.is_lt)
+        mm(A("ps6", 0, K), c["ljk"], A("jk", 0, K), True, False)
+        if rnd == 0:
+            fill(A("cwin", 0, K), 0)
         cp(A("jl", 0, 32), A("ps0", 0, 32))
         tt(A("oh", 0, K), IX("rf", 0, F, "jl", 0, 32), KC, OP.is_equal)
-        tolist(A("ps1", 0, 32), "pi", "oh", 0, K, False, True)
-        tolist(A("ps2", 0, 32), "p128", "oh", 0, K, False, False)
-        tolist(A("ps3", 0, 32), "one", "oh", 0, K, True, False)
+        act(A("jb", 0, 32), A("ps0", 0, 32), AF.Copy)
+        mm(A("ps0", 0, 32), c["i16"], A("jb", 0, 32), True, False)
+        mms([(A("ps2", 0, 32), c["i16"], A("jb", 0, 32), True, False), (A("ps2", 0, 32), c["i143"], A("vl", 0, 32), False, False)])
+        tolist(A("ps0", 0, 32), "pi", "oh", 0, K, False, True)
         tt(A("lh", 0, K), IX("lb", 0, F, "jl", 0, 32), A("oh", 0, K), OP.mult)
         tolist(A("ps2", 0, 32), "neg", "lh", 0, K, False, True)
-        ts(A("t1u", 0, 32), A("ps1", 0, 32), 8.0, OP.add)
+        ts(A("t1u", 0, 32), A("ps0", 0, 32), 8.0, OP.add)
         ts(A("t0u", 0, 32), A("ps2", 0, 32), 8.0, OP.add)
-        mm(A("ps6", 0, K), c["obpi"], A("oh", 0, K), False, False)
-        mm(A("ps6", 0, K), c["obm"], A("lh", 0, K), False, True)
-        mm(A("ps5", 0, K), c["obn"], A("oh", 0, K), True, False)
-        mm(A("ps5", 0, K), OB, A("lh", 0, K), False, True)
-        act(A("t0c", 0, K), A("ps6", 0, K), AF.Identity, bias=-P / 2.0)
-        act(A("lrep", 0, K), A("ps5", 0, K), AF.Copy)
+        mm(A("ps6", 0, K), c["loh"], A("oh", 0, K), False, False)
+        mm(A("ps6", 0, K), c["llh"], A("lh", 0, K), False, False)
         for h in range(2):
             a, b = h * 256, h * 256 + 256
             act(A("r1", a, b), IX("run", 0, P + 8, "t1u", 16 * h, 16 * h + 16), AF.Identity, bias=1.0)
             tt(A("zi", a, b), IX("run", 0, P + 8, "t0u", 16 * h, 16 * h + 16), A("r1", a, b), OP.subtract)
             ts(A("zi", a, b), A("zi", a, b), 255, OP.bitwise_and)
             act(A("zb", a, b), A("zi", a, b), AF.Identity, bias=255.0, scale=-1.0)
-            tolist(A("ps3", 16 * h, 16 * h + 16), "w2", "zb", a, b, False, h == 1)
-        cp(A("hi", 0, 32), A("ps3", 0, 32))
-        ts(A("ow", 0, 32), A("hi", 0, 32), 15, OP.bitwise_and)
-        ind = A("ind", 0, 288)
-        tt(ind, IX("ow", 0, 32, "cu", 2, 20), OWN, OP.is_equal)
-        mm(A("ps7", 0, 288), OB, ind, True, True)
-        mm(A("ps4", 0, 288), c["nui"], ind, True, False)
-        ts(A("owf", 0, 32), A("ow", 0, 32), 256.0, OP.mult)
-        mm(A("ps0", 0, 32), c["i4352"], A("ind", 256, 288), True, False)
-        mm(A("ps0", 0, 32), I16, A("owf", 0, 32), False, False)
-        scan(A("cs", 0, 288), M32, A("ps7", 0, 288), 0.0, OP.mult, OP.add)
-        mm(A("ps4", 0, 288), I16, A("cs", 0, 288), False, True)
-        tt(A("prod", 0, 288), ind, A("ps4", 0, 288), OP.mult)
-        for o in range(9):
-            mm(A("ps0", 0, 32), I16, A("prod", 32 * o, 32 * o + 32), False, o == 8)
-        ts(A("ql", 0, 32), A("ps0", 0, 32), -256.0, OP.add)
-        cp(IX("swin", 0, 9 * ST, "ql", 0, 32), A("zb", 0, K))
+            tolist(A(("ps3", "ps1")[h], 0, 16), "w2", "zb", a, b, True, True)
+        for h, (hs, cb_, pb, ob) in enumerate((("ps3", "ps7", "ps4", "ps0"), ("ps1", "ps5", "ps2", "ps3"))):
+            a, b, e = 16 * h, 16 * h + 16, 144 * h
+            tt(A("hi", a, b), A(hs, 0, 16), A("vl", a, b), OP.add)
+            ts(A("ow", a, b), A("hi", a, b), 15, OP.bitwise_and)
+            ind = A("ind", e, e + 144)
+            tt(ind, IX("ow", a, b, "cu", 2, 11), OWN, OP.is_equal)
+            mm(A(cb_, 0, 144), OB, ind, True, h == 0)
+            if h == 1:
+                mm(A(cb_, 0, 144, 16), I16, A("cs", 15, 144, 16), False, True)
+            mm(A(pb, 0, 144), c["nui"], ind, True, False)
+            ts(A("owf", a, b), A("ow", a, b), 256.0, OP.mult)
+            mms([(A(ob, 0, 16), c["i4352"], A("ind", e + 128, e + 144), True, False), (A(ob, 0, 16), I16, A("owf", a, b), False, False)])
+            scan(A("cs", e, e + 144), A("cj", 224, 368), A(cb_, 0, 144), 0.0, OP.mult, OP.add)
+            mm(A(pb, 0, 144), I16, A("cs", e, e + 144), False, True)
+            tt(A("prod", e, e + 144), ind, A(pb, 0, 144), OP.mult)
+            mms([(A(ob, 0, 16), I16, A("prod", e + 16 * o, e + 16 * o + 16), False, o == 8) for o in range(9)])
+            ts(A("ql", a, b), A(ob, 0, 16), -256.0, OP.add)
+            cp(IX("swin", 0, 9 * ST, "ql", a, b), A("zb", 16 * a, 16 * b))
         land = "land%d" % rnd
-        send(lambda r: A("swin", r * ST, r * ST + 32), A(land, rank * 32, rank * 32 + 32), "ka%d" % rnd, "ks%d" % rnd, [A("fwin", 0, 9 * ST)] if rnd == 0 else [])
-        cp(A(land, rank * 32, rank * 32 + 32), A("swin", rank * ST, rank * ST + 32))
+        send(lambda r: A("swin", r * ST, r * ST + 32), A(land, rank * 32, rank * 32 + 32), "ka%d" % rnd, "ks%d" % rnd)
+        act(A(land, rank * 32, rank * 32 + 32), A("swin", rank * ST, rank * ST + 32), AF.Copy)
         if rnd == 0:
-            ms(A("cwin", 0, K), 0.0)
             for o in range(8):
-                ms(A("swin", o * ST, o * ST + 32), -1.0)
+                fill(A("swin", o * ST, o * ST + 32), -1)
+
+    def gathered():
+        count = lambda x, h: [(A("ps7", x, x + 16), I16, A("prod", 144 * h + 16 * o, 144 * h + 16 * o + 16), False, o == 8) for o in range(9)]
+        for h in range(2):
+            mms([(A("ps7", 32 + 16 * h, 48 + 16 * h), c["p64"], A("ind", 144 * h + 128, 144 * h + 144), True, False)] + count(32 + 16 * h, h))
+            mms([(A("ps7", 16 * h, 16 * h + 16), IS16, A("owf", 16 * h, 16 * h + 16), True, False)] + count(16 * h, h))
+        snt = A("snt", 0, 32)
+        ts(snt, A("ps7", 32, 64), 32.0, OP.is_lt)
+        ts(A("sid", 0, 32), A("ps7", 0, 32), -16.0, OP.add)
+        mms([(A("ps4", 64, 96), I32, K2, True, False), (A("ps4", 64, 96), c["n8k"], snt, False, True),
+             (A("ps4", 0, 32), OB, snt, True, True), (A("ps4", 32, 64), c["nui"], snt, True, True)])
+        mms([(A("ps6", x, K, 16), c[x], A("sid", 0, 32), False, x == 15) for x in range(16)])
+        act(A("rec", 0, K), A("ps6", 0, K), AF.Identity, bias=RB)
+        act(A("rwin", 0, KS), RD, AF.Copy)
+        scan(A("ci", 0, 32), A("ps4", 0, 32), A("ck", 1600, 1632), 0.0, OP.add, OP.add)
+        tt(A("o1", 0, 32), A("ps4", 32, 64), A("ci", 0, 32), OP.add)
+        tt(A("o2", 0, 32), A("ps4", 64, 96), A("o1", 0, 32), OP.max)
+        cp(A("cof", 0, 32), A("o2", 0, 32))
+        cp(IX("rwin", 0, KS + K, "cof", 0, 32), A("rec", 0, K))
+        act(A("rb", 0, KS), A("rwin", 0, KS), AF.Copy)
+        tolist(A("ps7", 0, 17), "r0", "rb", 0, KS, True, True)
+        mm(A("ps4", 0, KS), c["r1"], A("rb", 0, KS), True, True)
+        mm(A("ps6", 0, KS), R2, A("rwin", 0, KS), True, True)
+        cp(A("qc", 0, 17), A("ps7", 0, 17))
+        act(A("lrep", 0, KS), A("ps4", 0, KS), AF.Copy)
+        act(A("t0c", 0, KS), A("ps6", 0, KS), AF.Copy)
 
     def owner(rnd):
         ld = "land%d" % rnd
         land = A(ld, 0, 256)
         nel = A("nel", 0, 256)
         arrive("ka%d" % rnd, [A(ld, 32 * r, 32 * r + 32) for r in range(8) if r != rank])
-        if rnd == 0:
-            mm(A("ps2", 0, 256), c["obw2"], land, True, True)
+        mm(A("ps2", 0, 256), c["obw2"], land, True, True)
+        act(A("qb", 0, 256), A("ps2", 0, 256), AF.Identity, bias=128.50003, scale=2.0 ** -15)
         tolist(A("ps1", 0, 16), "w2", ld, 0, 256, True, True)
-        if rnd == 1:
-            mm(A("ps2", 0, 256), c["obw2"], land, True, True)
+        mm(A("ps5", 0, 256), c["obw8"], land, True, False)
+        mm(A("ps5", 0, 256), c["n2k"], A("qb", 0, 256), False, True)
+        back = 2048.0 * 129 - rank / 8.0
+        ts(A("prh", 0, 256), A("ps5", 0, 256), back, OP.add)
         act(A("nel" if rnd == 0 else "inv", 0, 256), land, AF.Relu, scale=-1.0)
         cp(A("hli", 0, 16), A("ps1", 0, 16))
         if rnd == 1:
             ts(A("pl2", 0, 16), A("hli", 0, 16), 32767, OP.bitwise_and, 4, OP.arith_shift_right)
             cp(A("plu", 0, 16), A("pl2", 0, 16))
             tt(A("ne", 0, 256), IX("store", 0, TS + 256, "plu", 0, 16), land, OP.not_equal)
-            tolist(A("ps6", 0, 16), "one", "ne", 0, 256, True, True)
-            mm(A("ps5", 0, 256), c["obm"], A("inv", 0, 256), True, False)
-            mm(A("ps5", 0, 256), OB, A("ne", 0, 256), False, True)
-            act(nel, A("ps5", 0, 256), AF.Relu, bias=1.0, scale=-1.0)
+            tolist(A("ps0", 0, 16), "one", "ne", 0, 256, True, True)
+            mm(A("ps2", 0, 256), c["obm"], A("inv", 0, 256), True, False)
+            mm(A("ps2", 0, 256), OB, A("ne", 0, 256), False, True)
+            act(nel, A("ps2", 0, 256), AF.Relu, bias=1.0, scale=-1.0)
         ts(A("pli", 0, 16), A("hli", 0, 16), 2 ** 21 + 32767, OP.bitwise_and, 4, OP.arith_shift_right)
-        cp(A("hri", 0, 256), A("ps2", 0, 256))
-        ts(A("hri", 0, 256), A("hri", 0, 256), 32767, OP.bitwise_and, 4, OP.arith_shift_right)
-        cp(A("prh", 0, 256), A("hri", 0, 256))
         mm(A("ps3", 0, 256), c["ob4"], nel, True, False)
         if rnd == 0:
             cp(A("pm", 0, 16), A("pli", 0, 16))
         else:
-            ts(A("sn", 0, 16), A("ps6", 0, 16), 0.0, OP.is_equal, 4096.0, OP.mult)
+            ts(A("sn", 0, 16), A("ps0", 0, 16), 0.0, OP.is_equal, 4096.0, OP.mult)
             tt(A("pm", 0, 16), A("sn", 0, 16), A("pli", 0, 16), OP.add)
-        m = 0
-        for a in range(16):
-            n = 256 - 16 * a
-            ts(A("mb", m, m + n), A("prh", 16 * a, 256), A("pm", a, a + 1), OP.is_equal)
-            mm(A("ps3", 16 * a, 16 * a + 16), c["obp"], A("mb", m, m + 16), False, a == 15)
+        at = [256 * a - 8 * a * (a - 1) for a in range(17)]
+
+        def weigh(a, last):
+            l = [(A("ps3", 16 * a, 16 * a + 16), c["obp"], A("mb", at[a], at[a] + 16), False, last and a == 15)]
             if a < 15:
-                mm(A("ps3", 16 * a + 16, 256), c["ob4"], A("mb", m + 16, m + n), False, False)
-            m += n
+                l.append((A("ps3", 16 * a + 16, 256), c["ob4"], A("mb", at[a] + 16, at[a + 1]), False, last))
+            return l
+        act(A("pm", 16, 32), A("pm", 0, 16), AF.Identity, bias=-back)
+        for a in range(SA, 16):
+            act(A("mb", at[a], at[a + 1]), A("ps5", 16 * a, 256), AF.Abs, bias=A("pm", 16 + a, 17 + a), scale=-1.0)
+        act(A("mb", at[SA], at[16]), A("mb", at[SA], at[16]), AF.Relu, bias=1.0, scale=-1.0)
+        for a in range(SA):
+            ts(A("mb", at[a], at[a + 1]), A("prh", 16 * a, 256), A("pm", a, a + 1), OP.is_equal)
+            if a == SA - 2:
+                mms(sum([weigh(x, False) for x in range(SA, 16)], []))
+            mms(weigh(a, a == SA - 1))
         tt(A("nw", 0, 256), A("ps3", 0, 256), THR, OP.is_lt)
-        send(lambda r: A("nw", r * 32, r * 32 + 32), A("fwin", rank * ST, rank * ST + 32), "fa%d" % rnd, "fs%d" % rnd)
-        cp(A("fwin", rank * ST, rank * ST + 32), A("nw", rank * 32, rank * 32 + 32))
-        arrive("fa%d" % rnd, [A("fwin", ST * r, ST * r + 32) for r in range(8) if r != rank])
+        send(lambda r: A("nw", r * 32, r * 32 + 32), A("fwin", rank * 32, rank * 32 + 32), "fa%d" % rnd, "fs%d" % rnd)
+        act(A("fwin", rank * 32, rank * 32 + 32), A("nw", rank * 32, rank * 32 + 32), AF.Copy)
+        if rnd == 0:
+            iota(A("kidb", 0, W), [[1, W]], 0, 0, False)
+        arrive("fa%d" % rnd, [A("fwin", 32 * r, 32 * r + 32) for r in range(8) if r != rank])
 
     def store(rnd):
-        tolist(A("ps7", 0, 16), "six", "nw", 0, 256, True, True)
+        tolist(A("ps5", 0, 16), "six", "nw", 0, 256, True, True)
         tt(A("sx", 0, 16), A("pli", 0, 16), QC, OP.subtract)
-        tt(A("sy", 0, 16), A("ps7", 0, 16), A("sx", 0, 16), OP.mult)
+        tt(A("sy", 0, 16), A("ps5", 0, 16), A("sx", 0, 16), OP.mult)
         tt(A("sz", 0, 16), A("sy", 0, 16), QC, OP.add)
         cp(A("su", 0, 16), A("sz", 0, 16))
         cp(IX("store", 0, TS + 256, "su", 0, 16), A("land%d" % rnd, 0, 256))
@@ -521,26 +598,27 @@ def build(core, T, topo):
     def nextfront(rnd):
         hold = A("hold", 0, F)
         starts = A("pwin", 0, 2 * F, 2)
-        mm(A("ps0", 0, 33), I32, NC, True, False)
-        tt(A("xl", 0, KS), IX("fwin", 0, 9 * ST + 16, "ql", 0, 33), A("lrep", 0, KS), OP.mult)
+        mm(A("ps0", 0, 17), I32, NC, True, False)
+        tt(A("xl", 0, KS), IX("fwin", 0, KS, "qc", 0, 17), A("lrep", 0, KS), OP.mult)
         scan(A("cum", 1, KS + 1), A("xl", 0, KS), CAPH, 0.0, OP.add, OP.min)
-        tolist(A("ps0", 0, 33), "n256", "xl", 0, KS, False, True)
-        tolist(A("ps1", 0, 33), "h8", "cum", 0, KS, True, False)
-        act(A("yb", 0, 33), A("ps0", 0, 33), AF.Relu)
-        mm(A("ps1", 0, 33), I32, A("yb", 0, 33), False, True)
+        tolist(A("ps0", 0, 17), "n256", "xl", 0, KS, False, True)
+        tolist(A("ps1", 0, 17), "h8", "cum", 0, KS, True, False)
+        act(A("yb", 0, 17), A("ps0", 0, 17), AF.Relu)
+        mm(A("ps1", 0, 17), I32, A("yb", 0, 17), False, True)
         ts(A("ex", 0, KS), A("cum", 1, KS + 1), float(F), OP.is_gt, 4096.0, OP.mult)
-        cp(A("ofu", 0, 33), A("ps1", 0, 33))
-        tt(IX("pwin", 0, 2624, "ofu", 0, 33), A("t0c", 0, KS), A("ex", 0, KS), OP.add)
+        cp(A("ofu", 0, 17), A("ps1", 0, 17))
+        tt(IX("pwin", 0, 1600, "ofu", 0, 17), A("t0c", 0, KS), A("ex", 0, KS), OP.add)
         scan(hold, A("xf", 0, F), starts, -4096.0, OP.add, OP.max)
         tolist(A("ps2", 0, 14), "h16", "hold", 0, F, True, True)
         ts(A("tju", 0, 14), A("ps2", 0, 14), P / 2.0, OP.add, float(P), OP.min)
         iu, iv = IX("tuv", 0, TW, "tju", 0, 14), IX("tuv", TW, 2 * TW, "tju", 0, 14)
         ts(A("drp", 0, F), hold, -1.0, OP.mult, -2000.0, OP.min)
         if rnd == 0:
-            cp(A("kk", 0, F), iu)
-            cp(A("kk", F, 2 * F), iv)
+            for a, b in ((0, 2), (2, 14)):
+                for h in range(2):
+                    cp(A("kk", h * F + 16 * a, h * F + 16 * b), IX("tuv", h * TW, h * TW + TW, "tju", a, b))
             tt(A("nf", 0, F), starts, A("drp", 0, F), OP.is_le)
-            ms(A("pwin", 0, 2 * F), -2048.0)
+            fill(A("pwin", 0, 2 * F), -2048)
         else:
             row = (0, 128, 16)
             tt(A("fin", 2 * F, 3 * F), starts, A("drp", 0, F), OP.is_gt)
@@ -555,17 +633,19 @@ def build(core, T, topo):
         big(rnd)
         tables(rnd)
         control(rnd)
+        gathered()
         owner(rnd)
         store(rnd)
         nextfront(rnd)
     return ops
 
 
-def schedule(ops, hop=0.045):
-    n = len(ops)
+ORDER = "B2A.AKAMALANASAOAPAQARATA*A(A=A/AUB0AVB)B7B<B=B:B>B;CIAXBTC*AYCCB(BYB-BVBUC(BWC)BXCDAWAFA2A?A1B1ACAJAEADA7A<A0A8A3A;A6AHA:A9AIAGA4A5A@AAA>ABA)CEB@BHBEBKBAB/B*BQBRBSBNBPB,B+BOB4CJBBB3BDC+CLC.C0BCC-C1BGCNBJCOBMCHCMB.B5C,C6C4C5C8C;C:C3CFCGBFBLBIC/CPCKB6A+A,A-CRB?C7CSEMEVC9B9B8ENCTCVCWC2CQCUCXCYH@D(D*D:D)D+D8D;DHD.D-D,D9D/DID<D>D=DJE1DXDYD0D?DKD1D4DLD2D5D@DOE(DADDDME2DBDPDEDNE)DQE3E*D3E;E>D6DFDCDTE+D7E4E,E<E5E-E6DUDRE.E7DGE8DVDSE/E9E0E?E=EAEDDWE:F-F/E@F.EBF4F0F1F2F3F5F7FNFMF6FLFOF:F@F8EGF;FAEEFYFQECFRFPF<G(FSEFFTEHFUEIFVEJFWEKFXG-ELF=G)FFFBF>G*F?G.G+G/FCFGC=F9G0FDFHFIEOC?FEG4G1G3FJG,G2G6FKG:G5G7G;G<C@CBG?G@C<G=G>C>CAGAGDGEGFGIGBGCGGGHGQGKGRGSGJG8GLGTGUGVGMGYGWGNH(GOH)GXH7H*H8H9GPH+H,H-G9H:H;H=H<H>HAHBEPEYESEQERF(H?H.EXHCHDHEHMIPHNHPHQHOHTHFHRHWHHHUHVHSHXI.I/HYI(I)I0I1I2I4I6I8I:I<I>I@ICIKI3I5I7I9I*I+I,I-I;I=I?IAIBIDIEHIHGIJILHJIMINIOEUEWETHKIGF,NFHLIFH5H3H6H/IIIQIRISIUF+F)F*IWITIVIXIYJ(J+J0J)J*J,J.J-J/J7J9J8JIJ:IHH0H1H4H2J1JGJJJYJHJWJ=J;JLJ<JKJMK@K(J>JXJNJ?K5K6K)JCJ@KAK,J3JOJDJAK-K7J4JPJSK+K8K*K1K.KBKMJEJBKJJQJTK;K2KDK/KEK<KKJUJRJ5JFKCK9K:K=KFJVK>KGK0J6K3K4K?KHKSKPLILJKNJ2KLKIL<LCL>KOL?L@L=M)LALDLBKQLFM,M+M*LEKRKTM.LPLOLGKVKULKM/LQM-M0KXM1M6M2M3KYM4L(M5KWM:LRLLM7LMM9LSL)M<LNM8LULVLWL3L*M>LHLXM=LTMBM@M?MALYMCM;L8L9M(MDMHMMMEMIMJMKMNMOMPMLMRMSMWMTMFMQMXMUMVN-N.MYN/N(N)N0N1N2N*L7L2L,L.L;N3N5N6N+N7N,N=N4N8N9N>N?N@MGN:NANBNDNCNGN<NENHNINJNKL:L-N;NSNVO)NTO(NUL+NLNWO.NXO*O+O,O-O/O0O1NYO3O4O2O<O>OJO@OBODOFOHOQOLOXONO5O6O7O8O9O:O;L/L0L1O=O?OAOCOEOGOIOKOMOOOPOROSP,OTNNNONMOWNPOYP(NROUNQL6L4P)P*P+OVP-P/P.P0P3P1L5P2P4P5P6P9P7P:P8P<P;P>P?P="
+
+
+def needs(ops):
     ent = {}
-    succ = [[] for _ in ops]
-    left = [0] * n
+    pred = []
     sent = None
     for i, o in enumerate(ops):
         deps = set()
@@ -585,8 +665,22 @@ def schedule(ops, hop=0.045):
                 e[:] = [y for y in e if not (c0 <= y[0] and y[1] <= c1)]
             e.append((c0, c1, i, w))
         deps.discard(i)
-        left[i] = len(deps)
-        for j in deps:
+        pred.append(deps)
+    return pred
+
+
+def schedule(ops, hop=0.045):
+    n = len(ops)
+    pred = needs(ops)
+    given = [(ord(ORDER[2 * x]) - 65) * 50 + ord(ORDER[2 * x + 1]) - 40 for x in range(len(ORDER) // 2)]
+    if sorted(given) == list(range(n)):
+        at = {i: x for x, i in enumerate(given)}
+        if all(at[j] < at[i] for i in range(n) for j in pred[i]):
+            return [ops[i] for i in given]
+    succ = [[] for _ in ops]
+    left = [len(p) for p in pred]
+    for i, p in enumerate(pred):
+        for j in p:
             succ[j].append(i)
     tail = [0.0] * n
     for i in range(n - 1, -1, -1):

import math
from concourse.bass import DstId, RemoteDMATransfer
from concourse.mybir import AluOpType as OP, ActivationFunctionType as AF

W, F, P, K, TS = 3072, 224, 3584, 512, 2048
CW, NCH, LC = 448, 8, 28
ST = 512
TW = P + 16
KS = 256 + 16
SA = 11
CLAMP = 6912.0
LN4, LN2 = math.log(4.0), math.log(2.0)
CFG = {
    "vs": ["vvvvvvsv", "vvvvvvsv"],
    "qs": ["ssssszzz", "ssssszzz"],
    "gr": [[[0, 1], [2, 3], [4, 5], [6], [7]], [[0, 1], [2, 3], [4, 5], [6], [7]]],
}

SCRATCH = {}
for _d, _l in (
    ("int32", "kidb:3072 fuv:28 fsb:224 rmi:2 zi:512 hi:32 ow:32 hli:16 pli:16 pl2:16 cint:160 cpi:160"),
    ("uint16", "uv:28 kk:448 cof:32 jl:32 t1u:32 t0u:32 ql:32 qc:18 plu:16 su:16 ofu:18 tju:16 cu:24"),
    ("float16", "prh:256 uvh:448 cs:288 prod:288 owf:32 cum:280 hold:224 ch:1000"),
    ("bfloat16", "vecb:3072 markb:3072 va:1792 vb:1792 nz:1792 qa:3584 mq:3584 nf:232 fsf:224 adv:224 lbn:224 z0:232 drp:224 cand:224 lb:224 "
     "nls:16 cwin:3808 jk:512 oh:512 lh:512 lrep:272 zb:512 ind:288 swin:4608 fwin:272 land0:256 land1:256 store:2304 inv:256 ne:256 "
     "nel:256 mb:2176 nw:256 xl:272 xf:224 sid:32 snt:32 vl:32 jb:32 qb:256 rb:272 cb:6640 cj:1400"),
    ("float32", "dd:3584 run:3592 tuv:7200 eb:232 bc:224 rmf:2 yl:224 cinc:224 rf:224 ci:32 o1:32 o2:32 r1:512 pm:32 sn:16 sx:16 sy:16 sz:16 "
     "yb:18 t0c:272 ex:272 pwin:1600 fin:672 rec:512 rwin:784 cf:720 ck:3000"),
):
    for _x in _l.split():
        SCRATCH[_x.split(":")[0]] = ("sbuf", [128, int(_x.split(":")[1])], _d)
for _x in range(8):
    SCRATCH["ps%d" % _x] = ("psum", [128, 512], "float32")
SEMAPHORES = ["qv", "qs", "qt", "qg"] + ["d_" + _x for _x in "l0 l1 l2 l3 l4 l5 w0 w1 w2 w3 ka0 ka1 fa0 fa1 ks0 ks1 fs0 fs1".split()]


def A(b, c0, c1, st=1, p=None):
    return (b, c0, c1, st, p)


def IX(b, c0, c1, off, o0, o1):
    return (b, c0, c1, off, o0, o1)


def bank(b):
    return b.startswith("ps") and b[2:].isdigit()


CYCLE = 0.00095
GATHER, SCATTER = 1.4, 2.5


def estimate(q, out, ins, two):
    n = (out[2] - out[1] + out[3] - 1) // out[3] if len(out) == 5 else 0
    if q == "t":
        return max(64, n) * (4 if SCRATCH[ins[0][0]][2] == "float32" else 1) * CYCLE / 2
    for a, rate in ((out, SCATTER), (ins[0], GATHER)):
        if len(a) == 6:
            return 0.06 + 16 * (a[5] - a[4]) * rate * CYCLE
    f = 1.0
    if q == "g":
        return 0.13 + 2 * n * CYCLE
    if q == "v" and two and not any(bank(a[0]) for a in ins):
        f = 2.0
    elif q == "v" and not two and all(SCRATCH[a[0]][2] in ("bfloat16", "float16", "uint16") for a in [out] + ins):
        f = 0.5
    return max(64, n * f) * CYCLE + 0.02


def build(core, T, topo):
    rank = T.rank_of(core)
    ops = []
    isap = lambda s: isinstance(s, tuple)

    def X(a):
        if len(a) == 6:
            return T[a[0]][:, a[1]:a[2]].indirect(T[a[3]][:, a[4]:a[5]])
        p = a[4]
        if p is None:
            return T[a[0]][:, a[1]:a[2]:a[3]] if a[3] != 1 else T[a[0]][:, a[1]:a[2]]
        return T[a[0]][p[0]:p[1]:p[2], a[1]:a[2]]

    def acc(a):
        return [(a[0], a[1], a[2]), (a[3], a[4], a[5])] if len(a) == 6 else [(a[0], a[1], a[2])]

    def add(q, fn, reads, writes, sem=None, inc=0, est=None, two=False):
        rd = []
        wr = []
        for a in reads:
            rd += acc(a)
        for a in writes:
            x = acc(a)
            wr += x[:1]
            rd += x[1:]
        whole = [len(a) == 5 and a[3] == 1 and a[4] is None for a in writes]
        if est is None:
            est = estimate(q, writes[0], [a for a in reads if a[2] - a[1] > 1] or reads[:1] or [writes[0]], two)
        ops.append({"q": q, "fn": fn, "r": rd, "w": wr, "whole": whole, "sem": sem, "inc": inc, "est": est})

    def tt(out, a, b, op):
        add("v", lambda g: g.vector.tensor_tensor(X(out), X(a), X(b), op), [a, b], [out], two=True)

    def ts(out, a, s1, op0, s2=None, op1=None):
        rd = [a] + [s for s in (s1, s2) if isap(s)]
        x = lambda s: X(s) if isap(s) else s
        if op1 is None:
            add("v", lambda g: g.vector.tensor_scalar(X(out), X(a), x(s1), None, op0), rd, [out])
        else:
            add("v", lambda g: g.vector.tensor_scalar(X(out), X(a), x(s1), x(s2), op0, op1), rd, [out])

    def cp(out, a):
        add("v", lambda g: g.vector.tensor_copy(X(out), X(a)), [a], [out])

    def ms(out, v):
        add("v", lambda g: g.vector.memset(X(out), v), [], [out])

    def scan(out, a, b, init, op0, op1):
        rd = [a, b] + ([init] if isap(init) else [])
        add("v", lambda g: g.vector.tensor_tensor_scan(X(out), X(a), X(b), X(init) if isap(init) else init, op0, op1), rd, [out])

    def act(out, a, func, bias=0.0, scale=1.0):
        rd = [a] + [s for s in (scale, bias) if isap(s)]
        x = lambda s: X(s) if isap(s) else s
        add("s", lambda g: g.scalar.activation(X(out), X(a), func, bias=x(bias), scale=x(scale)), rd, [out])

    def mms(lst):
        def fn(g):
            return [g.tensor.matmul(X(o), X(l), X(r), s0, s1) for o, l, r, s0, s1 in lst][-1]
        add("t", fn, list(dict.fromkeys([x[1] for x in lst] + [x[2] for x in lst])), [lst[0][0]], est=sum(estimate("t", x[0], [x[1]], False) for x in lst))

    def mm(out, l, r, start, stop):
        mms([(out, l, r, start, stop)])

    def iota(out, pat, base, cm, f):
        if f:
            add("g", lambda g: g.iota(X(out), pat, base, cm, allow_small_or_imprecise_dtypes=True), [], [out])
        else:
            add("g", lambda g: g.iota(X(out), pat, base, cm), [], [out])

    def fill(a, v):
        iota(a, [[0, a[2] - a[1]]], v, 0, True)

    def dma(q, out, a, sem, est):
        o = (lambda: T[out][:]) if isinstance(out, str) else (lambda: X(out))
        i = (lambda: T[a][:]) if isinstance(a, str) else (lambda: X(a))
        e = (lambda g: g.sync) if q == "y" else (lambda g: g.scalar)
        add(q, lambda g: e(g).dma_start(o(), i()), [] if isinstance(a, str) else [a], [] if isinstance(out, str) else [out], "d_" + sem, 16, est)

    def share(a, b):
        return len(topo.engines(a, b)) // 8

    def send(src, dst, rsem, lsem, after=()):
        others = [r for r in range(8) if r != rank]

        def fn(g):
            tr = []
            for n, r in enumerate(others):
                d = T.cores[r]
                rid, pid = topo.addr(d)[:2]
                e = share(core, d)
                m = 0
                for x in topo.engines(core, d)[n * e:n * e + e]:
                    m |= 1 << x
                tr.append(RemoteDMATransfer(dst_ids=[DstId(rid=rid, pnc=pid)], dma_engine_mask=m, remote_sem=T.sem["d_" + rsem], srcs=[X(src(r))], dsts=[X(dst)]))
            return g.remote_dma_fused(tr, local_sem=T.sem["d_" + lsem])
        add("g", fn, [src(r) for r in others] + list(after), [], "d_" + lsem, sum(share(core, T.cores[r]) for r in others), 2.5)

    def arrive(rsem, dsts):
        add("x", None, [], dsts, "d_" + rsem, sum(share(T.cores[r], core) for r in range(8) if r != rank), 0.3)

    dma("y", A("fuv", 0, 14), "fu", "l0", 2.0)
    dma("y", A("fuv", 14, 28), "fv", "l1", 2.0)
    dma("s", A("fsb", 0, F, 1, (0, 8, 1)), "fs", "l2", 2.0)
    dma("y", A("kidb", 0, W), "kids", "l3", 8.3)
    dma("y", A("vecb", 0, W), "vec", "l4", 5.1)
    dma("y", A("markb", 0, W), "mark", "l5", 5.1)
    KC = A("ck", 0, K)
    S16 = A("ck", 512, 545)
    QM = A("ck", 560, 816)
    THR = A("ck", 816, 1072)
    CAP = A("ck", 1072, 1072 + KS)
    K2 = A("ck", 1344, 1376)
    EI = 1376
    R2 = A("ck", 1400, 1528)
    ZERO = A("ck", 1600, 1824)
    JC = A("ck", 1824, 1838)
    QC = A("ck", 1840, 1856)
    NC = A("ck", 1856, 1873)
    I32 = A("ck", 1920, 2048)
    D, DLO, DHI = A("ck", 2048, 2176), A("ck", 2176, 2304), A("ck", 2304, 2432)
    MH, U = A("ck", 2432, 2560), A("ck", 2560, 2688)
    RD = A("ck", 2688, 2688 + KS)
    JV = A("cj", 0, F)
    M16 = A("cj", 224, 672)
    OWN = A("cj", 960, 1104)
    ONE = A("cj", 225, 226)
    iota(A("cint", 0, 1), [[0, 1]], 0, 1, False)
    iota(A("cint", 8, 152), [[1, 144]], 0, 0, False)
    iota(S16, [[16, 33]], 0, 0, True)
    fill(A("cj", 224, 672), 1)
    for a, v in ((A("nf", F, F + 8), 0), (A("eb", 0, 8), 0), (A("z0", 0, 8), 1), (A("run", 0, 8), 0), (ZERO, 0)):
        fill(a, v)
    iota(QM, [[0, 16], [1, 16]], 0, 0, True)
    iota(JV, [[1, F]], 0, 0, True)
    fill(A("cwin", 0, K), 0)
    iota(KC, [[1, K]], -8192, 0, True)
    iota(CAP, [[1, KS]], 256, 0, True)
    iota(A("cj", 960, 1088), [[2, 8], [0, 16]], 1, 0, True)
    fill(A("cj", 1088, 1104), 0)
    for o in range(8):
        fill(A("swin", o * ST, o * ST + 32), -1)
    for a, v in ((A("fwin", 256, KS), 0), (A("fwin", 256, 257), 1), (A("store", 0, TS + 256), -1), (A("pwin", 0, 2 * F), -2048), (A("xf", 0, F), 1)):
        fill(a, v)
    P0 = A("cf", 0, 1)
    PI = A("cf", 1, 2)
    PG = A("cf", 2, 3)
    PB = A("cf", 3, 4)
    W2 = A("cf", 4, 5)
    MB = A("cf", 5, 6)
    MBN = A("cf", 6, 7)
    PW = A("cf", 7, 8)
    P128 = A("cf", 8, 9)
    P129 = A("cf", 9, 10)
    RB = A("cf", 10, 11)
    NL4 = A("cf", 12, 13)
    cp(P0, A("cint", 0, 1))
    ts(A("cpi", 0, 1), A("cint", 0, 1), 15, OP.bitwise_and)
    ts(A("cpi", 1, 2), A("cint", 0, 1), 4, OP.arith_shift_right)
    cp(A("cf", 1, 3), A("cpi", 0, 2))
    ts(PB, PG, 16.0, OP.mult, 16.0, OP.add)
    ts(W2, PI, -28.0, OP.mult, 510.0, OP.add)
    ts(MB, PI, 15.0, OP.is_equal, 2.0 ** 19, OP.mult)
    ts(MBN, MB, -1.0, OP.mult, -0.5, OP.add)
    ts(P128, PI, -1.0, OP.mult, 143.1, OP.add)
    ts(P129, PI, -143.0, OP.add)
    YC = A("cf", 16, 160)
    Y128 = A("cf", 16, 144)
    MI = A("cf", 160, 288)
    MG = A("cf", 288, 416)
    BLK = A("cf", 416, 544)
    T1 = A("cf", 544, 672)
    cp(YC, A("cint", 8, 152))
    ts(A("cpi", 8, 136), A("cint", 8, 136), 15, OP.bitwise_and)
    cp(MI, A("cpi", 8, 136))
    ts(A("cint", 8, 136), A("cint", 8, 136), 4, OP.arith_shift_right)
    cp(MG, A("cint", 8, 136))
    ts(BLK, MG, PG, OP.is_equal)
    nb = [0]
    c = {}
    sel_ = {}

    def cbuf(n):
        nb[0] += n
        return A("cb", nb[0] - n, nb[0])

    def mksel(name, wt):
        a = cbuf(144)
        if wt is None:
            ts(a, YC, PB, OP.is_equal)
        else:
            act(a, A("cb", sel_["one"], sel_["one"] + 144), AF.Copy, scale=wt)
        sel_[name] = a[1]

    def sel(name, i):
        if name in ("h16", "h8"):
            b = {"h16": 0, "h8": 144}[name] + 16 - i
            return A("ch", b, b + 128)
        b = sel_[name] + 16 - i
        return A("cb", b, b + 128)

    def tolist(out, name, b, c0, c1, start, stop):
        mms([(out, sel(name, x), A(b, c0 + x, c1, 16), start and x == 0, stop and x == 15) for x in range(16)])

    mksel("one", None)
    IDN, IDM, OB, REP = cbuf(128), cbuf(128), cbuf(128), cbuf(128)
    I16, IM16, CAPH, IS16 = A("ch", 288, 416), A("ch", 416, 544), A("ch", 544, 544 + KS), A("ch", 816, 944)
    ts(IDN, Y128, P0, OP.is_equal)
    act(IDM, IDN, AF.Copy, scale=-1.0)
    act(I32, IDN, AF.Copy)
    act(OB, BLK, AF.Copy)
    ts(REP, MG, P0, OP.is_equal)
    ts(I16, Y128, P0, OP.is_equal)
    ts(IM16, Y128, P0, OP.is_equal, -1.0, OP.mult)
    ms(A("cj", 224, 672, 16), 0.0)
    ms(A("cu", 0, 2), 0)
    cp(A("uv", 0, 28), A("fuv", 0, 28))
    add("v", lambda g: g.vector.tensor_copy(T.fsf[0:8, :], T.fsb[0:8, :]), [A("fsb", 0, F)], [A("fsf", 0, F)])
    add("t", lambda g: g.tensor.matmul(T.ps0[:, 0:F], T.cb[0:8, REP[1]:REP[2]], T.fsf[0:8, :], True, True), [REP, A("fsf", 0, F)], [A("ps0", 0, F)])
    ts(A("nf", 0, F), A("ps0", 0, F), -1.0, OP.mult, 1.0, OP.add)
    mksel("neg", -1.0)
    cp(A("kk", 0, F), IX("kidb", 0, W, "uv", 0, 14))
    cp(A("kk", F, 2 * F), IX("kidb", 0, W, "uv", 14, 28))
    for name, wt in (("six", 1.0 / 16), ("pi", PI), ("w2", W2), ("n256", -256.0)):
        mksel(name, wt)
    act(PW, PI, AF.Exp, scale=-LN2)
    act(THR, QM, AF.Exp, bias=math.log(2.5), scale=-LN2)
    ts(D, MI, PI, OP.subtract)
    ts(T1, BLK, 64.0, OP.mult, -64.0, OP.add)
    tt(DLO, D, T1, OP.add)
    tt(DHI, D, T1, OP.subtract)
    for k, (src, v, op) in enumerate(((DLO, 1.0, OP.is_ge), (DHI, 12.0, OP.is_le), (DHI, -4.0, OP.is_le))):
        c["wc%d" % k], c["b%d" % k] = cbuf(128), cbuf(128)
        ts(c["wc%d" % k], src, v, op)
        act(c["b%d" % k], D, AF.Exp, bias=-16.0 * k * LN4, scale=-LN4)
        tt(c["b%d" % k], c["b%d" % k], c["wc%d" % k], OP.mult)
    c["nui"] = cbuf(128)
    ts(c["nui"], DHI, 0.0, OP.is_le, -1.0, OP.mult)
    for name, wt in (("p64", 64.0), ("n8k", -8192.0), ("i4352", 4352.0), ("i16", 16.0), ("i143", 143.0), ("n2k", -2048.0)):
        c[name] = cbuf(128)
        act(c[name], IDN, AF.Copy, scale=wt)
    ei = lambda x: A("ck", EI + x, EI + x + 1)
    ts(A("ck", EI, EI + 16), A("cf", 16, 32), PI, OP.is_equal)
    for name, wt in (("obw2", W2), ("obp", PW), ("ob4", 4.0), ("obm", -1.0), ("r1", ei(1))):
        c[name] = cbuf(128)
        act(c[name], BLK, AF.Copy, scale=wt)
    c["obw8"] = cbuf(128)
    act(c["obw8"], c["obw2"], AF.Copy, scale=1.0 / 16)
    act(R2, BLK, AF.Copy, scale=ei(2))
    mksel("r0", ei(0))
    tt(MH, MI, T1, OP.subtract)
    for name in ("to0", "to1", "ljk", "llh", "loh"):
        c[name] = cbuf(128)
    for name, v in (("to0", 0.0), ("to1", 1.0), ("ljk", 2.0)):
        ts(c[name], MH, v, OP.is_equal)
    tt(c["llh"], c["to1"], c["ljk"], OP.subtract)
    act(U, c["ljk"], AF.Copy, scale=144.0)
    act(c["loh"], c["to1"], AF.Copy, scale=P129)
    tt(c["loh"], c["loh"], U, OP.add)
    for x in range(16):
        c[x] = cbuf(128)
        act(c[x], c["to0"], AF.Copy, scale=ei(x))
    ts(RB, ei(2), -P / 2.0, OP.mult)
    ts(A("cf", 13, 14), ei(0), 258.0, OP.mult)
    ts(A("cf", 14, 15), ei(1), F + 1.0, OP.mult)
    ts(RD, CAP, 0.0, OP.mult, A("cf", 13, 14), OP.add)
    ts(A("ck", RD[1] + 256, RD[1] + 257), ei(0), 256.0, OP.mult, A("cf", 14, 15), OP.add)
    ts(IS16, Y128, P0, OP.is_equal, 1.0 / 16, OP.mult)
    ts(A("ch", 0, 144), YC, PB, OP.is_equal, 1.0 / 16, OP.mult)
    ts(A("ch", 144, 288), YC, PB, OP.is_equal, 1.0 / 8, OP.mult)
    ts(JC, A("ck", 512, 526), PI, OP.add, float(P), OP.add)
    ts(QC, A("ck", 512, 528), PI, OP.add, float(TS), OP.add)
    ts(K2, A("ck", 512, 544), PI, OP.add, float(KS), OP.add)
    ts(NC, A("ck", 512, 529), PI, OP.add, 0.5, OP.add)
    ts(NC, NC, 2.0, OP.mult)
    ts(A("cu", 2, 12), A("ck", 1600, 1610), PI, OP.add)
    cp(CAPH, CAP)
    ts(A("cum", 0, 8), A("ck", 1600, 1608), 0.0, OP.add)
    add("s", lambda g: g.scalar.activation(X(A("cf", 11, 12)), X(ONE), AF.Ln, scale=0.25), [ONE, PW, THR, c["b0"], c["b1"], c["b2"]], [A("cf", 11, 12)], est=1.6)
    add("v", lambda g: g.vector.reciprocal(T.cf[:, 12:13], T.cf[:, 11:12]), [A("cf", 11, 12)], [NL4])

    def side():
        ts(A("lbn", 0, F), A("nf", 1, F + 1), MB, OP.mult, MBN, OP.add)
        ts(A("uvh", 0, 2 * F), A("kk", 0, 2 * F), -1536.0, OP.add)
        mm(A("ps7", 0, F), I16, A("uvh", 0, F), True, False)
        mm(A("ps7", 0, F), IM16, A("uvh", F, 2 * F), False, True)
        act(A("adv", 0, F), A("ps7", 0, F), AF.Abs)

    def big(rnd):
        vs, qs, gr = [CFG[k][rnd] for k in ("vs", "qs", "gr")]
        for n, grp in enumerate(gr):
            for i in grp:
                vl = (i % 4) * CW
                va, vb = A("va", vl, vl + CW), A("vb", vl, vl + CW)
                iv = IX("vecb", 0, W, "kk", F + i * LC, F + i * LC + LC)
                act(va, IX("vecb", 0, W, "kk", i * LC, i * LC + LC), AF.Copy)
                if vs[i] == "s":
                    act(vb, iv, AF.Copy)
                else:
                    tt(vb, iv, va, OP.subtract)
            j0, j1 = grp[0] * LC, (grp[-1] + 1) * LC
            vl, vh = (grp[0] % 4) * CW, (grp[-1] % 4 + 1) * CW
            raw = [i for i in grp if vs[i] == "s"]
            sb = A("ps%d" % (4 + n % 2), 0, j1 - j0)
            if len(raw) == len(grp):
                mms([(sb, IDN, A("va", vl + x, vh, 16), x == 0, False) for x in range(16)])
            mms([(sb, IDM, A("vb", vl + x, vh, 16), x == 0 and len(raw) < len(grp), x == 15 and len(raw) in (0, len(grp))) for x in range(16)])
            if 0 < len(raw) < len(grp):
                mms([(A(sb[0], raw[0] * LC - j0, (raw[-1] + 1) * LC - j0), IDN, A("va", (raw[0] % 4) * CW + x, (raw[-1] % 4 + 1) * CW, 16), False, x == 15) for x in range(16)])
            for i in grp:
                vl = (i % 4) * CW
                two = vs[i] == "s"
                if two:
                    mm(A("ps%d" % (i % 4), 0, CW), IDN, A("va", vl, vl + CW), True, False)
                mm(A("ps%d" % (i % 4), 0, CW), IDM, A("vb", vl, vl + CW), not two, False)
            scan(A("eb", 1 + j0, 1 + j1), sb, A("nf", 1 + j0, 1 + j1), A("eb", j0, j0 + 1), OP.add, OP.mult)
            ts(A("bc", j0, j1), A("eb", j0, j1), CLAMP, OP.min, -CLAMP, OP.max)
            for i in grp:
                lo, vl = i * CW, (i % 4) * CW
                mm(A("ps%d" % (i % 4), 0, CW, 16), I32, A("bc", i * LC, i * LC + LC), False, True)
                scan(A("dd", lo, lo + CW), M16, A("ps%d" % (i % 4), 0, CW), 0.0, OP.mult, OP.add)
                act(A("nz", vl, vl + CW), A("dd", lo, lo + CW), AF.Abs)
                if i % 2 == 1:
                    tolist(A("ps6", (i - 1) * LC, (i + 1) * LC), "neg", "nz", vl - CW, vl + CW, True, True)
        marks(rnd, [i for i in range(NCH) if i < (qs + "z").index("z")])

    def marks(rnd, chunks):
        qs = CFG["qs"][rnd]
        for i in chunks:
            lo = i * CW
            d, m, qa = [A(b, lo, lo + CW) for b in ("dd", "mq", "qa")]
            iu, iv = IX("markb", 0, W, "kk", i * LC, i * LC + LC), IX("markb", 0, W, "kk", F + i * LC, F + i * LC + LC)
            if qs[i] == "v":
                cp(qa, iu)
            else:
                act(qa, iu, AF.Copy)
            if qs[i] != "z":
                tt(m, iv, qa, OP.max)
            else:
                act(m, iv, AF.Copy)
                ps, more = A("ps%d" % (5 if i % 2 else 1), 0, CW), A("va", (i % 4) * CW, (i % 4 + 1) * CW)
                mms([(ps, IDN, m, True, False), (ps, IDM, qa, False, True)])
                act(more, ps, AF.Relu)
                mms([(ps, IDN, qa, True, False), (ps, IDN, more, False, True)])
                m = ps
            init = 0.0 if i == 0 else A("run", lo + 7, lo + 8)
            if i == NCH // 2:
                cp(A("rmi", 0, 1), A("run", lo + 7, lo + 8))
                ts(A("rmi", 1, 2), A("rmi", 0, 1), 255, OP.bitwise_and)
                cp(A("rmf", 0, 1), A("rmi", 1, 2))
                init = A("rmf", 0, 1)
            scan(A("run", lo + 8, lo + 8 + CW), d, m, init, OP.add, OP.add)

    def tables(rnd):
        for h in range(2):
            act(A("tuv", h * TW + P, h * TW + TW), IX("kidb", 0, W, "cu", 0, 1), AF.Copy)
            for i in range(NCH):
                act(A("tuv", h * TW + i * CW, h * TW + i * CW + CW), IX("kidb", 0, W, "kk", h * F + i * LC, h * F + i * LC + LC), AF.Copy)

    def control(rnd):
        cnt = A("ps6", 0, F)
        cand = A("cand", 0, F)
        tt(A("z0", 2, 2 + F), cnt, A("lbn", 0, F), OP.is_ge)
        tt(A("drp", 0, F), A("adv", 0, F), cnt, OP.is_le)
        for k in range(3):
            mm(A("ps1", 0, F), c["wc%d" % k], A("z0", 2 - k, 2 - k + F), k == 0, False)
        mm(A("ps1", 0, F), c["p64"], A("z0", 2, 2 + F), False, False)
        mm(A("ps1", 0, F), c["n8k"], A("drp", 0, F), False, True)
        for k in range(3):
            mm(A("ps0", 0, F), c["b%d" % k], A("z0", 2 - k, 2 - k + F), k == 0, k == 2)
        ts(cand, A("ps1", 0, F), 64.0, OP.is_gt)
        act(A("yl", 0, F), A("ps0", 0, F), AF.Ln, bias=2.0 ** -60)
        act(A("lb", 0, F), A("yl", 0, F), AF.Identity, bias=P128, scale=NL4)
        marks(rnd, [i for i in range(NCH) if i >= (CFG["qs"][rnd] + "z").index("z")])
        mm(A("ps7", 32, 46), I32, JC, True, False)
        tolist(A("ps2", 0, 14), "one", "cand", 0, F, True, True)
        mm(A("ps3", 0, F), OB, cand, True, True)
        mm(A("ps4", 0, F), c["nui"], cand, True, False)
        mm(A("ps4", 0, F), c["n8k"], cand, False, False)
        cp(A("nls", 0, 14), A("ps2", 0, 14))
        nls = A("nls", 0, 14)
        mms([(A("ps7", 32, 46), c["n8k"], nls, False, True), (A("ps7", 0, 14), OB, nls, True, True), (A("ps7", 16, 30), c["nui"], nls, True, True)])
        scan(A("ci", 0, 14), A("ps7", 0, 14), A("ck", 1600, 1614), 0.0, OP.add, OP.add)
        tt(A("o1", 0, 14), A("ps7", 16, 30), A("ci", 0, 14), OP.add)
        tt(A("o2", 0, 14), A("ps7", 32, 46), A("o1", 0, 14), OP.max)
        cp(A("cof", 0, 14), A("o2", 0, 14))
        cp(IX("cwin", 0, P + F, "cof", 0, 14), JV)
        scan(A("jk", 0, K), A("cwin", 0, K), A("cwin", 0, K), 0.0, OP.max, OP.max)
        scan(A("cinc", 0, F), A("ps3", 0, F), ZERO, 0.0, OP.add, OP.add)
        mm(A("ps4", 0, F), I32, A("cinc", 0, F), False, True)
        act(A("rf", 0, F), A("ps4", 0, F), AF.Copy)
        tolist(A("ps0", 0, 32), "six", "jk", 0, K, True, True)
        ts(A("vl", 0, 32), K2, -float(KS), OP.add, A("cinc", F - 1, F), OP.is_lt)
        mm(A("ps6", 0, K), c["ljk"], A("jk", 0, K), True, False)
        if rnd == 0:
            fill(A("cwin", 0, K), 0)
        cp(A("jl", 0, 32), A("ps0", 0, 32))
        tt(A("oh", 0, K), IX("rf", 0, F, "jl", 0, 32), KC, OP.is_equal)
        act(A("jb", 0, 32), A("ps0", 0, 32), AF.Copy)
        mm(A("ps0", 0, 32), c["i16"], A("jb", 0, 32), True, False)
        mms([(A("ps2", 0, 32), c["i16"], A("jb", 0, 32), True, False), (A("ps2", 0, 32), c["i143"], A("vl", 0, 32), False, False)])
        tolist(A("ps0", 0, 32), "pi", "oh", 0, K, False, True)
        tt(A("lh", 0, K), IX("lb", 0, F, "jl", 0, 32), A("oh", 0, K), OP.mult)
        tolist(A("ps2", 0, 32), "neg", "lh", 0, K, False, True)
        ts(A("t1u", 0, 32), A("ps0", 0, 32), 8.0, OP.add)
        ts(A("t0u", 0, 32), A("ps2", 0, 32), 8.0, OP.add)
        mm(A("ps6", 0, K), c["loh"], A("oh", 0, K), False, False)
        mm(A("ps6", 0, K), c["llh"], A("lh", 0, K), False, False)
        for h in range(2):
            a, b = h * 256, h * 256 + 256
            act(A("r1", a, b), IX("run", 0, P + 8, "t1u", 16 * h, 16 * h + 16), AF.Identity, bias=1.0)
            tt(A("zi", a, b), IX("run", 0, P + 8, "t0u", 16 * h, 16 * h + 16), A("r1", a, b), OP.subtract)
            ts(A("zi", a, b), A("zi", a, b), 255, OP.bitwise_and)
            act(A("zb", a, b), A("zi", a, b), AF.Identity, bias=255.0, scale=-1.0)
            tolist(A(("ps3", "ps1")[h], 0, 16), "w2", "zb", a, b, True, True)
        for h, (hs, cb_, pb, ob) in enumerate((("ps3", "ps7", "ps4", "ps0"), ("ps1", "ps5", "ps2", "ps3"))):
            a, b, e = 16 * h, 16 * h + 16, 144 * h
            tt(A("hi", a, b), A(hs, 0, 16), A("vl", a, b), OP.add)
            ts(A("ow", a, b), A("hi", a, b), 15, OP.bitwise_and)
            ind = A("ind", e, e + 144)
            tt(ind, IX("ow", a, b, "cu", 2, 11), OWN, OP.is_equal)
            mm(A(cb_, 0, 144), OB, ind, True, h == 0)
            if h == 1:
                mm(A(cb_, 0, 144, 16), I16, A("cs", 15, 144, 16), False, True)
            mm(A(pb, 0, 144), c["nui"], ind, True, False)
            ts(A("owf", a, b), A("ow", a, b), 256.0, OP.mult)
            mms([(A(ob, 0, 16), c["i4352"], A("ind", e + 128, e + 144), True, False), (A(ob, 0, 16), I16, A("owf", a, b), False, False)])
            scan(A("cs", e, e + 144), A("cj", 224, 368), A(cb_, 0, 144), 0.0, OP.mult, OP.add)
            mm(A(pb, 0, 144), I16, A("cs", e, e + 144), False, True)
            tt(A("prod", e, e + 144), ind, A(pb, 0, 144), OP.mult)
            mms([(A(ob, 0, 16), I16, A("prod", e + 16 * o, e + 16 * o + 16), False, o == 8) for o in range(9)])
            ts(A("ql", a, b), A(ob, 0, 16), -256.0, OP.add)
            cp(IX("swin", 0, 9 * ST, "ql", a, b), A("zb", 16 * a, 16 * b))
        land = "land%d" % rnd
        send(lambda r: A("swin", r * ST, r * ST + 32), A(land, rank * 32, rank * 32 + 32), "ka%d" % rnd, "ks%d" % rnd)
        act(A(land, rank * 32, rank * 32 + 32), A("swin", rank * ST, rank * ST + 32), AF.Copy)
        if rnd == 0:
            for o in range(8):
                fill(A("swin", o * ST, o * ST + 32), -1)

    def gathered():
        count = lambda x, h: [(A("ps7", x, x + 16), I16, A("prod", 144 * h + 16 * o, 144 * h + 16 * o + 16), False, o == 8) for o in range(9)]
        for h in range(2):
            mms([(A("ps7", 32 + 16 * h, 48 + 16 * h), c["p64"], A("ind", 144 * h + 128, 144 * h + 144), True, False)] + count(32 + 16 * h, h))
            mms([(A("ps7", 16 * h, 16 * h + 16), IS16, A("owf", 16 * h, 16 * h + 16), True, False)] + count(16 * h, h))
        snt = A("snt", 0, 32)
        ts(snt, A("ps7", 32, 64), 32.0, OP.is_lt)
        ts(A("sid", 0, 32), A("ps7", 0, 32), -16.0, OP.add)
        mms([(A("ps4", 64, 96), I32, K2, True, False), (A("ps4", 64, 96), c["n8k"], snt, False, True),
             (A("ps4", 0, 32), OB, snt, True, True), (A("ps4", 32, 64), c["nui"], snt, True, True)])
        mms([(A("ps6", x, K, 16), c[x], A("sid", 0, 32), False, x == 15) for x in range(16)])
        act(A("rec", 0, K), A("ps6", 0, K), AF.Identity, bias=RB)
        act(A("rwin", 0, KS), RD, AF.Copy)
        scan(A("ci", 0, 32), A("ps4", 0, 32), A("ck", 1600, 1632), 0.0, OP.add, OP.add)
        tt(A("o1", 0, 32), A("ps4", 32, 64), A("ci", 0, 32), OP.add)
        tt(A("o2", 0, 32), A("ps4", 64, 96), A("o1", 0, 32), OP.max)
        cp(A("cof", 0, 32), A("o2", 0, 32))
        cp(IX("rwin", 0, KS + K, "cof", 0, 32), A("rec", 0, K))
        act(A("rb", 0, KS), A("rwin", 0, KS), AF.Copy)
        tolist(A("ps7", 0, 17), "r0", "rb", 0, KS, True, True)
        mm(A("ps4", 0, KS), c["r1"], A("rb", 0, KS), True, True)
        mm(A("ps6", 0, KS), R2, A("rwin", 0, KS), True, True)
        cp(A("qc", 0, 17), A("ps7", 0, 17))
        act(A("lrep", 0, KS), A("ps4", 0, KS), AF.Copy)
        act(A("t0c", 0, KS), A("ps6", 0, KS), AF.Copy)

    def owner(rnd):
        ld = "land%d" % rnd
        land = A(ld, 0, 256)
        nel = A("nel", 0, 256)
        arrive("ka%d" % rnd, [A(ld, 32 * r, 32 * r + 32) for r in range(8) if r != rank])
        mm(A("ps2", 0, 256), c["obw2"], land, True, True)
        act(A("qb", 0, 256), A("ps2", 0, 256), AF.Identity, bias=128.50003, scale=2.0 ** -15)
        tolist(A("ps1", 0, 16), "w2", ld, 0, 256, True, True)
        mm(A("ps5", 0, 256), c["obw8"], land, True, False)
        mm(A("ps5", 0, 256), c["n2k"], A("qb", 0, 256), False, True)
        back = 2048.0 * 129 - rank / 8.0
        ts(A("prh", 0, 256), A("ps5", 0, 256), back, OP.add)
        act(A("nel" if rnd == 0 else "inv", 0, 256), land, AF.Relu, scale=-1.0)
        cp(A("hli", 0, 16), A("ps1", 0, 16))
        if rnd == 1:
            ts(A("pl2", 0, 16), A("hli", 0, 16), 32767, OP.bitwise_and, 4, OP.arith_shift_right)
            cp(A("plu", 0, 16), A("pl2", 0, 16))
            tt(A("ne", 0, 256), IX("store", 0, TS + 256, "plu", 0, 16), land, OP.not_equal)
            tolist(A("ps0", 0, 16), "one", "ne", 0, 256, True, True)
            mm(A("ps2", 0, 256), c["obm"], A("inv", 0, 256), True, False)
            mm(A("ps2", 0, 256), OB, A("ne", 0, 256), False, True)
            act(nel, A("ps2", 0, 256), AF.Relu, bias=1.0, scale=-1.0)
        ts(A("pli", 0, 16), A("hli", 0, 16), 2 ** 21 + 32767, OP.bitwise_and, 4, OP.arith_shift_right)
        mm(A("ps3", 0, 256), c["ob4"], nel, True, False)
        if rnd == 0:
            cp(A("pm", 0, 16), A("pli", 0, 16))
        else:
            ts(A("sn", 0, 16), A("ps0", 0, 16), 0.0, OP.is_equal, 4096.0, OP.mult)
            tt(A("pm", 0, 16), A("sn", 0, 16), A("pli", 0, 16), OP.add)
        at = [256 * a - 8 * a * (a - 1) for a in range(17)]

        def weigh(a, last):
            l = [(A("ps3", 16 * a, 16 * a + 16), c["obp"], A("mb", at[a], at[a] + 16), False, last and a == 15)]
            if a < 15:
                l.append((A("ps3", 16 * a + 16, 256), c["ob4"], A("mb", at[a] + 16, at[a + 1]), False, last))
            return l
        act(A("pm", 16, 32), A("pm", 0, 16), AF.Identity, bias=-back)
        for a in range(SA, 16):
            act(A("mb", at[a], at[a + 1]), A("ps5", 16 * a, 256), AF.Abs, bias=A("pm", 16 + a, 17 + a), scale=-1.0)
        act(A("mb", at[SA], at[16]), A("mb", at[SA], at[16]), AF.Relu, bias=1.0, scale=-1.0)
        for a in range(SA):
            ts(A("mb", at[a], at[a + 1]), A("prh", 16 * a, 256), A("pm", a, a + 1), OP.is_equal)
            if a == SA - 2:
                mms(sum([weigh(x, False) for x in range(SA, 16)], []))
            mms(weigh(a, a == SA - 1))
        tt(A("nw", 0, 256), A("ps3", 0, 256), THR, OP.is_lt)
        send(lambda r: A("nw", r * 32, r * 32 + 32), A("fwin", rank * 32, rank * 32 + 32), "fa%d" % rnd, "fs%d" % rnd)
        act(A("fwin", rank * 32, rank * 32 + 32), A("nw", rank * 32, rank * 32 + 32), AF.Copy)
        if rnd == 0:
            iota(A("kidb", 0, W), [[1, W]], 0, 0, False)
        arrive("fa%d" % rnd, [A("fwin", 32 * r, 32 * r + 32) for r in range(8) if r != rank])

    def store(rnd):
        tolist(A("ps5", 0, 16), "six", "nw", 0, 256, True, True)
        tt(A("sx", 0, 16), A("pli", 0, 16), QC, OP.subtract)
        tt(A("sy", 0, 16), A("ps5", 0, 16), A("sx", 0, 16), OP.mult)
        tt(A("sz", 0, 16), A("sy", 0, 16), QC, OP.add)
        cp(A("su", 0, 16), A("sz", 0, 16))
        cp(IX("store", 0, TS + 256, "su", 0, 16), A("land%d" % rnd, 0, 256))
        if rnd == 1:
            dma("y", "yt", A("store", 0, TS), "w0", 4.1)

    def nextfront(rnd):
        hold = A("hold", 0, F)
        starts = A("pwin", 0, 2 * F, 2)
        mm(A("ps0", 0, 17), I32, NC, True, False)
        tt(A("xl", 0, KS), IX("fwin", 0, KS, "qc", 0, 17), A("lrep", 0, KS), OP.mult)
        scan(A("cum", 1, KS + 1), A("xl", 0, KS), CAPH, 0.0, OP.add, OP.min)
        tolist(A("ps0", 0, 17), "n256", "xl", 0, KS, False, True)
        tolist(A("ps1", 0, 17), "h8", "cum", 0, KS, True, False)
        act(A("yb", 0, 17), A("ps0", 0, 17), AF.Relu)
        mm(A("ps1", 0, 17), I32, A("yb", 0, 17), False, True)
        ts(A("ex", 0, KS), A("cum", 1, KS + 1), float(F), OP.is_gt, 4096.0, OP.mult)
        cp(A("ofu", 0, 17), A("ps1", 0, 17))
        tt(IX("pwin", 0, 1600, "ofu", 0, 17), A("t0c", 0, KS), A("ex", 0, KS), OP.add)
        scan(hold, A("xf", 0, F), starts, -4096.0, OP.add, OP.max)
        tolist(A("ps2", 0, 14), "h16", "hold", 0, F, True, True)
        ts(A("tju", 0, 14), A("ps2", 0, 14), P / 2.0, OP.add, float(P), OP.min)
        iu, iv = IX("tuv", 0, TW, "tju", 0, 14), IX("tuv", TW, 2 * TW, "tju", 0, 14)
        ts(A("drp", 0, F), hold, -1.0, OP.mult, -2000.0, OP.min)
        if rnd == 0:
            for a, b in ((0, 2), (2, 14)):
                for h in range(2):
                    cp(A("kk", h * F + 16 * a, h * F + 16 * b), IX("tuv", h * TW, h * TW + TW, "tju", a, b))
            tt(A("nf", 0, F), starts, A("drp", 0, F), OP.is_le)
            fill(A("pwin", 0, 2 * F), -2048)
        else:
            row = (0, 128, 16)
            tt(A("fin", 2 * F, 3 * F), starts, A("drp", 0, F), OP.is_gt)
            dma("y", "ys", A("fin", 2 * F, 3 * F, 1, row), "w3", 2.0)
            act(A("fin", F, 2 * F), iv, AF.Copy)
            dma("s", "yv", A("fin", F, 2 * F, 1, row), "w2", 2.0)
            cp(A("fin", 0, F), iu)
            dma("y", "yu", A("fin", 0, F, 1, row), "w1", 2.0)

    for rnd in range(2):
        side()
        big(rnd)
        tables(rnd)
        control(rnd)
        gathered()
        owner(rnd)
        store(rnd)
        nextfront(rnd)
    return ops


ORDER = "B2A.AKAMALANASAOAPAQARATA*A(A=A/AUB0AVB)B7B<B=B:B>B;CIAXBTC*AYCCB(BYB-BVBUC(BWC)BXCDAWAFA2A?A1B1ACAJAEADA7A<A0A8A3A;A6AHA:A9AIAGA4A5A@AAA>ABA)CEB@BHBEBKBAB/B*BQBRBSBNBPB,B+BOB4CJBBB3BDC+CLC.C0BCC-C1BGCNBJCOBMCHCMB.B5C,C6C4C5C8C;C:C3CFCGBFBLBIC/CPCKB6A+A,A-CRB?C7CSEMEVC9B9B8ENCTCVCWC2CQCUCXCYH@D(D*D:D)D+D8D;DHD.D-D,D9D/DID<D>D=DJE1DXDYD0D?DKD1D4DLD2D5D@DOE(DADDDME2DBDPDEDNE)DQE3E*D3E;E>D6DFDCDTE+D7E4E,E<E5E-E6DUDRE.E7DGE8DVDSE/E9E0E?E=EAEDDWE:F-F/E@F.EBF4F0F1F2F3F5F7FNFMF6FLFOF:F@F8EGF;FAEEFYFQECFRFPF<G(FSEFFTEHFUEIFVEJFWEKFXG-ELF=G)FFFBF>G*F?G.G+G/FCFGC=F9G0FDFHFIEOC?FEG4G1G3FJG,G2G6FKG:G5G7G;G<C@CBG?G@C<G=G>C>CAGAGDGEGFGIGBGCGGGHGQGKGRGSGJG8GLGTGUGVGMGYGWGNH(GOH)GXH7H*H8H9GPH+H,H-G9H:H;H=H<H>HAHBEPEYESEQERF(H?H.EXHCHDHEHMIPHNHPHQHOHTHFHRHWHHHUHVHSHXI.I/HYI(I)I0I1I2I4I6I8I:I<I>I@ICIKI3I5I7I9I*I+I,I-I;I=I?IAIBIDIEHIHGIJILHJIMINIOEUEWETHKIGF,NFHLIFH5H3H6H/IIIQIRISIUF+F)F*IWITIVIXIYJ(J+J0J)J*J,J.J-J/J7J9J8JIJ:IHH0H1H4H2J1JGJJJYJHJWJ=J;JLJ<JKJMK@K(J>JXJNJ?K5K6K)JCJ@KAK,J3JOJDJAK-K7J4JPJSK+K8K*K1K.KBKMJEJBKJJQJTK;K2KDK/KEK<KKJUJRJ5JFKCK9K:K=KFJVK>KGK0J6K3K4K?KHKSKPLILJKNJ2KLKIL<LCL>KOL?L@L=M)LALDLBKQLFM,M+M*LEKRKTM.LPLOLGKVKULKM/LQM-M0KXM1M6M2M3KYM4L(M5KWM:LRLLM7LMM9LSL)M<LNM8LULVLWL3L*M>LHLXM=LTMBM@M?MALYMCM;L8L9M(MDMHMMMEMIMJMKMNMOMPMLMRMSMWMTMFMQMXMUMVN-N.MYN/N(N)N0N1N2N*L7L2L,L.L;N3N5N6N+N7N,N=N4N8N9N>N?N@MGN:NANBNDNCNGN<NENHNINJNKL:L-N;NSNVO)NTO(NUL+NLNWO.NXO*O+O,O-O/O0O1NYO3O4O2O<O>OJO@OBODOFOHOQOLOXONO5O6O7O8O9O:O;L/L0L1O=O?OAOCOEOGOIOKOMOOOPOROSP,OTNNNONMOWNPOYP(NROUNQL6L4P)P*P+OVP-P/P.P0P3P1L5P2P4P5P6P9P7P:P8P<P;P>P?P="


def needs(ops):
    ent = {}
    pred = []
    sent = None
    for i, o in enumerate(ops):
        deps = set()
        if o["q"] == "x":
            deps.add(sent)
        elif o["q"] == "g" and o["sem"]:
            sent = i
        acc = [(b, c0, c1, w, wh) for w, lst in ((False, o["r"]), (True, o["w"])) for (b, c0, c1), wh in zip(lst, o["whole"] if w else [False] * len(lst))]
        acc = [(b, 0, 512, True, True) if bank(b) else (b, c0, c1, w, wh) for b, c0, c1, w, wh in acc]
        for b, c0, c1, w, wh in acc:
            for d0, d1, j, jw in ent.get(b, []):
                if d0 < c1 and c0 < d1 and (w or jw):
                    deps.add(j)
        for b, c0, c1, w, wh in acc:
            e = ent.setdefault(b, [])
            if w and wh:
                e[:] = [y for y in e if not (c0 <= y[0] and y[1] <= c1)]
            e.append((c0, c1, i, w))
        deps.discard(i)
        pred.append(deps)
    return pred


def schedule(ops, hop=0.045):
    n = len(ops)
    pred = needs(ops)
    given = [(ord(ORDER[2 * x]) - 65) * 50 + ord(ORDER[2 * x + 1]) - 40 for x in range(len(ORDER) // 2)]
    if sorted(given) == list(range(n)):
        at = {i: x for x, i in enumerate(given)}
        if all(at[j] < at[i] for i in range(n) for j in pred[i]):
            return [ops[i] for i in given]
    succ = [[] for _ in ops]
    left = [len(p) for p in pred]
    for i, p in enumerate(pred):
        for j in p:
            succ[j].append(i)
    tail = [0.0] * n
    for i in range(n - 1, -1, -1):
        tail[i] = ops[i]["est"] + max([tail[k] + (0.0 if ops[i]["q"] == "t" and ops[k]["q"] == "t" else hop) for k in succ[i]], default=0.0)
    can = [0.0] * n
    free = {}
    ready = {}
    for i, o in enumerate(ops):
        if left[i] == 0:
            ready.setdefault(o["q"], []).append(i)
    line = {q: [i for i, o in enumerate(ops) if o["q"] == q] for q in "gy"}
    order = []
    dmas = 0.0
    while len(order) < n:
        best = None
        for q, lst in ready.items():
            if q in line:
                lst = [i for i in lst if i == line[q][0]]
            if not lst:
                continue
            f = free.get(q, 0.0)
            m = min(max(f, can[i]) for i in lst)
            i = max((i for i in lst if max(f, can[i]) <= m), key=lambda i: tail[i])
            for j in lst:
                if m < can[j] < m + ops[i]["est"] and max(can[j] + tail[j], can[j] + ops[j]["est"] + tail[i]) < max(m + tail[i], m + ops[i]["est"] + tail[j]):
                    i, m = j, can[j]
            k = (max(f, can[i]), -tail[i], i)
            if best is None or k < best:
                best = k
        t, _, i = best
        o = ops[i]
        q = o["q"]
        ready[q].remove(i)
        if q in line:
            line[q].pop(0)
        end = t + o["est"]
        free[q] = end
        if o["sem"] and q in "ys":
            end = max(t, dmas) + o["est"]
            dmas = end - 2.0
            free[q] = t + 0.1
        elif o["sem"] and q == "g":
            free[q] = t + 1.0
        order.append(o)
        o["t0"], o["t1"] = t, end
        for k in succ[i]:
            can[k] = max(can[k], end + (0.0 if q == "t" and ops[k]["q"] == "t" else hop))
            left[k] -= 1
            if left[k] == 0:
                ready.setdefault(ops[k]["q"], []).append(k)
    return order


def sync(ops):
    ent = {}
    know = {}
    snap = []
    qn = {}
    for i, o in enumerate(ops):
        q = o["q"]
        deps = set()
        for w, lst in ((False, o["r"]), (True, o["w"])):
            for b, c0, c1 in lst:
                ps = bank(b)
                if ps:
                    c0, c1 = 0, 512
                for (d0, d1, j, jw) in ent.get(b, []):
                    if d0 >= c1 or c0 >= d1:
                        continue
                    same = ops[j]["q"] == q and ops[j]["sem"] is None
                    if ps and same and (q == "t" or not (w or jw)):
                        continue
                    if not (w or jw) and not ps:
                        continue
                    deps.add(j)
        kn = know.setdefault(q, {})
        waits = []
        for j in sorted(deps, reverse=True):
            key = ops[j]["sem"] or ops[j]["q"]
            if kn.get(key, -1) >= ops[j]["n"]:
                continue
            waits.append(j)
            for k, v in list(snap[j].items()) + [(key, ops[j]["n"])]:
                if kn.get(k, -1) < v:
                    kn[k] = v
        o["n"] = 0 if o["sem"] else qn.get(q, 0)
        qn[q] = qn.get(q, 0) + 1
        o["waits"] = waits
        snap.append(dict(kn))
        for w, lst in ((False, o["r"]), (True, o["w"])):
            for x, (b, c0, c1) in enumerate(lst):
                ps = bank(b)
                if ps:
                    c0, c1 = 0, 512
                e = ent.setdefault(b, [])
                if (ps and q != "t") or (w and not ps and o["whole"][x]):
                    e[:] = [y for y in e if not (c0 <= y[0] and y[1] <= c1)]
                elif ps:
                    e[:] = [y for y in e if ops[y[2]]["q"] == "t"][-1:] + [y for y in e if ops[y[2]]["q"] != "t"]
                e.append((c0, c1, i, w))
    need = set()
    for o in ops:
        need.update(o["waits"])
    cnt = {}
    for j, o in enumerate(ops):
        o["cnt"] = None
        if o["sem"] is None and j in need:
            cnt[o["q"]] = cnt.get(o["q"], 0) + 1
            o["cnt"] = cnt[o["q"]]
    return cnt


def rank_program(g, core, T, topo):
    if T.rank_of(core) is None:
        return
    ops = schedule(build(core, T, topo))
    cnt = sync(ops)
    sems = {"v": "qv", "s": "qs", "t": "qt", "g": "qg"}
    queue = {"v": g.vector, "s": g.scalar, "t": g.tensor, "g": g, "y": g.sync}
    done = {}
    for o in ops:
        if o["sem"]:
            done[o["sem"]] = o["inc"]
        if o["fn"] is None:
            continue
        best = {}
        for j in o["waits"]:
            d = ops[j]
            k, v = (d["sem"], d["inc"]) if d["sem"] else (sems[d["q"]], d["cnt"])
            best[k] = max(best.get(k, 0), v)
        for k, v in best.items():
            queue[o["q"]].wait_ge(T.sem[k], v)
        h = o["fn"](g)
        if o["cnt"] is not None:
            h.then_inc(T.sem[sems[o["q"]]], 1)
        elif o["sem"] and o["q"] != "g":
            h.then_inc(T.sem[o["sem"]], 16)
    for q, n in cnt.items():
        g.wait_ge(T.sem[sems[q]], n)
    for k, v in done.items():
        g.wait_ge(T.sem[k], v)
